import numpy as np, ml_dtypes
CORES = [23,119,17,113]
N = 4
import mx_ref
BF = ml_dtypes.bfloat16
def gentries(a):
    return np.ascontiguousarray(a.reshape(8, 16, -1).transpose(0, 2, 1)).reshape(8, -1)
def gtable(e):
    e = np.asarray(e); return np.ascontiguousarray(e.reshape(8, -1, 16).transpose(0, 2, 1)).reshape(128, -1).astype(np.int32)
def gcols(t, e):
    v = np.concatenate([t.reshape(8, 16, -1, 4), np.zeros((8, 16, 1, 4), BF)], axis=2)
    return np.ascontiguousarray(np.stack([v[g][:, e[g]] for g in range(8)])).reshape(128, -1)
def tile(rs):
    return np.stack(rs, axis=2).reshape(128, -1).astype(BF)
def pick(q, e):
    c = np.concatenate([q[0].reshape(128, -1, 4), np.zeros((128, 1, 4), np.uint8)], axis=1); s = np.concatenate([q[1], np.ones((16, 1), np.uint8)], axis=1)
    return (np.ascontiguousarray(c[:, e].reshape(128, -1)), np.ascontiguousarray(s[:, e]))
def join(*qs):
    return (np.concatenate([q[0] for q in qs], axis=1), np.concatenate([q[1] for q in qs], axis=1))
def put(q, e, v):
    c, s = q[0].reshape(128, -1, 4).copy(), q[1].copy(); c[:, e] = v[0].reshape(128, -1, 4); s[:, e] = v[1]
    return (c.reshape(128, -1), s)
def pk(c, s):
    return (np.ascontiguousarray(c), mx_ref.live(s))
def emit(q):
    return q[0], q[1]
def packed(v, rng):
    q = [mx_ref.quantize(np.ascontiguousarray(v[r])) for r in range(N)]
    return np.stack([a for a, b in q]), np.stack([mx_ref.plane(b, rng) for a, b in q])
def values_of_codes():
    e, c = np.zeros((128, 128, 4), np.float32), np.zeros((128, 2, 4), np.uint8)
    e[np.arange(128), np.arange(128), 0] = 1
    c[:127, :, 0] = np.arange(256).reshape(2, 128).T[:127]
    return mx_ref.matmul(mx_ref.quantize(e.reshape(128, 512).astype(BF)), (c.reshape(128, 8), np.full((16, 2), 127, np.uint8))).T.reshape(-1).astype(np.float64)
CODE_VALUE, SCALE_VALUE = values_of_codes(), 2.0 ** (np.arange(256) - 127.0)
def decode(q):
    return (CODE_VALUE[q[0]].reshape(16, 8, -1, 4) * SCALE_VALUE[q[1]][:, None, :, None] + 0.0).reshape(128, -1).astype(np.float32)
def f(rng, *shape):
    return mx_ref.flush((rng.standard_normal(shape, dtype=np.float32) * np.exp2(rng.integers(-2, 3, shape[:-1] + (1,)))).astype(BF))
def wide(rng, *shape, cols=0):
    v = rng.standard_normal(shape, dtype=np.float32) * np.exp2(rng.integers(-12, 13, shape)).astype(np.float32)
    if cols: v *= np.repeat(np.exp2(rng.integers(-cols, cols + 1, shape[:-2] + (1, shape[-1] // 4))) * (rng.random(shape[:-2] + (1, shape[-1] // 4)) > 0.0625), 4, axis=-1).astype(np.float32)
    return mx_ref.flush(v.astype(BF))
C, M, WIDTH = 384, 16, 24
ROUNDS = 3
def big(v):
    v = v.astype(np.float32)
    v[np.abs(v) < np.float32(2.0 ** -16)] = 0
    return v.astype(BF)
def numbers_of(rng):
    return {"x": np.array(f(rng, N, 128, 4 * C)), "u": np.array(f(rng, N, 128, 512)), "v": np.array(f(rng, N, 128, 512))}
def towers(rng):
    return np.stack([gtable(np.stack([rng.permutation(C) for g in range(8)])) for r in range(N)])
def layers(rng):
    w = f(rng, N, 128, 2048).astype(np.float32).reshape(N, 128, 512, 4)
    w[rng.random(w.shape) < 0.9375] = 0
    m = np.searchsorted(28.0 * 2.0 ** np.arange(-20.0, 30.0), np.sum(np.abs(w), axis=(1, 3), keepdims=True))
    return np.array(mx_ref.flush((w * (2.0 ** (20.0 - m)).astype(np.float32)).astype(BF))).astype(np.float32)
def mirror(k):
    w, i = np.zeros((N, 128, 4, 128, 4), np.float32), np.arange(128)
    for b in range(4): w[:, i, b, i, b] = 32 * k[:, None]
    return w.reshape(N, 128, 512, 4)
def weights(rng, w):
    c, s = packed(np.ascontiguousarray(w).reshape(N, 128, 2048).astype(BF), rng)
    return {"wc": c, "ws": s}
def setup_inputs(rng):
    return {**numbers_of(rng), "tw": towers(rng), **weights(rng, layers(rng))}
def setup_inputs_ties(rng):
    d = numbers_of(rng)
    x = d["x"].astype(np.float32).reshape(N, 8, 16, C, 4)
    x[:, :, :8] = 0
    x[:, :, 0, :, 0] = rng.integers(0, 4, (N, 8, C))
    n = (N, 8, 8, C, 4)
    a = (1 + (2 * rng.integers(0, 64, n) + 1) / 128) * np.exp2(rng.integers(-14, -7, n)) * rng.choice([-1.0, 1.0], n)
    a[:, :, 0, :, 0] = 1.96875
    x[:, :, 8:] = a * np.exp2(rng.integers(-2, 3, (N, 8, 1, 1, 1)))
    u = d["u"].reshape(N, 128, 128, 4)
    u[:, :, ::16] = 0
    o = rng.permutation(N)
    for r in range(N):
        for h in range(0, 128, 16): u[r, h, h, 0] = 0.0 if r == o[0] else -1.0 if r in (o[1], o[3]) else 1.0
    w = layers(rng)
    w.reshape(N, 128, 4, 8, 16, 4)[:, :, :, :, :8] = 0
    return {"x": x.reshape(N, 128, 4 * C).astype(BF), "u": u.reshape(N, 128, 512), "v": d["v"], "tw": towers(rng), **weights(rng, w)}
def setup_inputs_near(rng):
    d = numbers_of(rng)
    x = d["x"].astype(np.float32).reshape(N, 8, 16, C, 4)
    u = d["u"].reshape(N, 128, 128, 4)
    u[:, :, ::16] = 0
    x[:, :, 0] = 0
    x[:, :, 8:] = 0
    s = rng.integers(0, 16, (N, 8, C))
    o = rng.permutation(8) % 4
    turn = np.arange(N) % 2 == rng.integers(2)
    w = mirror(np.ones(N)).reshape(N, 128, 4, 128, 4)
    for g in range(8):
        h = 16 * g
        if o[g] < 3:
            k = 2.0 ** -30 if o[g] == 2 else 1.0
            x[:, g, 0, :, 0] = -1.0 if o[g] == 1 else 1.0
            x[:, g, 8] = ((s[:, g, :, None] >> np.arange(4)) & 1) * np.exp2(np.arange(4) - 23.0)
            x[:, g, 11, :, 0] = 2.0 ** -10
            u[:, h, h, 0] = k
            u[:, h + 8, h] = k
            u[:, h + 11, h, 0] = k
            if o[g] == 0:
                x[turn, g, 8] = 0
                u[turn, h + 8, h] = -4.0
        else:
            x[:, g, 9:11, :, 0] = (1 + rng.integers(0, 8, (N, 2, C)) / 8) * 2.0 ** -30
            x[:, g, 12, :, 0] = 2.0 ** -30
            u[:, h + 9, h, 0] = -2.0 ** -30
            u[:, h + 10, h, 0] = 1.125 * 2.0 ** -30
            x[turn, g, 9:11] = 0
            u[turn, h + 9, h, 0] = 2.0 ** -30
            u[turn, h + 10, h, 0] = -1.125 * 2.0 ** -30
            for i in (h + 9, h + 10): w[turn, i, :, i] *= np.float32(2.0 ** -9)
    far = rng.permutation(np.nonzero(o < 3)[0])[:4]
    for r in range(N):
        for g in far: x[r, g, 0, rng.integers(C), 0] = 2.0 ** 30 * rng.choice([-1.0, 1.0])
    return {"x": x.reshape(N, 128, 4 * C).astype(BF), "u": u.reshape(N, 128, 512), "v": d["v"], "tw": towers(rng), **weights(rng, w)}
def setup_inputs_huge(rng):
    d = numbers_of(rng)
    o = rng.permutation(N)
    c = rng.choice([-1.0, 1.0], N)
    x = (0.6 + 0.4 * rng.random((N, 128, C, 4))) * 2.0 ** 30 * c[:, None, None, None]
    x[o < N // 2] *= rng.choice([-1.0, 1.0], (N // 2, 1, C, 1))
    u = d["u"].astype(np.float32).reshape(N, 128, 128, 4)
    k = np.stack([rng.permutation(8) % 2 * 2.0 - 1.0 for r in range(N)])
    u[:, :, ::16] = 2.0 ** 30 * (1 - 0.1 * rng.random((N, 128, 8, 4))) * k[:, None, :, None]
    e = int(np.argmax(o))
    a = np.where(rng.random((128, C, 4)) < rng.random((1, C, 1)), 0.9375, 1.0)
    a[::8, :, 0] = 1.0
    x[e] = a * 2.0 ** 30 * c[e]
    u[e, :, ::16] = 2.0 ** 30 * k[e][None, :, None]
    return {"x": x.astype(np.float32).reshape(N, 128, 4 * C).astype(BF), "u": u.reshape(N, 128, 512).astype(BF), "v": d["v"], "tw": towers(rng), **weights(rng, mirror(c * np.roll(c, 1)))}
def setup_inputs_ends(rng):
    d = numbers_of(rng)
    s, k0 = rng.choice([-1.0, 1.0]), int(rng.integers(4))
    x = d["x"].astype(np.float32).reshape(N, 128, C, 4)
    u = d["u"].astype(np.float32).reshape(N, 128, 128, 4)
    w, m, p = layers(rng), mirror(np.ones(N)), []
    for r in range(N):
        k = (r + k0) % 4
        c = (rng.permutation(8) % 2 * 2.0 - 1.0)[None, :, None]
        e = np.stack([rng.permutation(C)] * 8)
        if k == 0:
            x[r], w[r], u[r, :, ::16] = s * 2.0 ** 30, 0.0, 2.0 ** 30 * c
            e[:] = np.arange(C)
        elif k == 1:
            x[r], w[r], u[r, :, ::16] = s * 2.0 ** -30, m[r], 2.0 ** -30 * c
            e[:] = np.arange(C)[::-1]
        elif k == 2:
            x[r] = 2.0 ** 30 * rng.choice([-1.0, 1.0], (1, C, 1))
            w[r] = 0.0625 * rng.choice([-1.0, 1.0], (1, 512, 1))
            u[r, :, ::16] = 2.0 ** 30 * c
        else:
            for g in range(8): e[g] = np.roll(np.arange(C), g)
        p.append(gtable(e))
    d["v"] = (np.where(d["v"] < 0, -1.0, 1.0) * np.where(rng.permutation(N) % 2, 2.0 ** -30, 2.0 ** 30)[:, None, None]).astype(np.float32).astype(BF)
    return {"x": x.reshape(N, 128, 4 * C).astype(BF), "u": u.reshape(N, 128, 512).astype(BF), "v": d["v"], "tw": np.stack(p), **weights(rng, w)}
def setup_inputs_spread(rng):
    d = setup_inputs(rng)
    d["x"] = big(wide(rng, N, 128, 4 * C, cols=4))
    return d
def check_inputs(d):
    b = []
    for k in ("x", "u", "v"):
        a = np.abs(d[k].astype(np.float32))
        if not (np.isfinite(a).all() and ((a == 0) | (a >= 2.0 ** -30) & (a <= 2.0 ** 30)).all()): b.append("a value of " + k)
    none, least, most = [emit(mx_ref.quantize(np.full((128, 16), k, np.float32).astype(BF)))[1][0, 0] for k in (0.0, 2.0 ** -30, 2.0 ** 30)]
    for r in range(N):
        if (np.sort(gentries(d["tw"][r]), axis=1) != np.arange(C)).any(): b.append("tw: a group's entries aren't a permutation")
        if ((d["wc"][r] == 0x7F) | (d["wc"][r] == 0xFF)).any(): b.append("wc: a code that is no number")
        s = mx_ref.live(d["ws"][r])
        if ((s != none) & ((s < least) | (s > most))).any(): b.append("ws: a scale out of range")
        elif not (np.sum(np.abs(decode(pk(d["wc"][r], d["ws"][r])).astype(np.float64)).reshape(128, 512, 4), axis=(0, 2)) <= 32).all(): b.append("W: the sizes of a column are beyond 32 together")
    return b
def reference(x, u, v, tw, wc, ws):
    qu = [mx_ref.quantize(u[r]) for r in range(N)]
    lay = [pk(wc[r], ws[r]) for r in range(N)]
    now = [x[r] for r in range(N)]
    base = [gentries(tw[r]).reshape(8, M, WIDTH) for r in range(N)]
    top = [gentries(tw[r]).reshape(8, M, WIDTH) for r in range(N)]
    up = np.zeros((N, 8, C), np.int64)
    for t in range(ROUNDS):
        h = WIDTH >> (t + 1)
        own, ends = [], []
        for r in range(N):
            q = mx_ref.quantize(now[r])
            s = mx_ref.matmul(qu[r], q)[::16] + np.float32(0.0)
            own.append(decode(q).astype(BF))
            score = np.take_along_axis(s, base[r].reshape(8, -1), axis=1).reshape(8, M, 2 * h)
            o = np.argsort(-score, axis=2, kind="stable")
            b, e = np.take_along_axis(base[r], o, axis=2), np.take_along_axis(top[r], o, axis=2)
            np.put_along_axis(up[r], e[:, :, :h].reshape(8, -1), np.roll(b[:, :, h:], 1, axis=1).reshape(8, -1), axis=1)
            base[r], top[r] = b[:, :, :h], np.roll(e[:, :, h:], 1, axis=1)
            np.put_along_axis(up[r], top[r].reshape(8, -1), np.stack([C + np.arange(M * h)] * 8), axis=1)
            a = gcols(own[r], top[r].reshape(8, -1)).astype(np.float32) + gcols(own[r], base[r].reshape(8, -1)).astype(np.float32)
            ends.append(mx_ref.quantize(np.ascontiguousarray((a * np.float32(0.5)).astype(BF))))
        for r in range(N):
            made = tile([mx_ref.matmul(pick(lay[r], np.arange(128 * b, 128 * b + 128)), ends[r - 1]) * np.float32(0.03125) for b in range(4)])
            near = gcols(np.concatenate([own[r], made], axis=1), up[r]).astype(np.float32)
            now[r] = ((own[r].astype(np.float32) + near) * np.float32(0.5)).astype(BF)
    y, op = np.zeros((N, 128, C), np.float32), np.zeros((N, 8, C), np.float32)
    oc, osc = np.zeros((N, 128, 4 * C), np.uint8), np.zeros((N, 16, C), np.uint8)
    for r in range(N):
        q = mx_ref.quantize(now[r])
        y[r] = mx_ref.matmul(mx_ref.quantize(v[r]), q)
        op[r] = up[r]
        oc[r], osc[r] = emit(q)
    return {"y": y, "op": op, "oc": oc, "osc": osc}

@@ -1,0 +1,548 @@
+from concourse.mybir import dt, AluOpType, ActivationFunctionType
+
+A = AluOpType
+COPY = ActivationFunctionType.Copy
+P = 384
+LANES = {1: 24, 2: 12, 3: 6}
+B0 = {1: 14, 2: 8, 3: 6}
+NR = {1: 576, 2: 144, 3: 48}
+NE = {1: 688, 2: 208, 3: 80}
+SG0 = {1: 0, 2: 44, 3: 58}
+VW = {1: 576, 2: 480, 3: 432}
+XB = {1: "X1", 2: "X2", 3: "X3", 4: "X2"}
+BF, F32, U16, I32, U8, FP8 = "bfloat16", "float32", "uint16", "int32", "uint8", "float8_e4m3fn_x4"
+
+SCRATCH = {}
+
+
+def _buf(name, cols, dtype, where="sbuf"):
+    SCRATCH[name] = (where, [128, cols], dtype)
+
+
+for _n, _c in (("QX1", P), ("QX2", P), ("QX3", P), ("QX4", P), ("QU", 128), ("UR", 128), ("QV", 128), ("WW", 512),
+               ("EC", 512), ("LX", P), ("LE2", 224), ("LE3", 176), ("QE1", 192), ("QE2", 128), ("QE3", 128)):
+    _buf(_n + "c", _c, FP8)
+    _buf(_n + "s", _c, U8)
+for _n, _c, _t in (
+        ("X1", 4 * P, BF), ("X2", 4 * P, BF), ("X3", 4 * P, BF), ("ub", 512, BF), ("vb", 512, BF), ("half", 704, BF),
+        ("zi", 516, BF), ("FP", 4 * P, BF), ("FQ", 960, BF), ("E1", 768, BF), ("E2", 512, BF), ("E3", 704, BF),
+        ("tmp", 832, BF), ("tb", 576, BF), ("m16s", 16, BF), ("m16", P, BF), ("seg16", P, BF), ("C", 576, BF), ("CS", 576, BF),
+        ("tw32", 24, I32), ("ic", 24, I32), ("mi", 16, I32), ("ui", 8, I32), ("ti", 96, I32),
+        ("tw16", 24, U16), ("il", 24, U16), ("ul", 8, U16), ("LL", 26, U16), ("SL", 12, U16),
+        ("US", 14, U16), ("BL", 24, U16), ("UL", 24, U16), ("SG", 64, U16),
+        ("cols", 8, F32), ("iotaR", 576, F32), ("J", 44, F32), ("KK", 24, F32), ("fe", 24, F32), ("R", 96, F32),
+        ("opc", 52, F32), ("UP", P, F32), ("ms", P, F32), ("ht", P, F32), ("ysb", P, F32),
+        ("SS", P, F32), ("GM", P, F32), ("SC", P, F32), ("BX", 576, F32), ("M", 688, F32), ("HS", 688, F32),
+        ("tf", 448, F32), ("sl", 32, F32), ("DB", 28, F32), ("VB", 208, F32), ("tbB", 24, F32), ("tbT", 12, F32)):
+    _buf(_n, _c, _t)
+for _r in (1, 2, 3):
+    _h = LANES[_r] // 2
+    for _n, _c, _t in (("V", 4 * VW[_r], BF), ("D0", NR[_r], BF), ("DS", NE[_r], BF), ("KA", 64, F32), ("T", NE[_r], F32),
+                       ("D", 28, F32), ("CL", B0[_r] + _h, U16),
+                       ("MN", NR[_r] // 16, U16), ("MX", NR[_r] // 16, U16), ("KL", NE[_r] // 16, U16)):
+        _buf(_n + str(_r), _c, _t)
+for _i in range(8):
+    _buf("p%d" % _i, 512, F32, "psum")
+
+NDMA = 26
+SEMAPHORES = ["vs", "ss", "ts", "gs", "loc", "axc", "axs", "all1", "a2c", "a2s", "a3c", "a3s"] + ["d%d" % i for i in range(NDMA)]
+
+
+def rank_program(g, core, T, topo):
+    rank = T.rank_of(core)
+    if rank is None:
+        return
+    nxt = T.cores[(rank + 1) % len(T.cores)]
+    rid, pid = topo.addr(nxt)[:2]
+    mask = topo.mask(core, nxt)
+    neng = len(topo.engines(core, nxt))
+
+    ENG = {"v": g.vector, "s": g.scalar, "t": g.tensor, "g": g, "y": g.sync}
+    QSEM = {"v": "vs", "s": "ss", "t": "ts", "g": "gs"}
+    cnt, known, wr, rd, nd = {}, {q: {} for q in ENG}, {}, {}, [0]
+
+    def before(q, reads, writes):
+        ev = []
+        for k in reads:
+            ev += wr.get(k, [])
+        for k in writes:
+            ev += wr.get(k, []) + rd.get(k, [])
+        for sem, val, clock in sorted(ev, key=lambda e: -e[1]):
+            if known[q].get(sem, 0) < val:
+                ENG[q].wait_ge(T.sem[sem], val)
+                for k2, v2 in clock.items():
+                    if known[q].get(k2, 0) < v2:
+                        known[q][k2] = v2
+
+    def after(q, sem, reads, writes):
+        clock = dict(known[q])
+        clock[sem] = cnt[sem]
+        ev = (sem, cnt[sem], clock)
+        for k in reads:
+            rd.setdefault(k, []).append(ev)
+        for k in writes:
+            wr[k] = [ev]
+            rd[k] = []
+
+    def op(q, reads, writes, fn):
+        before(q, reads, writes)
+        sem = QSEM[q]
+        fn().then_inc(T.sem[sem], 1)
+        cnt[sem] = cnt.get(sem, 0) + 1
+        after(q, sem, reads, writes)
+
+    def dma(q, out, in_, reads, writes):
+        before(q, reads, writes)
+        sem = "d%d" % nd[0]
+        nd[0] += 1
+        ENG[q].dma_start(out, in_).then_inc(T.sem[sem], 16)
+        cnt[sem] = 16
+        after(q, sem, reads, writes)
+
+    def send(out, in_, sem, reads, lands):
+        before("g", reads, [])
+        g.remote_dma(out, in_, T.sem[sem], T.sem.loc, pid, rid, mask)
+        cnt["loc"] = cnt.get("loc", 0) + neng
+        cnt[sem] = neng
+        wr[lands] = wr.get(lands, []) + [(sem, neng, {sem: neng})]
+
+    def ts(out, w, in0, rds, s1, op0, s2=None, op1=None):
+        if op1 is None:
+            op("v", rds, [w], lambda: g.vector.tensor_scalar(out, in0, s1, None, op0))
+        else:
+            op("v", rds, [w], lambda: g.vector.tensor_scalar(out, in0, s1, s2, op0, op1))
+
+    def tt(out, w, in0, in1, rds, o):
+        op("v", rds, [w], lambda: g.vector.tensor_tensor(out, in0, in1, o))
+
+    def vcopy(out, w, in_, rds):
+        op("v", rds, [w], lambda: g.vector.tensor_copy(out, in_))
+
+    def memset(out, w, k):
+        op("v", [], [w], lambda: g.vector.memset(out, k))
+
+    def scan(out, w, d0, d1, rds, o0, o1):
+        op("v", rds, [w], lambda: g.vector.tensor_tensor_scan(out, d0, d1, 0.0, o0, o1))
+
+    def act(out, w, in_, rds, scale=None):
+        if scale is None:
+            op("s", rds, [w], lambda: g.scalar.activation(out, in_, COPY))
+        else:
+            op("s", rds, [w], lambda: g.scalar.activation(out, in_, COPY, scale=scale))
+
+    def fill(out, w, n, value):
+        act(out, w, T.half[:, 0:n], ["half"], scale=2.0 * value)
+
+    def quant(qc, qs, w, in_, rds):
+        op("v", rds, [w], lambda: g.vector.quantize_mx(qc, qs, in_))
+
+    def mm(bank, n, lc, ls, rc, rs, rds):
+        op("t", rds, ["p%d" % bank], lambda: g.tensor.matmul_mx(T["p%d" % bank][:, 0:n], lc, ls, rc, rs, True, True))
+
+    def iota(out, w, pattern, base, cm, flt=True):
+        if flt:
+            op("g", [], [w], lambda: g.iota(out, pattern, base, cm, allow_small_or_imprecise_dtypes=True))
+        else:
+            op("g", [], [w], lambda: g.iota(out, pattern, base, cm))
+
+    col = {k2: T.cols[:, i:i + 1] for i, k2 in enumerate(("i", "m0", "n0", "m15", "n15", "p4"))}
+
+    dma("s", T.tw32[:], T.tw[:, :], [], ["tw32"])
+    for c in range(3):
+        dma("y", T.X1[:, 512 * c:512 * c + 512], T.x[:, 512 * c:512 * c + 512], [], ["X1%d" % c])
+    dma("s", T.ub[:], T.u[:, :], [], ["ub"])
+    dma("y", T.WWc[:].bitcast(dt.uint8), T.wc[:, :], [], ["WWc"])
+    dma("y", T.WWs[:], T.ws[:, :], [], ["WWs"])
+    dma("y", T.vb[:], T.v[:, :], [], ["vb"])
+
+    iota(T.ic[:], "ic", [[0, 24]], 0, 1, False)
+    iota(T.J[:], "J", [[16, 44]], 0, 0)
+    iota(T.mi[:], "mi", [[1, 16]], 128, -1, False)
+    iota(T.iotaR[:], "iotaR", [[1, 576]], 0, 0)
+    iota(T.ui[:], "ui", [[16, 8]], 0, 0, False)
+    iota(T.KK[:], "KK", [[-1, 24]], 22, 0)
+    for r in (1, 2, 3):
+        iota(T.R[:, 32 * r - 32:32 * r - 32 + B0[r]], "Ra%d" % r, [[1, B0[r]]], 0, 0)
+        iota(T.R[:, 32 * r - 32 + B0[r]:32 * r], "Rb%d" % r, [[1, 32 - B0[r]]], LANES[r] // 2, 0)
+
+    ts(col["p4"], "p4", T.ic[:, 0:1], ["ic"], 4.0, A.mult, 3.0, A.add)
+    ts(T.ic[:], "ic", T.ic[:], ["ic"], 15, A.bitwise_and)
+    ts(T.mi[:], "mi", T.mi[:], ["mi"], 15, A.bitwise_and)
+    ts(col["i"], "ci", T.ic[:, 0:1], ["ic"], 1.0, A.mult)
+    vcopy(T.il[:], "il", T.ic[:], ["ic"])
+    ts(T.m16s[:], "m16s", T.mi[:], ["mi"], 0.0, A.is_equal)
+    ts(T.J[:], "J", T.J[:], ["J", "ci"], col["i"], A.add)
+    memset(T.half[:], "half", 0.5)
+    for k2, val, o in (("m0", 0.0, A.is_equal), ("n0", 0.0, A.not_equal), ("m15", 15.0, A.is_equal), ("n15", 15.0, A.not_equal)):
+        ts(col[k2], k2, T.ic[:, 0:1], ["ic"], val, o)
+
+    def pair_lists(r):
+        W, n = LANES[r], NR[r] // 16
+        j = T.J[:, 0:n]
+        k, kw, kp, mn, mx = T.ti[:, 0:n], T.tf[:, 0:n], T.tf[:, 48:48 + n], T.tf[:, 96:96 + n], T.tf[:, 144:144 + n]
+        ts(k, "k", j, ["J"], 1.0 / W, A.mult, -(W - 1) / (2.0 * W), A.add)
+        yield
+        ts(kw, "kw", k, ["k"], -float(W), A.mult)
+        yield
+        tt(kp, "kp", j, kw, ["J", "kw"], A.add)
+        yield
+        tt(mn, "mn", k, kp, ["k", "kp"], A.min)
+        tt(mx, "mx", k, kp, ["k", "kp"], A.max)
+        yield
+        ts(T["MX%d" % r][:], "MX%d" % r, mx, ["mx"], 16.0, A.mult, 15.0, A.add)
+        ts(T["MN%d" % r][:], "MN%d" % r, mn, ["mn"], 16.0, A.mult, 15.0, A.add)
+        yield
+
+    def key_lists(r):
+        n, L, b0 = NE[r] // 16, LANES[r] + 1, B0[r]
+        j = T.J[:, 0:n]
+        sg, sl, ps, ad = T.ti[:, 48:48 + n], T.tf[:, 192:192 + n], T.tf[:, 256:256 + n], T.tf[:, 320:320 + n]
+        ts(sg, "sg", j, ["J"], 1.0 / L, A.mult, -(L - 1) / (2.0 * L), A.add)
+        yield
+        ts(sl, "slv", sg, ["sg"], -float(L), A.mult)
+        vcopy(T.SG[:, SG0[r]:SG0[r] + n], "SG%d" % r, sg, ["sg"])
+        yield
+        tt(ps, "psv", j, sl, ["J", "slv"], A.add)
+        yield
+        if r == 1:
+            vcopy(T.KL1[:], "KL1", ps, ["psv"])
+        else:
+            ts(ad, "adv", j, ["J"], float(b0 * L), A.is_ge, float(L), A.mult)
+            yield
+            tt(sl, "slv", ps, ad, ["psv", "adv"], A.add)
+            yield
+            vcopy(T["KL%d" % r][:], "KL%d" % r, sl, ["slv"])
+        yield
+
+    def thresholds(r):
+        W = LANES[r]
+        L, b0, n = W + 1, B0[r], NE[r]
+        ns = b0 + W // 2 + 1
+        t, R, a, b = T["T%d" % r], T.R[:, 32 * r - 32:32 * r], "Ra%d" % r, "Rb%d" % r
+        ts(R[:, 0:b0], a, R[:, 0:b0], [a, "m0"], col["m0"], A.subtract, 0.0, A.max)
+        yield
+        u = T.tf[:, 416:416 + ns]
+        ts(u, "uv", R[:, 0:ns], [a, b], 0.5, A.mult, -(W - 0.5), A.add)
+        yield
+        act(t[:], "T%d" % r, R.indirect(T.SG[:, SG0[r]:SG0[r] + n // 16]), [a, b, "SG%d" % r])
+        yield
+        yield
+        yield
+        tt(t[:, W:ns * L:L], "T%d" % r, R[:, 0:ns], u, [a, b, "uv"], A.mult)
+        yield
+
+    def together(*gens):
+        gens = list(gens)
+        while gens:
+            gens = [x for x in gens if next(x, 1) is None]
+            yield
+
+    def signs(r):
+        W, d, k = LANES[r], T["D0%d" % r], "D0%d" % r
+        fill(d[:], k, NR[r], 1.0)
+        fill(d[:, 0:W * W:W], k, W, 0.0)
+        fill(d[:, 1:(W + 1) * (W - 2) + 2:W + 1], k, W - 1, -1.0)
+        fill(d[:, W * W - 1:W * W], k, 1, -1.0)
+
+    def resets(r):
+        W = LANES[r]
+        L, ns = W + 1, B0[r] + W // 2 + 1
+        e, k = T["DS%d" % r], "DS%d" % r
+        fill(e[:], k, NE[r], 1.0)
+        if r == 1:
+            fill(T.KA1[:, 24:25], "KA1z", 1, 1e6)
+        else:
+            fill(T["KA%d" % r][:, W:2 * W + 2:L], "KA%dz" % r, 2, 1e6)
+            fill(T["KA%d" % r][:, 32 + W:32 + 2 * W + 2:L], "KB%dz" % r, 2, 1e6)
+        fill(e[:, 0:ns * L:L], k, ns, 0.0)
+
+    for _ in together(pair_lists(1), key_lists(1)):
+        pass
+    vcopy(T.ul[:], "ul", T.ui[:], ["ui"])
+    vcopy(T.tw16[:], "tw16", T.tw32[:], ["tw32"])
+    ts(T.zi[:], "zi", T.iotaR[:, 0:516], ["iotaR", "p4"], col["p4"], A.is_equal, 0.5, A.mult)
+
+    act(T.m16[:], "m16", T.m16s[:, 0:16].indirect(T.il[:, 0:24]), ["m16s", "il"])
+    fill(T.seg16[:], "seg16", P, 1.0)
+    fill(T.KK[:, 23:24], "KK", 1, 1.0)
+    fill(T.seg16[:, 0:P:16], "seg16", 24, 0.0)
+    act(T.ms[:], "ms", T.iotaR[:, 0:P].indirect(T.tw16[:, 0:24]), ["iotaR", "tw16"])
+    dma("y", T.fe[:, :], T.ms[0:128:16, :], ["ms"], ["fe"])
+
+    CH = {1: [(0, 128), (128, 128), (256, 128)], 2: [(0, 256), (256, 128)], 3: [(0, 256), (256, 128)], 4: [(0, 192), (192, 192)]}
+    QK = {r: ["QX%d%d" % (r, i) for i in range(len(CH[r]))] for r in CH}
+    SK = {r: ["SS%d" % i for i in range(len(CH[r]))] for r in CH}
+
+    def quant_x(r):
+        for i, (a, n) in enumerate(CH[r]):
+            quant(T["QX%dc" % r][:, a:a + n], T["QX%ds" % r][:, a:a + n], QK[r][i], T[XB[r]][:, 4 * a:4 * (a + n)],
+                  ["X1%d" % i] if r == 1 else [XB[r] + "t%d" % t for t in range(5)])
+
+    def score_products(r):
+        for i, (a, n) in enumerate(CH[r]):
+            mm(4 + i, n, T.URc[:], T.URs[:], T["QX%dc" % r][:, a:a + n], T["QX%ds" % r][:, a:a + n], ["URc", "URs", QK[r][i]])
+
+    def unpack_products(qc, qs, banks, rds):
+        for b in range(4):
+            mm(banks[b], P, T.ECc[:, 128 * b:128 * b + 128], T.ECs[:, 128 * b:128 * b + 128], qc, qs, ["EC%d" % b] + rds)
+
+    def plane(r, t):
+        return T["V%d" % r][:, VW[r] * t:VW[r] * t + P]
+
+    def own_plane(r, t):
+        act(plane(r, t), "F%d%d" % (r, t), T["p%d" % t][:, 0:P], ["p%d" % t])
+
+    def second_planes():
+        for t, e in ((0, P), (1, P), (2, 192)):
+            act(T.FQ[:, P * t:P * t + e], "FQ%d" % t, T["p%d" % t][:, 0:e], ["p%d" % t])
+
+    def sort_keys(r, tbls, meanwhile):
+        W = LANES[r]
+        n16, n = 16 * W, NR[r]
+        tt(T.GM[:, 0:n16], "GM", T.SS[:].indirect(T.BL[:, 0:W]), T.m16[:, 0:n16], SK[r] + ["BL", "m16"], A.mult)
+        scan(T.SC[:, 0:n16], "SC", T.seg16[:, 0:n16], T.GM[:, 0:n16], ["seg16", "GM"], A.mult, A.add)
+        mn, mx, mnk, mxk = T["MN%d" % r], T["MX%d" % r], "MN%d" % r, "MX%d" % r
+        cuts = [(0, n)] if r > 1 else [(0, 192), (192, 384), (384, 576)]
+        for a, b in cuts:
+            lst = mx[:, a // 16:b // 16]
+            if r == 1:
+                act(T.BX[:, a:b], "BX%d" % a, T.SC[:].indirect(lst), ["SC", mxk])
+            else:
+                vcopy(T.BX[:, a:b], "BX%d" % a, T.SC[:].indirect(lst), ["SC", mxk])
+        meanwhile()
+        for a, b in cuts:
+            tt(T.C[:, a:b], "C%d" % a, T.SC[:].indirect(mn[:, a // 16:b // 16]), T.BX[:, a:b], ["SC", mnk, "BX%d" % a], A.is_ge)
+        scan(T.CS[:, 0:n], "CS", T["D0%d" % r][:], T.C[:, 0:n], ["D0%d" % r] + ["C%d" % a for a, b in cuts], A.mult, A.add)
+        add_keys(r, 0, "KA", tbls)
+
+    def add_keys(r, a, nm, tbls):
+        W = LANES[r]
+        for i, (tb, key) in enumerate(tbls):
+            c = a + i * (W + 1)
+            tt(T["KA%d" % r][:, c:c + W], "%s%d%d" % (nm, r, i), tb, T.CS[:, W - 1:W * W:W], [key, "CS"], A.subtract)
+
+    def extract(r, a, nm, d, dk):
+        W = LANES[r]
+        L, n = W + 1, NE[r]
+        ns = B0[r] + W // 2 + 1
+        width = 25 if r == 1 else 2 * L
+        rds = ["%s%d%d" % (nm, r, i) for i in range(1 if r == 1 else 2)] + ["%s%dz" % (nm, r)]
+        tt(T.M[:, 0:n], "M", T["KA%d" % r][:, a:a + width].indirect(T["KL%d" % r][:]), T["T%d" % r][:],
+           rds + ["KL%d" % r, "T%d" % r], A.min)
+        scan(T.HS[:, 0:n], "HS", T["DS%d" % r][:], T.M[:, 0:n], ["DS%d" % r, "M"], A.mult, A.add)
+        tt(d[:, 0:ns - 1], dk, T.HS[:, 2 * L - 1:ns * L:L], T.HS[:, L - 1:(ns - 1) * L:L], ["HS"], A.subtract)
+
+    def first_lists(r):
+        d, dk = T["D%d" % r], "D%d" % r
+        extract(r, 0, "KA", d, dk)
+        ts(T["CL%d" % r][:], "CL%d" % r, d[:, 0:B0[r] + LANES[r] // 2], [dk], 1024.0, A.mult, 383.0, A.min)
+
+    def select(out, w, a0, a1, m, n, rds, t1, t2):
+        ts(t1, "sel1" + w, a0, rds + [n], col[n], A.mult)
+        ts(t2, "sel2" + w, a1, rds + [m], col[m], A.mult)
+        tt(out, w, t1, t2, ["sel1" + w, "sel2" + w], A.add)
+
+    def lower(r, d, dk, out, w):
+        h = LANES[r] // 2
+        select(out, w, d[:, 0:h], d[:, 1:h + 1], "m0", "n0", [dk], T.tf[:, 352:352 + h], T.tf[:, 366:366 + h])
+
+    def upper_bases(r, d, dk, dz):
+        h, a = LANES[r] // 2, B0[r]
+        select(T.sl[:, 0:h + 1], "us", d[:, a - 1:a + h], d[:, a:a + h + 1], "m15", "n15", [dk, dz],
+               T.tf[:, 380:380 + h + 1], T.tf[:, 394:394 + h + 1])
+        ts(T.US[:, 0:h + 1], "US", T.sl[:, 0:h + 1], ["us"], 1024.0, A.mult, 383.0, A.min)
+
+    def rows_of_bases(r):
+        h = LANES[r] // 2
+        act(T.VB[:, 0:16 * (h + 1)], "VB", T.iotaR[:, 0:P].indirect(T.US[:, 0:h + 1]), ["iotaR", "US"])
+
+    def scatter_tops(r):
+        h, b0 = LANES[r] // 2, B0[r]
+        op("v", ["CL%d" % r, "iotaR"], ["UP"],
+           lambda: g.vector.tensor_copy(T.UP[:].indirect(T["CL%d" % r][:, b0:b0 + h]), T.iotaR[:, P:P + 16 * h]))
+
+    def scatter_links(r, low, lowk):
+        op("v", [lowk, "VB"], ["UP"], lambda: g.vector.tensor_copy(T.UP[:].indirect(low), T.VB[:, 15:15 + 8 * LANES[r]]))
+
+    def mask_up():
+        scan(T.ms[:], "ms", T.UP[:], T.m16[:], ["UP", "m16"], A.add, A.mult)
+
+    def blend_list():
+        scan(T.ht[:], "ht", T.seg16[:], T.ms[:], ["seg16", "ms"], A.mult, A.add)
+        vcopy(T.UL[:], "UL", T.ht[:, 15:P:16], ["ht"])
+
+    def shift_tops(r):
+        h, b0 = LANES[r] // 2, B0[r]
+        d, dk = T["D%d" % r], "D%d" % r
+        dma("y", T.tbT[1:128, 0:h], d[0:127, b0:b0 + h], [dk], ["tbT"])
+        dma("y", T.tbT[0:128:16, 0:h], d[15:128:16, b0:b0 + h], [dk], ["tbT"])
+
+    def make_e(r, win, wkeys, lst, lkey, meanwhile):
+        h, b0 = LANES[r] // 2, B0[r]
+        n = 16 * (h + 1)
+        for t in range(4):
+            act(T.tmp[:, n * t:n * t + n], "tmp%d" % t, win(t).indirect(lst[:, 0:h + 1]), [wkeys[t], lkey])
+        second_planes()
+        meanwhile()
+        for t in range(4):
+            tt(T["E%d" % r][:, t:64 * h:4], "E%d%d" % (r, t), win(t).indirect(lst[:, b0:b0 + h]),
+               T.tmp[:, n * t + 1:n * t + 1 + 16 * h], [wkeys[t], lkey, "tmp%d" % t], A.add)
+
+    def layer(r, ec, es, ekeys, n):
+        h, w, v = LANES[r] // 2, VW[r], T["V%d" % r]
+        for b in range(4):
+            mm(4 + b, n, T.WWc[:, 128 * b:128 * b + 128], T.WWs[:, 128 * b:128 * b + 128], ec, es, ["WWc", "WWs"] + ekeys)
+        for b in range(4):
+            act(v[:, w * b + P:w * b + P + 16 * h], "H%d%d" % (r, b), T["p%d" % (4 + b)][:, 0:16 * h], ["p%d" % (4 + b)], scale=0.015625)
+
+    def blend(r):
+        h, w = LANES[r] // 2, VW[r]
+        v, xn, xk = T["V%d" % r], T[XB[r + 1]], XB[r + 1]
+
+        def near(t, a, b):
+            return v[:, w * t:w * t + P + 16 * h].indirect(T.UL[:, a // 16:b // 16])
+
+        def keys(t):
+            return ["F%d%d" % (r, t), "H%d%d" % (r, t), "UL"]
+        act(T.tb[:, 0:P], "tb0", near(3, 0, P), keys(3))
+        act(T.tb[:, P:576], "tb1", near(2, 192, P), keys(2))
+        for t, e in ((0, P), (1, P), (2, 192)):
+            tt(xn[:, t:4 * e:4], xk + "t%d" % t, near(t, 0, e), T.FQ[:, P * t:P * t + e], keys(t) + ["FQ%d" % t], A.add)
+        tt(xn[:, 3:4 * P:4], xk + "t3", T.tb[:, 0:P], T.p3[:, 0:P], ["tb0", "p3"], A.add)
+        tt(xn[:, 770:4 * P:4], xk + "t4", T.tb[:, P:576], T.p2[:, 192:P], ["tb1", "p2"], A.add)
+
+    def later_pads():
+        memset(T.E2[:, 384:512], "E2z", 0.0)
+        memset(T.E3[:, 192:704], "E3z", 0.0)
+        quant(T.LE2c[:, 96:224], T.LE2s[:, 96:224], "LE2z", T.E3[:, 192:704], ["E3z"])
+        quant(T.LE3c[:, 48:176], T.LE3s[:, 48:176], "LE3z", T.E3[:, 192:704], ["E3z"])
+
+    f1, f2, f2t = thresholds(1), together(pair_lists(2), key_lists(2)), thresholds(2)
+    f3 = together(pair_lists(3), key_lists(3), thresholds(3))
+
+    def pump(f, n=99):
+        for _ in range(n):
+            if next(f, 1) is not None:
+                break
+
+    quant_x(1)
+    quant(T.QUc[:], T.QUs[:], "QU", T.ub[:], ["ub"])
+    vcopy(T.URc[:].bitcast(dt.uint32), "URc", T.QUc[:].bitcast(dt.uint32).indirect(T.ul[:, 0:8]), ["QU", "ul"])
+    act(T.URs[:], "URs", T.QUs[:].indirect(T.ul[:, 0:8]), ["QU", "ul"])
+    send(T.LXc[:].bitcast(dt.uint8), T.QX1c[:].bitcast(dt.uint8), "axc", QK[1], "LX")
+    send(T.LXs[:], T.QX1s[:], "axs", QK[1], "LX")
+    score_products(1)
+    for i, (a, n) in enumerate(CH[1]):
+        act(T.SS[:, a:a + n], "SS%d" % i, T["p%d" % (4 + i)][:, 0:n], ["p%d" % (4 + i)])
+    pump(f1, 3)
+    signs(1)
+    for b in range(4):
+        quant(T.ECc[:, 128 * b:128 * b + 128], T.ECs[:, 128 * b:128 * b + 128], "EC%d" % b, T.zi[:, 3 - b:515 - b], ["zi"])
+    unpack_products(T.QX1c[:], T.QX1s[:], (0, 1, 2, 3), QK[1])
+    later_pads()
+    ts(T.sl[:, 0:24], "us", T.fe[:], ["fe"], 1.0 / 1024, A.mult)
+    vcopy(T.BL[:], "BL", T.fe[:], ["fe"])
+    tt(T.tbB[:], "tbB", T.sl[:, 0:24], T.KK[:], ["us", "KK"], A.add)
+
+    def r1_gap():
+        pump(f1)
+        pump(f2, 2)
+        resets(1)
+        pump(f2t, 3)
+    sort_keys(1, [(T.tbB[:], "tbB")], r1_gap)
+    for t in range(4):
+        own_plane(1, t)
+    first_lists(1)
+    send(T.LL[:], T.CL1[:], "all1", ["CL1"], "LL")
+
+    fill(T.D1[:, 26:27], "Dz1", 1, 0.0)
+    fill(T.DB[:, 14:15], "DBz2", 1, 0.0)
+    iota(T.opc[:, 0:48], "opc", [[1, 3], [3, 16]], P + 3, 0)
+    iota(T.opc[:, 48:51], "opf", [[1, 3]], P, 0)
+    unpack_products(T.LXc[:], T.LXs[:], (4, 5, 6, 7), ["LX"])
+    upper_bases(1, T.D1, "D1", "Dz1")
+    scatter_tops(1)
+    for t in range(4):
+        act(T.FP[:, P * t:P * t + P], "FP%d" % t, T["p%d" % (4 + t)][:, 0:P], ["p%d" % (4 + t)])
+        if t == 1:
+            rows_of_bases(1)
+    lower(1, T.D1, "D1", T.tbB[:, 0:12], "tbB")
+    ts(T.BL[:, 0:12], "BL", T.tbB[:, 0:12], ["tbB"], 1024.0, A.mult)
+    tt(T.tbB[:, 0:12], "tbB", T.tbB[:, 0:12], T.KK[:, 12:24], ["tbB", "KK"], A.add)
+    pump(f2)
+    pump(f2t)
+    scatter_links(1, T.BL[:, 0:12], "BL")
+    shift_tops(1)
+    make_e(1, lambda t: T.FP[:, P * t:P * t + P], ["FP%d" % t for t in range(4)], T.LL, "LL", mask_up)
+    quant(T.QE1c[:], T.QE1s[:], "QE1", T.E1[:], ["E1%d" % t for t in range(4)])
+    layer(1, T.QE1c[:], T.QE1s[:], ["QE1"], 192)
+    blend_list()
+    blend(1)
+
+    for r in (2, 3):
+        W = LANES[r]
+        h, b0 = W // 2, B0[r]
+        n = 16 * h
+        tbB, tbT = T.tbB[:, 0:W], T.tbT[:, 0:W]
+        quant_x(r)
+        score_products(r)
+        unpack_products(T["QX%dc" % r][:], T["QX%ds" % r][:], (0, 1, 2, 3), QK[r])
+        if r == 2:
+            signs(2)
+            resets(2)
+        tt(tbT, "tbT", tbT, T.KK[:, 24 - W:24], ["tbT", "KK"], A.add)
+        vcopy(T.SS[:, 0:256], "SS0", T.p4[:, 0:256], ["p4"])
+        act(T.SS[:, 256:P], "SS1", T.p5[:, 0:128], ["p5"])
+        for t in range(4):
+            own_plane(r, t)
+        if r == 2:
+            signs(3)
+            resets(3)
+        sort_keys(r, [(tbB, "tbB"), (tbT, "tbT")], lambda: None)
+        first_lists(r)
+
+        def e_gap():
+            add_keys(r, 32, "KB", [(tbT, "tbT"), (tbB, "tbB")])
+        make_e(r, lambda t: plane(r, t), ["F%d%d" % (r, t) for t in range(4)], T["CL%d" % r], "CL%d" % r, e_gap)
+        quant(T["QE%dc" % r][:], T["QE%ds" % r][:], "QE%d" % r, T["E%d" % r][:, 0:512], ["E%d%d" % (r, t) for t in range(4)] + ["E%dz" % r])
+        send(T["LE%dc" % r][:, 0:n].bitcast(dt.uint8), T["QE%dc" % r][:, 0:n].bitcast(dt.uint8), "a%dc" % r, ["QE%d" % r], "LE%d" % r)
+        send(T["LE%ds" % r][:, 0:n], T["QE%ds" % r][:, 0:n], "a%ds" % r, ["QE%d" % r], "LE%d" % r)
+        if r == 2:
+            shift_tops(2)
+        else:
+            fill(T.DB[:, 9:10], "DBz3", 1, 0.0)
+        extract(r, 32, "KB", T.DB, "DB")
+        upper_bases(r, T.DB, "DB", "DBz%d" % r)
+        rows_of_bases(r)
+        scatter_tops(r)
+        lower(r, T.DB, "DB", T.sl[:, 16:16 + h], "tl")
+        ts(T.SL[:, 0:h], "SL", T.sl[:, 16:16 + h], ["tl"], 1024.0, A.mult)
+        scatter_links(r, T.SL[:, 0:h], "SL")
+        mask_up()
+        blend_list()
+        if r == 2:
+            lower(2, T.D2, "D2", T.tbB[:, 0:6], "tbB")
+            ts(T.BL[:, 0:6], "BL", T.tbB[:, 0:6], ["tbB"], 1024.0, A.mult)
+            tt(T.tbB[:, 0:6], "tbB", T.tbB[:, 0:6], T.KK[:, 18:24], ["tbB", "KK"], A.add)
+            pump(f3)
+        else:
+            op("v", ["opc", "opf"], ["opc"], lambda: g.vector.tensor_copy(T.opc[:, 15:48:16], T.opc[:, 48:51]))
+            op("v", ["opc", "CL3"], ["UP"], lambda: g.vector.tensor_copy(T.UP[:].indirect(T.CL3[:, b0:b0 + h]), T.opc[:, 0:48]))
+            dma("y", T.op[:, :], T.UP[0:128:16, :], ["UP"], ["op"])
+            quant(T.QVc[:], T.QVs[:], "QV", T.vb[:], ["vb"])
+        layer(r, T["LE%dc" % r][:, 0:128], T["LE%ds" % r][:, 0:128], ["LE%d" % r, "LE%dz" % r], 128)
+        blend(r)
+
+    quant_x(4)
+    for i, (a, n) in enumerate(CH[4]):
+        mm(4 + i, n, T.QVc[:], T.QVs[:], T.QX4c[:, a:a + n], T.QX4s[:, a:a + n], ["QV", QK[4][i]])
+    dma("s", T.oc[:, :], T.QX4c[:].bitcast(dt.uint8), QK[4], ["oc"])
+    for k2 in range(4):
+        dma("s" if k2 < 2 else "y", T.osc[4 * k2:4 * k2 + 4, :], T.QX4s[32 * k2:32 * k2 + 4, :], QK[4], ["osc%d" % k2])
+    for i, (a, n) in enumerate(CH[4]):
+        vcopy(T.ysb[:, a:a + n], "ysb%d" % i, T["p%d" % (4 + i)][:, 0:n], ["p%d" % (4 + i)])
+        dma("y", T.y[:, a:a + n], T.ysb[:, a:a + n], ["ysb%d" % i], ["y%d" % i])
+
+    for sem, val in cnt.items():
+        if known["g"].get(sem, 0) < val:
+            g.wait_ge(T.sem[sem], val)

@@ -1,16 +1,19 @@
 from concourse.mybir import dt, AluOpType, ActivationFunctionType
 
 A = AluOpType
-COPY = ActivationFunctionType.Copy
+AF = ActivationFunctionType
 P = 384
 LANES = {1: 24, 2: 12, 3: 6}
 B0 = {1: 14, 2: 8, 3: 6}
 NR = {1: 576, 2: 144, 3: 48}
 NE = {1: 688, 2: 208, 3: 80}
-SG0 = {1: 0, 2: 44, 3: 58}
-VW = {1: 576, 2: 480, 3: 432}
+K0 = {1: 0, 2: 32, 3: 64}
+VW = 576
+LAND = {1: 96, 2: 0, 3: 480}
+OWN = (P, 96)
 XB = {1: "X1", 2: "X2", 3: "X3", 4: "X2"}
 BF, F32, U16, I32, U8, FP8 = "bfloat16", "float32", "uint16", "int32", "uint8", "float8_e4m3fn_x4"
+SIZE = {BF: 2, F32: 4, U16: 2, I32: 4, U8: 1, FP8: 4}
 
 SCRATCH = {}
 
@@ -20,32 +23,48 @@ def _buf(name, cols, dtype, where="sbuf"):
 
 
 for _n, _c in (("QX1", P), ("QX2", P), ("QX3", P), ("QX4", P), ("QU", 128), ("UR", 128), ("QV", 128), ("WW", 512),
-               ("EC", 512), ("LX", P), ("LE2", 224), ("LE3", 176), ("QE1", 192), ("QE2", 128), ("QE3", 128)):
+               ("EC", 512), ("LB", 528), ("QE1", 192), ("QE2", 128), ("QE3", 128)):
     _buf(_n + "c", _c, FP8)
     _buf(_n + "s", _c, U8)
 for _n, _c, _t in (
-        ("X1", 4 * P, BF), ("X2", 4 * P, BF), ("X3", 4 * P, BF), ("ub", 512, BF), ("vb", 512, BF), ("half", 704, BF),
-        ("zi", 516, BF), ("FP", 4 * P, BF), ("FQ", 960, BF), ("E1", 768, BF), ("E2", 512, BF), ("E3", 704, BF),
-        ("tmp", 832, BF), ("tb", 576, BF), ("m16s", 16, BF), ("m16", P, BF), ("seg16", P, BF), ("C", 576, BF), ("CS", 576, BF),
+        ("X1", 4 * P, BF), ("X2", 4 * P, BF), ("X3", 4 * P, BF), ("ub", 512, BF), ("vb", 512, BF), ("half", 688, BF),
+        ("zi", 516, BF), ("FP", 4 * P, BF), ("V", 4 * VW, BF), ("FQ", 2 * P, BF), ("E", 768, BF), ("tmp", 832, BF), ("tb", 4 * P, BF),
+        ("m16s", 16, BF), ("m16", P, BF), ("hold", P, BF), ("climb", P, BF), ("C", 576, BF), ("CS", 576, BF),
         ("tw32", 24, I32), ("ic", 24, I32), ("mi", 16, I32), ("ui", 8, I32), ("ti", 96, I32),
-        ("tw16", 24, U16), ("il", 24, U16), ("ul", 8, U16), ("LL", 26, U16), ("SL", 12, U16),
-        ("US", 14, U16), ("BL", 24, U16), ("UL", 24, U16), ("SG", 64, U16),
-        ("cols", 8, F32), ("iotaR", 576, F32), ("J", 44, F32), ("KK", 24, F32), ("fe", 24, F32), ("R", 96, F32),
-        ("opc", 52, F32), ("UP", P, F32), ("ms", P, F32), ("ht", P, F32), ("ysb", P, F32),
-        ("SS", P, F32), ("GM", P, F32), ("SC", P, F32), ("BX", 576, F32), ("M", 688, F32), ("HS", 688, F32),
-        ("tf", 448, F32), ("sl", 32, F32), ("DB", 28, F32), ("VB", 208, F32), ("tbB", 24, F32), ("tbT", 12, F32)):
+        ("tw16", 24, U16), ("il", 24, U16), ("ul", 8, U16), ("LL", 26, U16), ("CB", 16, U16), ("BL", 24, U16), ("UL", 24, U16),
+        ("cols", 8, F32), ("iotaR", 576, F32), ("J", 44, F32), ("KK", 24, F32), ("fe", 24, F32), ("opc", 52, F32),
+        ("UP", P + 16, F32), ("ms", P, F32), ("ht", P, F32), ("ysb", P, F32), ("SS", P, F32), ("GM", P, F32), ("SC", P, F32),
+        ("BX", 576, F32), ("M", 688, F32), ("HS", 688, F32), ("tf", 448, F32), ("sl", 24, F32), ("DB", 16, F32),
+        ("VB", 208, F32), ("tbB", 24, F32), ("tbT", 12, F32), ("nB", 12, F32), ("nT", 12, F32), ("KA", 80, F32)):
     _buf(_n, _c, _t)
 for _r in (1, 2, 3):
     _h = LANES[_r] // 2
-    for _n, _c, _t in (("V", 4 * VW[_r], BF), ("D0", NR[_r], BF), ("DS", NE[_r], BF), ("KA", 64, F32), ("T", NE[_r], F32),
-                       ("D", 28, F32), ("CL", B0[_r] + _h, U16),
-                       ("MN", NR[_r] // 16, U16), ("MX", NR[_r] // 16, U16), ("KL", NE[_r] // 16, U16)):
+    _L = LANES[_r] + 1
+    for _n, _c, _t in (("D0", NR[_r], BF), ("DS", NE[_r], BF), ("T", (B0[_r] + _h + 3) * _L, F32), ("D", 28, F32),
+                       ("CL", B0[_r] + _h, U16), ("MN", NR[_r] // 16, U16), ("MX", NR[_r] // 16, U16),
+                       ("KL", NE[_r] // 16, U16), ("KB", NE[_r] // 16, U16)):
         _buf(_n + str(_r), _c, _t)
 for _i in range(8):
     _buf("p%d" % _i, 512, F32, "psum")
 
-NDMA = 26
+NDMA = 40
 SEMAPHORES = ["vs", "ss", "ts", "gs", "loc", "axc", "axs", "all1", "a2c", "a2s", "a3c", "a3s"] + ["d%d" % i for i in range(NDMA)]
+
+
+def v(name, a=0, b=None, step=1, rows=None):
+    return {"n": name, "a": a, "b": SCRATCH[name][1][1] if b is None else b, "s": step, "rows": rows, "by": None, "as": None}
+
+
+def by(win, lst):
+    return dict(win, by=lst)
+
+
+def words(x):
+    return dict(x, **{"as": dt.uint32})
+
+
+def raw(x):
+    return dict(x, **{"as": dt.uint8})
 
 
 def rank_program(g, core, T, topo):
@@ -59,14 +78,46 @@ def rank_program(g, core, T, topo):
 
     ENG = {"v": g.vector, "s": g.scalar, "t": g.tensor, "g": g, "y": g.sync}
     QSEM = {"v": "vs", "s": "ss", "t": "ts", "g": "gs"}
-    cnt, known, wr, rd, nd = {}, {q: {} for q in ENG}, {}, {}, [0]
+    cnt, known, seen, nd = {}, {q: {} for q in ENG}, {}, [0]
 
-    def before(q, reads, writes):
+    def ap(x):
+        if not isinstance(x, dict):
+            return x
+        a = T[x["n"]][x["rows"] if x["rows"] is not None else slice(None), x["a"]:x["b"]:x["s"]]
+        if x["as"] is not None:
+            a = a.bitcast(x["as"])
+        return a if x["by"] is None else a.indirect(ap(x["by"]))
+
+    def bits(x, blocks=False):
+        where, shape, dtype = SCRATCH[x["n"]]
+        if where == "psum":
+            return 1
+        m = 0
+        k = 16 // SIZE[dtype] if blocks else 1
+        for c in range(x["a"], x["b"], x["s"]):
+            m |= ((1 << k) - 1) << (c - c % k)
+        return m
+
+    def touches(q, reads, writes, dma_):
+        acc = []
+        for x in reads:
+            if isinstance(x, dict):
+                acc.append((x["n"], bits(x), False))
+                if x["by"] is not None:
+                    acc.append((x["by"]["n"], bits(x["by"]), False))
+        for x in writes:
+            if isinstance(x, dict):
+                acc.append((x["n"], bits(x, dma_), True))
+                if x["by"] is not None:
+                    acc.append((x["by"]["n"], bits(x["by"]), False))
+        return acc
+
+    def before(q, acc):
         ev = []
-        for k in reads:
-            ev += wr.get(k, [])
-        for k in writes:
-            ev += wr.get(k, []) + rd.get(k, [])
+        for n, m, w in acc:
+            for m2, w2, q2, e in seen.get(n, []):
+                if m & m2 and (w or w2 or (SCRATCH[n][0] == "psum" and q != q2)):
+                    ev.append(e)
         for sem, val, clock in sorted(ev, key=lambda e: -e[1]):
             if known[q].get(sem, 0) < val:
                 ENG[q].wait_ge(T.sem[sem], val)
@@ -74,161 +125,147 @@ def rank_program(g, core, T, topo):
                     if known[q].get(k2, 0) < v2:
                         known[q][k2] = v2
 
-    def after(q, sem, reads, writes):
+    def after(q, sem, acc):
         clock = dict(known[q])
         clock[sem] = cnt[sem]
-        ev = (sem, cnt[sem], clock)
-        for k in reads:
-            rd.setdefault(k, []).append(ev)
-        for k in writes:
-            wr[k] = [ev]
-            rd[k] = []
+        for n, m, w in acc:
+            old = seen.get(n, [])
+            if w:
+                old = [e for e in old if e[0] & ~m]
+            seen[n] = old + [(m, w, q, (sem, cnt[sem], clock))]
 
     def op(q, reads, writes, fn):
-        before(q, reads, writes)
+        acc = touches(q, reads, writes, False)
+        before(q, acc)
         sem = QSEM[q]
         fn().then_inc(T.sem[sem], 1)
         cnt[sem] = cnt.get(sem, 0) + 1
-        after(q, sem, reads, writes)
+        after(q, sem, acc)
 
-    def dma(q, out, in_, reads, writes):
-        before(q, reads, writes)
+    def dma(q, out, in_):
+        acc = touches(q, [in_], [out], True)
+        before(q, acc)
         sem = "d%d" % nd[0]
         nd[0] += 1
-        ENG[q].dma_start(out, in_).then_inc(T.sem[sem], 16)
+        ENG[q].dma_start(ap(out), ap(in_)).then_inc(T.sem[sem], 16)
         cnt[sem] = 16
-        after(q, sem, reads, writes)
+        after(q, sem, acc)
 
-    def send(out, in_, sem, reads, lands):
-        before("g", reads, [])
-        g.remote_dma(out, in_, T.sem[sem], T.sem.loc, pid, rid, mask)
+    def send(out, in_, sem):
+        before("g", touches("g", [in_], [], False))
+        g.remote_dma(ap(out), ap(in_), T.sem[sem], T.sem.loc, pid, rid, mask)
         cnt["loc"] = cnt.get("loc", 0) + neng
         cnt[sem] = neng
-        wr[lands] = wr.get(lands, []) + [(sem, neng, {sem: neng})]
+        seen.setdefault(out["n"], []).append((bits(out), True, "r", (sem, neng, {sem: neng})))
 
-    def ts(out, w, in0, rds, s1, op0, s2=None, op1=None):
+    def ts(out, in0, s1, op0, s2=None, op1=None):
         if op1 is None:
-            op("v", rds, [w], lambda: g.vector.tensor_scalar(out, in0, s1, None, op0))
+            op("v", [in0, s1], [out], lambda: g.vector.tensor_scalar(ap(out), ap(in0), ap(s1), None, op0))
         else:
-            op("v", rds, [w], lambda: g.vector.tensor_scalar(out, in0, s1, s2, op0, op1))
+            op("v", [in0, s1, s2], [out], lambda: g.vector.tensor_scalar(ap(out), ap(in0), ap(s1), ap(s2), op0, op1))
 
-    def tt(out, w, in0, in1, rds, o):
-        op("v", rds, [w], lambda: g.vector.tensor_tensor(out, in0, in1, o))
+    def tt(out, in0, in1, o):
+        op("v", [in0, in1], [out], lambda: g.vector.tensor_tensor(ap(out), ap(in0), ap(in1), o))
 
-    def vcopy(out, w, in_, rds):
-        op("v", rds, [w], lambda: g.vector.tensor_copy(out, in_))
+    def vcopy(out, in_):
+        op("v", [in_], [out], lambda: g.vector.tensor_copy(ap(out), ap(in_)))
 
-    def memset(out, w, k):
-        op("v", [], [w], lambda: g.vector.memset(out, k))
+    def memset(out, k):
+        op("v", [], [out], lambda: g.vector.memset(ap(out), k))
 
-    def scan(out, w, d0, d1, rds, o0, o1):
-        op("v", rds, [w], lambda: g.vector.tensor_tensor_scan(out, d0, d1, 0.0, o0, o1))
+    def scan(out, d0, d1, o0, o1):
+        op("v", [d0, d1], [out], lambda: g.vector.tensor_tensor_scan(ap(out), ap(d0), ap(d1), 0.0, o0, o1))
 
-    def act(out, w, in_, rds, scale=None):
-        if scale is None:
-            op("s", rds, [w], lambda: g.scalar.activation(out, in_, COPY))
+    def act(out, in_, func=AF.Copy, **kw):
+        op("s", [in_] + list(kw.values()), [out], lambda: g.scalar.activation(ap(out), ap(in_), func, **{k: ap(x) for k, x in kw.items()}))
+
+    def fill(out, n, value):
+        act(out, v("half", 0, n), scale=2.0 * value)
+
+    def quant(q, a, b, in_):
+        qc, qs = v(q + "c", a, b), v(q + "s", a, b)
+        op("v", [in_], [qc, qs], lambda: g.vector.quantize_mx(ap(qc), ap(qs), ap(in_)))
+
+    def mm(bank, l, la, r, ra, n):
+        sides = [v(l + "c", la, la + 128), v(l + "s", la, la + 128), v(r + "c", ra, ra + n), v(r + "s", ra, ra + n)]
+        out = v("p%d" % bank, 0, n)
+        op("t", sides, [out], lambda: g.tensor.matmul_mx(ap(out), *[ap(x) for x in sides], True, True))
+
+    def iota(out, pattern, base, cm=0):
+        if SCRATCH[out["n"]][2] == I32:
+            op("g", [], [out], lambda: g.iota(ap(out), pattern, base, cm))
         else:
-            op("s", rds, [w], lambda: g.scalar.activation(out, in_, COPY, scale=scale))
+            op("g", [], [out], lambda: g.iota(ap(out), pattern, base, cm, allow_small_or_imprecise_dtypes=True))
 
-    def fill(out, w, n, value):
-        act(out, w, T.half[:, 0:n], ["half"], scale=2.0 * value)
-
-    def quant(qc, qs, w, in_, rds):
-        op("v", rds, [w], lambda: g.vector.quantize_mx(qc, qs, in_))
-
-    def mm(bank, n, lc, ls, rc, rs, rds):
-        op("t", rds, ["p%d" % bank], lambda: g.tensor.matmul_mx(T["p%d" % bank][:, 0:n], lc, ls, rc, rs, True, True))
-
-    def iota(out, w, pattern, base, cm, flt=True):
-        if flt:
-            op("g", [], [w], lambda: g.iota(out, pattern, base, cm, allow_small_or_imprecise_dtypes=True))
+    def evac(q, out, in_, scale=None):
+        if q == "s":
+            act(out, in_, **({} if scale is None else {"scale": scale}))
+        elif scale is None:
+            vcopy(out, in_)
         else:
-            op("g", [], [w], lambda: g.iota(out, pattern, base, cm))
+            ts(out, in_, scale, A.mult)
 
-    col = {k2: T.cols[:, i:i + 1] for i, k2 in enumerate(("i", "m0", "n0", "m15", "n15", "p4"))}
-
-    dma("s", T.tw32[:], T.tw[:, :], [], ["tw32"])
-    for c in range(3):
-        dma("y", T.X1[:, 512 * c:512 * c + 512], T.x[:, 512 * c:512 * c + 512], [], ["X1%d" % c])
-    dma("s", T.ub[:], T.u[:, :], [], ["ub"])
-    dma("y", T.WWc[:].bitcast(dt.uint8), T.wc[:, :], [], ["WWc"])
-    dma("y", T.WWs[:], T.ws[:, :], [], ["WWs"])
-    dma("y", T.vb[:], T.v[:, :], [], ["vb"])
-
-    iota(T.ic[:], "ic", [[0, 24]], 0, 1, False)
-    iota(T.J[:], "J", [[16, 44]], 0, 0)
-    iota(T.mi[:], "mi", [[1, 16]], 128, -1, False)
-    iota(T.iotaR[:], "iotaR", [[1, 576]], 0, 0)
-    iota(T.ui[:], "ui", [[16, 8]], 0, 0, False)
-    iota(T.KK[:], "KK", [[-1, 24]], 22, 0)
-    for r in (1, 2, 3):
-        iota(T.R[:, 32 * r - 32:32 * r - 32 + B0[r]], "Ra%d" % r, [[1, B0[r]]], 0, 0)
-        iota(T.R[:, 32 * r - 32 + B0[r]:32 * r], "Rb%d" % r, [[1, 32 - B0[r]]], LANES[r] // 2, 0)
-
-    ts(col["p4"], "p4", T.ic[:, 0:1], ["ic"], 4.0, A.mult, 3.0, A.add)
-    ts(T.ic[:], "ic", T.ic[:], ["ic"], 15, A.bitwise_and)
-    ts(T.mi[:], "mi", T.mi[:], ["mi"], 15, A.bitwise_and)
-    ts(col["i"], "ci", T.ic[:, 0:1], ["ic"], 1.0, A.mult)
-    vcopy(T.il[:], "il", T.ic[:], ["ic"])
-    ts(T.m16s[:], "m16s", T.mi[:], ["mi"], 0.0, A.is_equal)
-    ts(T.J[:], "J", T.J[:], ["J", "ci"], col["i"], A.add)
-    memset(T.half[:], "half", 0.5)
-    for k2, val, o in (("m0", 0.0, A.is_equal), ("n0", 0.0, A.not_equal), ("m15", 15.0, A.is_equal), ("n15", 15.0, A.not_equal)):
-        ts(col[k2], k2, T.ic[:, 0:1], ["ic"], val, o)
+    col = {k2: v("cols", i, i + 1) for i, k2 in enumerate(("i", "m0", "minus0", "rise"))}
 
     def pair_lists(r):
         W, n = LANES[r], NR[r] // 16
-        j = T.J[:, 0:n]
-        k, kw, kp, mn, mx = T.ti[:, 0:n], T.tf[:, 0:n], T.tf[:, 48:48 + n], T.tf[:, 96:96 + n], T.tf[:, 144:144 + n]
-        ts(k, "k", j, ["J"], 1.0 / W, A.mult, -(W - 1) / (2.0 * W), A.add)
+        j = v("J", 0, n)
+        k, kw, kp, mn, mx = v("ti", 0, n), v("tf", 0, n), v("tf", 48, 48 + n), v("tf", 96, 96 + n), v("tf", 144, 144 + n)
+        ts(k, j, 1.0 / W, A.mult, -(W - 1) / (2.0 * W), A.add)
         yield
-        ts(kw, "kw", k, ["k"], -float(W), A.mult)
+        ts(kw, k, -float(W), A.mult)
         yield
-        tt(kp, "kp", j, kw, ["J", "kw"], A.add)
+        tt(kp, j, kw, A.add)
         yield
-        tt(mn, "mn", k, kp, ["k", "kp"], A.min)
-        tt(mx, "mx", k, kp, ["k", "kp"], A.max)
+        tt(mn, k, kp, A.min)
+        tt(mx, k, kp, A.max)
         yield
-        ts(T["MX%d" % r][:], "MX%d" % r, mx, ["mx"], 16.0, A.mult, 15.0, A.add)
-        ts(T["MN%d" % r][:], "MN%d" % r, mn, ["mn"], 16.0, A.mult, 15.0, A.add)
+        ts(v("MX%d" % r), mx, 16.0, A.mult, 15.0, A.add)
+        ts(v("MN%d" % r), mn, 16.0, A.mult, 15.0, A.add)
         yield
 
     def key_lists(r):
         n, L, b0 = NE[r] // 16, LANES[r] + 1, B0[r]
-        j = T.J[:, 0:n]
-        sg, sl, ps, ad = T.ti[:, 48:48 + n], T.tf[:, 192:192 + n], T.tf[:, 256:256 + n], T.tf[:, 320:320 + n]
-        ts(sg, "sg", j, ["J"], 1.0 / L, A.mult, -(L - 1) / (2.0 * L), A.add)
+        j = v("J", 0, n)
+        sg, sl, ps, ad = v("ti", 48, 48 + n), v("tf", 192, 192 + n), v("tf", 240, 240 + n), v("tf", 288, 288 + n)
+        s1, s2 = v("tf", 304, 304 + n), v("tf", 320, 320 + n)
+        ts(sg, j, 1.0 / L, A.mult, -(L - 1) / (2.0 * L), A.add)
         yield
-        ts(sl, "slv", sg, ["sg"], -float(L), A.mult)
-        vcopy(T.SG[:, SG0[r]:SG0[r] + n], "SG%d" % r, sg, ["sg"])
+        ts(sl, sg, -float(L), A.mult)
+        if r > 1:
+            ts(ad, j, float(b0 * L), A.is_ge, float(L), A.mult)
         yield
-        tt(ps, "psv", j, sl, ["J", "slv"], A.add)
+        tt(ps, j, sl, A.add)
         yield
         if r == 1:
-            vcopy(T.KL1[:], "KL1", ps, ["psv"])
+            vcopy(v("KL1"), ps)
         else:
-            ts(ad, "adv", j, ["J"], float(b0 * L), A.is_ge, float(L), A.mult)
+            tt(s1, ps, ad, A.add)
+            tt(s2, ps, ad, A.subtract)
             yield
-            tt(sl, "slv", ps, ad, ["psv", "adv"], A.add)
-            yield
-            vcopy(T["KL%d" % r][:], "KL%d" % r, sl, ["slv"])
+            vcopy(v("KL%d" % r), s1)
+            ts(v("KB%d" % r), s2, float(L), A.add)
         yield
 
-    def thresholds(r):
+    def threshold_rows(r):
+        L, b0, t = LANES[r] + 1, B0[r], "T%d" % r
+        iota(v(t, 0, b0 * L), [[1, b0], [0, L]], 0)
+        iota(v(t, b0 * L), [[1, LANES[r] // 2 + 3], [0, L]], LANES[r] // 2)
+
+    def tower0(r):
+        x = v("T%d" % r, 0, B0[r] * (LANES[r] + 1))
+        act(x, x, AF.Relu, bias=col["minus0"])
+
+    def cancels(r):
         W = LANES[r]
-        L, b0, n = W + 1, B0[r], NE[r]
-        ns = b0 + W // 2 + 1
-        t, R, a, b = T["T%d" % r], T.R[:, 32 * r - 32:32 * r], "Ra%d" % r, "Rb%d" % r
-        ts(R[:, 0:b0], a, R[:, 0:b0], [a, "m0"], col["m0"], A.subtract, 0.0, A.max)
+        L, t = W + 1, "T%d" % r
+        ns = B0[r] + W // 2 + 1
+        u = v("tf", 416, 416 + ns)
+        ts(u, v(t, 0, ns * L, L), 0.5, A.mult, -(W - 0.5), A.add)
         yield
-        u = T.tf[:, 416:416 + ns]
-        ts(u, "uv", R[:, 0:ns], [a, b], 0.5, A.mult, -(W - 0.5), A.add)
+        tt(v(t, W, ns * L, L), v(t, 0, ns * L, L), u, A.mult)
         yield
-        act(t[:], "T%d" % r, R.indirect(T.SG[:, SG0[r]:SG0[r] + n // 16]), [a, b, "SG%d" % r])
-        yield
-        yield
-        yield
-        tt(t[:, W:ns * L:L], "T%d" % r, R[:, 0:ns], u, [a, b, "uv"], A.mult)
+        ts(v(t, W, W + 1), col["m0"], -P / 1024.0, A.mult)
         yield
 
     def together(*gens):
@@ -238,310 +275,315 @@ def rank_program(g, core, T, topo):
             yield
 
     def signs(r):
-        W, d, k = LANES[r], T["D0%d" % r], "D0%d" % r
-        fill(d[:], k, NR[r], 1.0)
-        fill(d[:, 0:W * W:W], k, W, 0.0)
-        fill(d[:, 1:(W + 1) * (W - 2) + 2:W + 1], k, W - 1, -1.0)
-        fill(d[:, W * W - 1:W * W], k, 1, -1.0)
+        W, d = LANES[r], "D0%d" % r
+        fill(v(d), NR[r], 1.0)
+        fill(v(d, 0, W * W, W), W, 0.0)
+        fill(v(d, 1, (W + 1) * (W - 2) + 2, W + 1), W - 1, -1.0)
+        fill(v(d, W * W - 1, W * W), 1, -1.0)
 
     def resets(r):
         W = LANES[r]
-        L, ns = W + 1, B0[r] + W // 2 + 1
-        e, k = T["DS%d" % r], "DS%d" % r
-        fill(e[:], k, NE[r], 1.0)
-        if r == 1:
-            fill(T.KA1[:, 24:25], "KA1z", 1, 1e6)
-        else:
-            fill(T["KA%d" % r][:, W:2 * W + 2:L], "KA%dz" % r, 2, 1e6)
-            fill(T["KA%d" % r][:, 32 + W:32 + 2 * W + 2:L], "KB%dz" % r, 2, 1e6)
-        fill(e[:, 0:ns * L:L], k, ns, 0.0)
-
-    for _ in together(pair_lists(1), key_lists(1)):
-        pass
-    vcopy(T.ul[:], "ul", T.ui[:], ["ui"])
-    vcopy(T.tw16[:], "tw16", T.tw32[:], ["tw32"])
-    ts(T.zi[:], "zi", T.iotaR[:, 0:516], ["iotaR", "p4"], col["p4"], A.is_equal, 0.5, A.mult)
-
-    act(T.m16[:], "m16", T.m16s[:, 0:16].indirect(T.il[:, 0:24]), ["m16s", "il"])
-    fill(T.seg16[:], "seg16", P, 1.0)
-    fill(T.KK[:, 23:24], "KK", 1, 1.0)
-    fill(T.seg16[:, 0:P:16], "seg16", 24, 0.0)
-    act(T.ms[:], "ms", T.iotaR[:, 0:P].indirect(T.tw16[:, 0:24]), ["iotaR", "tw16"])
-    dma("y", T.fe[:, :], T.ms[0:128:16, :], ["ms"], ["fe"])
-
-    CH = {1: [(0, 128), (128, 128), (256, 128)], 2: [(0, 256), (256, 128)], 3: [(0, 256), (256, 128)], 4: [(0, 192), (192, 192)]}
-    QK = {r: ["QX%d%d" % (r, i) for i in range(len(CH[r]))] for r in CH}
-    SK = {r: ["SS%d" % i for i in range(len(CH[r]))] for r in CH}
-
-    def quant_x(r):
-        for i, (a, n) in enumerate(CH[r]):
-            quant(T["QX%dc" % r][:, a:a + n], T["QX%ds" % r][:, a:a + n], QK[r][i], T[XB[r]][:, 4 * a:4 * (a + n)],
-                  ["X1%d" % i] if r == 1 else [XB[r] + "t%d" % t for t in range(5)])
-
-    def score_products(r):
-        for i, (a, n) in enumerate(CH[r]):
-            mm(4 + i, n, T.URc[:], T.URs[:], T["QX%dc" % r][:, a:a + n], T["QX%ds" % r][:, a:a + n], ["URc", "URs", QK[r][i]])
-
-    def unpack_products(qc, qs, banks, rds):
-        for b in range(4):
-            mm(banks[b], P, T.ECc[:, 128 * b:128 * b + 128], T.ECs[:, 128 * b:128 * b + 128], qc, qs, ["EC%d" % b] + rds)
-
-    def plane(r, t):
-        return T["V%d" % r][:, VW[r] * t:VW[r] * t + P]
-
-    def own_plane(r, t):
-        act(plane(r, t), "F%d%d" % (r, t), T["p%d" % t][:, 0:P], ["p%d" % t])
-
-    def second_planes():
-        for t, e in ((0, P), (1, P), (2, 192)):
-            act(T.FQ[:, P * t:P * t + e], "FQ%d" % t, T["p%d" % t][:, 0:e], ["p%d" % t])
-
-    def sort_keys(r, tbls, meanwhile):
-        W = LANES[r]
-        n16, n = 16 * W, NR[r]
-        tt(T.GM[:, 0:n16], "GM", T.SS[:].indirect(T.BL[:, 0:W]), T.m16[:, 0:n16], SK[r] + ["BL", "m16"], A.mult)
-        scan(T.SC[:, 0:n16], "SC", T.seg16[:, 0:n16], T.GM[:, 0:n16], ["seg16", "GM"], A.mult, A.add)
-        mn, mx, mnk, mxk = T["MN%d" % r], T["MX%d" % r], "MN%d" % r, "MX%d" % r
-        cuts = [(0, n)] if r > 1 else [(0, 192), (192, 384), (384, 576)]
-        for a, b in cuts:
-            lst = mx[:, a // 16:b // 16]
-            if r == 1:
-                act(T.BX[:, a:b], "BX%d" % a, T.SC[:].indirect(lst), ["SC", mxk])
-            else:
-                vcopy(T.BX[:, a:b], "BX%d" % a, T.SC[:].indirect(lst), ["SC", mxk])
-        meanwhile()
-        for a, b in cuts:
-            tt(T.C[:, a:b], "C%d" % a, T.SC[:].indirect(mn[:, a // 16:b // 16]), T.BX[:, a:b], ["SC", mnk, "BX%d" % a], A.is_ge)
-        scan(T.CS[:, 0:n], "CS", T["D0%d" % r][:], T.C[:, 0:n], ["D0%d" % r] + ["C%d" % a for a, b in cuts], A.mult, A.add)
-        add_keys(r, 0, "KA", tbls)
-
-    def add_keys(r, a, nm, tbls):
-        W = LANES[r]
-        for i, (tb, key) in enumerate(tbls):
-            c = a + i * (W + 1)
-            tt(T["KA%d" % r][:, c:c + W], "%s%d%d" % (nm, r, i), tb, T.CS[:, W - 1:W * W:W], [key, "CS"], A.subtract)
-
-    def extract(r, a, nm, d, dk):
-        W = LANES[r]
-        L, n = W + 1, NE[r]
         ns = B0[r] + W // 2 + 1
-        width = 25 if r == 1 else 2 * L
-        rds = ["%s%d%d" % (nm, r, i) for i in range(1 if r == 1 else 2)] + ["%s%dz" % (nm, r)]
-        tt(T.M[:, 0:n], "M", T["KA%d" % r][:, a:a + width].indirect(T["KL%d" % r][:]), T["T%d" % r][:],
-           rds + ["KL%d" % r, "T%d" % r], A.min)
-        scan(T.HS[:, 0:n], "HS", T["DS%d" % r][:], T.M[:, 0:n], ["DS%d" % r, "M"], A.mult, A.add)
-        tt(d[:, 0:ns - 1], dk, T.HS[:, 2 * L - 1:ns * L:L], T.HS[:, L - 1:(ns - 1) * L:L], ["HS"], A.subtract)
-
-    def first_lists(r):
-        d, dk = T["D%d" % r], "D%d" % r
-        extract(r, 0, "KA", d, dk)
-        ts(T["CL%d" % r][:], "CL%d" % r, d[:, 0:B0[r] + LANES[r] // 2], [dk], 1024.0, A.mult, 383.0, A.min)
-
-    def select(out, w, a0, a1, m, n, rds, t1, t2):
-        ts(t1, "sel1" + w, a0, rds + [n], col[n], A.mult)
-        ts(t2, "sel2" + w, a1, rds + [m], col[m], A.mult)
-        tt(out, w, t1, t2, ["sel1" + w, "sel2" + w], A.add)
-
-    def lower(r, d, dk, out, w):
-        h = LANES[r] // 2
-        select(out, w, d[:, 0:h], d[:, 1:h + 1], "m0", "n0", [dk], T.tf[:, 352:352 + h], T.tf[:, 366:366 + h])
-
-    def upper_bases(r, d, dk, dz):
-        h, a = LANES[r] // 2, B0[r]
-        select(T.sl[:, 0:h + 1], "us", d[:, a - 1:a + h], d[:, a:a + h + 1], "m15", "n15", [dk, dz],
-               T.tf[:, 380:380 + h + 1], T.tf[:, 394:394 + h + 1])
-        ts(T.US[:, 0:h + 1], "US", T.sl[:, 0:h + 1], ["us"], 1024.0, A.mult, 383.0, A.min)
-
-    def rows_of_bases(r):
-        h = LANES[r] // 2
-        act(T.VB[:, 0:16 * (h + 1)], "VB", T.iotaR[:, 0:P].indirect(T.US[:, 0:h + 1]), ["iotaR", "US"])
-
-    def scatter_tops(r):
-        h, b0 = LANES[r] // 2, B0[r]
-        op("v", ["CL%d" % r, "iotaR"], ["UP"],
-           lambda: g.vector.tensor_copy(T.UP[:].indirect(T["CL%d" % r][:, b0:b0 + h]), T.iotaR[:, P:P + 16 * h]))
-
-    def scatter_links(r, low, lowk):
-        op("v", [lowk, "VB"], ["UP"], lambda: g.vector.tensor_copy(T.UP[:].indirect(low), T.VB[:, 15:15 + 8 * LANES[r]]))
-
-    def mask_up():
-        scan(T.ms[:], "ms", T.UP[:], T.m16[:], ["UP", "m16"], A.add, A.mult)
-
-    def blend_list():
-        scan(T.ht[:], "ht", T.seg16[:], T.ms[:], ["seg16", "ms"], A.mult, A.add)
-        vcopy(T.UL[:], "UL", T.ht[:, 15:P:16], ["ht"])
-
-    def shift_tops(r):
-        h, b0 = LANES[r] // 2, B0[r]
-        d, dk = T["D%d" % r], "D%d" % r
-        dma("y", T.tbT[1:128, 0:h], d[0:127, b0:b0 + h], [dk], ["tbT"])
-        dma("y", T.tbT[0:128:16, 0:h], d[15:128:16, b0:b0 + h], [dk], ["tbT"])
-
-    def make_e(r, win, wkeys, lst, lkey, meanwhile):
-        h, b0 = LANES[r] // 2, B0[r]
-        n = 16 * (h + 1)
-        for t in range(4):
-            act(T.tmp[:, n * t:n * t + n], "tmp%d" % t, win(t).indirect(lst[:, 0:h + 1]), [wkeys[t], lkey])
-        second_planes()
-        meanwhile()
-        for t in range(4):
-            tt(T["E%d" % r][:, t:64 * h:4], "E%d%d" % (r, t), win(t).indirect(lst[:, b0:b0 + h]),
-               T.tmp[:, n * t + 1:n * t + 1 + 16 * h], [wkeys[t], lkey, "tmp%d" % t], A.add)
-
-    def layer(r, ec, es, ekeys, n):
-        h, w, v = LANES[r] // 2, VW[r], T["V%d" % r]
-        for b in range(4):
-            mm(4 + b, n, T.WWc[:, 128 * b:128 * b + 128], T.WWs[:, 128 * b:128 * b + 128], ec, es, ["WWc", "WWs"] + ekeys)
-        for b in range(4):
-            act(v[:, w * b + P:w * b + P + 16 * h], "H%d%d" % (r, b), T["p%d" % (4 + b)][:, 0:16 * h], ["p%d" % (4 + b)], scale=0.015625)
-
-    def blend(r):
-        h, w = LANES[r] // 2, VW[r]
-        v, xn, xk = T["V%d" % r], T[XB[r + 1]], XB[r + 1]
-
-        def near(t, a, b):
-            return v[:, w * t:w * t + P + 16 * h].indirect(T.UL[:, a // 16:b // 16])
-
-        def keys(t):
-            return ["F%d%d" % (r, t), "H%d%d" % (r, t), "UL"]
-        act(T.tb[:, 0:P], "tb0", near(3, 0, P), keys(3))
-        act(T.tb[:, P:576], "tb1", near(2, 192, P), keys(2))
-        for t, e in ((0, P), (1, P), (2, 192)):
-            tt(xn[:, t:4 * e:4], xk + "t%d" % t, near(t, 0, e), T.FQ[:, P * t:P * t + e], keys(t) + ["FQ%d" % t], A.add)
-        tt(xn[:, 3:4 * P:4], xk + "t3", T.tb[:, 0:P], T.p3[:, 0:P], ["tb0", "p3"], A.add)
-        tt(xn[:, 770:4 * P:4], xk + "t4", T.tb[:, P:576], T.p2[:, 192:P], ["tb1", "p2"], A.add)
-
-    def later_pads():
-        memset(T.E2[:, 384:512], "E2z", 0.0)
-        memset(T.E3[:, 192:704], "E3z", 0.0)
-        quant(T.LE2c[:, 96:224], T.LE2s[:, 96:224], "LE2z", T.E3[:, 192:704], ["E3z"])
-        quant(T.LE3c[:, 48:176], T.LE3s[:, 48:176], "LE3z", T.E3[:, 192:704], ["E3z"])
-
-    f1, f2, f2t = thresholds(1), together(pair_lists(2), key_lists(2)), thresholds(2)
-    f3 = together(pair_lists(3), key_lists(3), thresholds(3))
+        fill(v("DS%d" % r), NE[r], 1.0)
+        fill(v("DS%d" % r, 0, ns * (W + 1), W + 1), ns, 0.0)
 
     def pump(f, n=99):
         for _ in range(n):
             if next(f, 1) is not None:
                 break
 
-    quant_x(1)
-    quant(T.QUc[:], T.QUs[:], "QU", T.ub[:], ["ub"])
-    vcopy(T.URc[:].bitcast(dt.uint32), "URc", T.QUc[:].bitcast(dt.uint32).indirect(T.ul[:, 0:8]), ["QU", "ul"])
-    act(T.URs[:], "URs", T.QUs[:].indirect(T.ul[:, 0:8]), ["QU", "ul"])
-    send(T.LXc[:].bitcast(dt.uint8), T.QX1c[:].bitcast(dt.uint8), "axc", QK[1], "LX")
-    send(T.LXs[:], T.QX1s[:], "axs", QK[1], "LX")
-    score_products(1)
-    for i, (a, n) in enumerate(CH[1]):
-        act(T.SS[:, a:a + n], "SS%d" % i, T["p%d" % (4 + i)][:, 0:n], ["p%d" % (4 + i)])
+    def plane(t, a=0, b=P):
+        return v("V", VW * t + a, VW * t + b)
+
+    def unpack(q, a, bank):
+        for b in range(4):
+            mm(bank + b, "EC", 128 * b, q, a, P)
+
+    def own_planes():
+        for t in range(4):
+            act(plane(t), v("p%d" % t, 0, P))
+            if t < 2:
+                dma("y", v("FQ", P * t, P * t + OWN[t]), plane(t, 0, OWN[t]))
+
+    def gather_scores(r):
+        n = 16 * LANES[r]
+        tt(v("GM", 0, n), by(v("SS"), v("BL", 0, LANES[r])), v("m16", 0, n), A.mult)
+        scan(v("SC", 0, n), v("hold", 0, n), v("GM", 0, n), A.mult, A.add)
+
+    def pairs(r, q, a, b):
+        src = by(v("SC"), v("MX%d" % r, a // 16, b // 16))
+        (act if q == "s" else vcopy)(v("BX", a, b), src)
+
+    def compare(r, a, b):
+        tt(v("C", a, b), by(v("SC"), v("MN%d" % r, a // 16, b // 16)), v("BX", a, b), A.is_ge)
+
+    def keys(r, tables):
+        W, n = LANES[r], NR[r]
+        scan(v("CS", 0, n), v("D0%d" % r), v("C", 0, n), A.mult, A.add)
+        for i, tb in enumerate(tables):
+            c = K0[r] + i * (W + 1)
+            tt(v("KA", c, c + W), v(tb, 0, W), v("CS", W - 1, W * W, W), A.subtract)
+
+    def extract(r, lst, d):
+        W = LANES[r]
+        L, n = W + 1, NE[r]
+        ns = B0[r] + W // 2 + 1
+        tt(v("M", 0, n), by(v("KA", K0[r], K0[r] + (L if r == 1 else 2 * L)), v(lst)), v("T%d" % r, 0, n), A.min)
+        scan(v("HS", 0, n), v("DS%d" % r), v("M", 0, n), A.mult, A.add)
+        tt(v(d, 0, ns - 1), v("HS", 2 * L - 1, ns * L, L), v("HS", L - 1, (ns - 1) * L, L), A.subtract)
+
+    def first_lists(r):
+        extract(r, "KL%d" % r, "D%d" % r)
+        ts(v("CL%d" % r), v("D%d" % r, 0, B0[r] + LANES[r] // 2), 1024.0, A.mult, P - 1.0, A.min)
+
+    def next_tables(r):
+        h, b0, d = LANES[r] // 2, B0[r], "D%d" % r
+        dma("y", v("nB", 0, h), v(d, 0, h))
+        dma("y", v("nT", 0, h, rows=slice(1, 128)), v(d, b0, b0 + h, rows=slice(0, 127)))
+        dma("y", v("nB", 0, h, rows=slice(0, 128, 16)), v(d, 1, h + 1, rows=slice(0, 128, 16)))
+        dma("y", v("nT", 0, h, rows=slice(0, 128, 16)), v(d, b0, b0 + h, rows=slice(15, 128, 16)))
+
+    def rows_of_bases(r, lst):
+        h = LANES[r] // 2
+        act(v("VB", 1, 1 + 16 * h), by(v("iotaR", 0, P), v(lst, B0[r], B0[r] + h)))
+
+    def scatter_links(r):
+        h = LANES[r] // 2
+        vcopy(by(v("UP"), v("CB", 0, h + 1)), v("VB", 0, 16 * h + 16))
+
+    def scatter_tops(r, values):
+        h, b0 = LANES[r] // 2, B0[r]
+        vcopy(by(v("UP"), v("CL%d" % r, b0, b0 + h)), values)
+
+    def blend_list():
+        scan(v("ht"), v("climb"), v("UP", 0, P), A.add, A.max)
+        ts(v("UL"), v("ht", 15, P, 16), col["rise"], A.subtract)
+
+    def make_e(r, win, lst):
+        h, b0 = LANES[r] // 2, B0[r]
+        n = 16 * (h + 1)
+        for t in range(4):
+            act(v("tmp", n * t, n * t + n), by(win(t), v(lst, 0, h + 1)))
+        for t in range(4):
+            tt(v("E", t, 64 * h, 4), by(win(t), v(lst, b0, b0 + h)), v("tmp", n * t + 1, n * t + 1 + 16 * h), A.add)
+
+    def layer(q, a, n):
+        for b in (3, 0, 2, 1):
+            mm(4 + b, "WW", 128 * b, q, a, n)
+
+    def take_h(r, q, b, off):
+        n = 8 * LANES[r]
+        evac(q, plane(b, P, P + n), v("p%d" % (4 + b), off, off + n), 0.015625)
+
+    def near(r, t, a, b):
+        return by(plane(t, 0, P + 8 * LANES[r]), v("UL", a // 16, b // 16))
+
+    def fetch(r, t, a, b):
+        act(v("tb", P * t + a, P * t + b), near(r, t, a, b))
+
+    def add_fetched(r, t, a, b):
+        tt(v(XB[r + 1], 4 * a + t, 4 * b, 4), v("tb", P * t + a, P * t + b), v("p%d" % t, a, b), A.add)
+
+    def add_near(r, t, a, b):
+        tt(v(XB[r + 1], 4 * a + t, 4 * b, 4), near(r, t, a, b), v("FQ", P * t + a, P * t + b), A.add)
+
+    def blend(r, off):
+        take_h(r, "s", 3, off)
+        for b in (0, 2, 1):
+            take_h(r, "v", b, off)
+        for t, a, b in ((3, 0, P), (2, 0, P), (1, 96, 256), (1, 256, P)):
+            fetch(r, t, a, b)
+        add_near(r, 0, 0, P)
+        add_fetched(r, 3, 0, P)
+        add_near(r, 1, 0, 96)
+        for t, a, b in ((2, 0, P), (1, 96, 256), (1, 256, P)):
+            add_fetched(r, t, a, b)
+
+    dma("y", v("tw32"), T.tw[:, :])
+    dma("s", v("ub"), T.u[:, :])
+    for c in range(3):
+        dma("y", v("X1", 512 * c, 512 * c + 512), T.x[:, 512 * c:512 * c + 512])
+
+    iota(v("ic"), [[0, 24]], 0, 1)
+    iota(v("mi"), [[1, 16]], 128, -1)
+    iota(v("J"), [[16, 44]], 0)
+    iota(v("iotaR", 0, P), [[1, P]], 0)
+    iota(v("ui"), [[16, 8]], 0)
+    iota(v("KK"), [[-1, 24]], 22)
+    memset(v("half"), 0.5)
+    ts(v("ic"), v("ic"), 15, A.bitwise_and)
+    ts(v("mi"), v("mi"), 15, A.bitwise_and)
+    vcopy(v("il"), v("ic"))
+    ts(v("m16s"), v("mi"), 0.0, A.is_equal)
+    ts(col["i"], v("ic", 0, 1), 1.0, A.mult)
+    act(v("m16"), by(v("m16s"), v("il")))
+    ts(col["m0"], v("ic", 0, 1), 0.0, A.is_equal)
+    ts(v("J"), v("J"), col["i"], A.add)
+    ts(col["minus0"], v("ic", 0, 1), 0.0, A.is_equal, -1.0, A.mult)
+    f1 = together(pair_lists(1), key_lists(1))
     pump(f1, 3)
+    vcopy(v("tw16"), v("tw32"))
+    act(v("ms"), by(v("iotaR", 0, P), v("tw16")))
+    dma("y", v("fe"), v("ms", rows=slice(0, 128, 16)))
+    vcopy(v("ul"), v("ui"))
+    quant("QU", 0, 128, v("ub"))
+    pump(f1, 1)
+    vcopy(words(v("URc")), by(words(v("QUc")), v("ul")))
+    act(v("URs"), by(v("QUs"), v("ul")))
+    act(v("hold"), v("m16"), AF.Identity, scale=-1.0, bias=1.0)
+    for c in range(3):
+        quant("QX1", 128 * c, 128 * c + 128, v("X1", 512 * c, 512 * c + 512))
+        if c == 0:
+            pump(f1)
+    dma("y", raw(v("WWc")), T.wc[:, :])
+    dma("y", v("WWs"), T.ws[:, :])
+
+    send(raw(v("LBc", LAND[1], LAND[1] + P)), raw(v("QX1c")), "axc")
+    send(v("LBs", LAND[1], LAND[1] + P), v("QX1s"), "axs")
+    op("g", [v("half", 0, 516)], [v("zi")], lambda: g.affine_select(T.zi[:], T.half[:, 0:516], [[1, 516]], A.is_equal, 0.0, -3, -4))
+    threshold_rows(1)
+    iota(v("iotaR", P), [[1, 576 - P]], P)
+    threshold_rows(2)
+    threshold_rows(3)
+    iota(v("opc", 0, 48), [[1, 3], [3, 16]], P + 3)
+    iota(v("opc", 48, 51), [[1, 3]], P)
+    for c in range(3):
+        mm(4 + c, "UR", 0, "QX1", 128 * c, 128)
+    for c in range(3):
+        evac("sv"[c // 2], v("SS", 128 * c, 128 * c + 128), v("p%d" % (4 + c), 0, 128))
+    memset(v("KK", 23, 24), 1.0)
+    memset(v("KA"), 1e6)
+    vcopy(v("BL"), v("fe"))
+    ts(v("sl"), v("fe"), 1.0 / 1024, A.mult)
     signs(1)
-    for b in range(4):
-        quant(T.ECc[:, 128 * b:128 * b + 128], T.ECs[:, 128 * b:128 * b + 128], "EC%d" % b, T.zi[:, 3 - b:515 - b], ["zi"])
-    unpack_products(T.QX1c[:], T.QX1s[:], (0, 1, 2, 3), QK[1])
-    later_pads()
-    ts(T.sl[:, 0:24], "us", T.fe[:], ["fe"], 1.0 / 1024, A.mult)
-    vcopy(T.BL[:], "BL", T.fe[:], ["fe"])
-    tt(T.tbB[:], "tbB", T.sl[:, 0:24], T.KK[:], ["us", "KK"], A.add)
-
-    def r1_gap():
-        pump(f1)
-        pump(f2, 2)
-        resets(1)
-        pump(f2t, 3)
-    sort_keys(1, [(T.tbB[:], "tbB")], r1_gap)
-    for t in range(4):
-        own_plane(1, t)
+    gather_scores(1)
+    thirds = ((0, 192), (192, 384), (384, 576))
+    for a, b in thirds:
+        pairs(1, "s", a, b)
+    tt(v("tbB"), v("sl"), v("KK"), A.add)
+    for b in range(2):
+        quant("EC", 128 * b, 128 * b + 128, v("zi", 3 - b, 515 - b))
+    tower0(1)
+    resets(1)
+    f1 = cancels(1)
+    for a, b in thirds:
+        compare(1, a, b)
+        if a == 0:
+            for b in range(2, 4):
+                quant("EC", 128 * b, 128 * b + 128, v("zi", 3 - b, 515 - b))
+    unpack("QX1", 0, 0)
+    pump(f1, 2)
+    keys(1, ["tbB"])
+    pump(f1)
+    own_planes()
     first_lists(1)
-    send(T.LL[:], T.CL1[:], "all1", ["CL1"], "LL")
+    send(v("LL"), v("CL1"), "all1")
 
-    fill(T.D1[:, 26:27], "Dz1", 1, 0.0)
-    fill(T.DB[:, 14:15], "DBz2", 1, 0.0)
-    iota(T.opc[:, 0:48], "opc", [[1, 3], [3, 16]], P + 3, 0)
-    iota(T.opc[:, 48:51], "opf", [[1, 3]], P, 0)
-    unpack_products(T.LXc[:], T.LXs[:], (4, 5, 6, 7), ["LX"])
-    upper_bases(1, T.D1, "D1", "Dz1")
-    scatter_tops(1)
+    rows_of_bases(1, "CL1")
+    unpack("LB", LAND[1], 4)
     for t in range(4):
-        act(T.FP[:, P * t:P * t + P], "FP%d" % t, T["p%d" % (4 + t)][:, 0:P], ["p%d" % (4 + t)])
-        if t == 1:
-            rows_of_bases(1)
-    lower(1, T.D1, "D1", T.tbB[:, 0:12], "tbB")
-    ts(T.BL[:, 0:12], "BL", T.tbB[:, 0:12], ["tbB"], 1024.0, A.mult)
-    tt(T.tbB[:, 0:12], "tbB", T.tbB[:, 0:12], T.KK[:, 12:24], ["tbB", "KK"], A.add)
-    pump(f2)
-    pump(f2t)
-    scatter_links(1, T.BL[:, 0:12], "BL")
-    shift_tops(1)
-    make_e(1, lambda t: T.FP[:, P * t:P * t + P], ["FP%d" % t for t in range(4)], T.LL, "LL", mask_up)
-    quant(T.QE1c[:], T.QE1s[:], "QE1", T.E1[:], ["E1%d" % t for t in range(4)])
-    layer(1, T.QE1c[:], T.QE1s[:], ["QE1"], 192)
+        act(v("FP", P * t, P * t + P), v("p%d" % (4 + t), 0, P))
+    next_tables(1)
+    ts(v("CB", 0, 14), v("D1", 0, 14), 1024.0, A.mult)
+    memset(v("VB", 0, 1), 0.0)
+    memset(v("VB", 193), 0.0)
+    ts(col["rise"], v("ic", 0, 1), -1024.0, A.mult, 15360.0, A.add)
+    ts(v("climb"), v("m16"), -33792.0, A.mult, 1024.0, A.add)
+    scatter_links(1)
+    scatter_tops(1, v("iotaR", P, P + 192))
+    f2 = together(pair_lists(2), key_lists(2))
+    pump(f2, 2)
+    make_e(1, lambda t: v("FP", P * t, P * t + P), "LL")
+    quant("QE1", 0, 192, v("E"))
+    layer("QE1", 0, 192)
+    tower0(2)
     blend_list()
-    blend(1)
+    blend(1, 0)
+    signs(2)
+    resets(2)
+    dma("y", v("vb"), T.v[:, :])
 
+    f2c, f3, f3c = cancels(2), together(pair_lists(3), key_lists(3)), cancels(3)
     for r in (2, 3):
         W = LANES[r]
         h, b0 = W // 2, B0[r]
-        n = 16 * h
-        tbB, tbT = T.tbB[:, 0:W], T.tbT[:, 0:W]
-        quant_x(r)
-        score_products(r)
-        unpack_products(T["QX%dc" % r][:], T["QX%ds" % r][:], (0, 1, 2, 3), QK[r])
+        n, q = 16 * h, "QX%d" % r
+        quant(q, 0, 256, v(XB[r], 0, 1024))
+        quant(q, 256, P, v(XB[r], 1024))
+        mm(4, "UR", 0, q, 0, 256)
+        mm(5, "UR", 0, q, 256, 128)
+        unpack(q, 0, 0)
+        ts(v("BL", 0, W), v("nB", 0, W), 1024.0, A.mult)
         if r == 2:
-            signs(2)
-            resets(2)
-        tt(tbT, "tbT", tbT, T.KK[:, 24 - W:24], ["tbT", "KK"], A.add)
-        vcopy(T.SS[:, 0:256], "SS0", T.p4[:, 0:256], ["p4"])
-        act(T.SS[:, 256:P], "SS1", T.p5[:, 0:128], ["p5"])
-        for t in range(4):
-            own_plane(r, t)
+            pump(f2)
+        evac("s", v("SS", 0, 256), v("p4", 0, 256))
+        evac("v", v("SS", 256, P), v("p5", 0, 128))
+        own_planes()
+        tt(v("tbB", 0, W), v("nB", 0, W), v("KK", 24 - W), A.add)
+        gather_scores(r)
+        tt(v("tbT", 0, W), v("nT", 0, W), v("KK", 24 - W), A.add)
+        pairs(r, "v", 0, NR[r])
         if r == 2:
+            pump(f2c, 1)
+        compare(r, 0, NR[r])
+        if r == 2:
+            pump(f2c, 1)
+        keys(r, ["tbB", "tbT"])
+        if r == 2:
+            pump(f2c)
+        first_lists(r)
+        make_e(r, plane, "CL%d" % r)
+        quant("QE%d" % r, 0, 128, v("E", 0, 512))
+        send(raw(v("LBc", LAND[r], LAND[r] + n)), raw(v("QE%dc" % r, 0, n)), "a%dc" % r)
+        send(v("LBs", LAND[r], LAND[r] + n), v("QE%ds" % r, 0, n), "a%ds" % r)
+        if r == 2:
+            next_tables(2)
+        extract(r, "KB%d" % r, "DB")
+        ts(v("CB", 0, b0 + h), v("DB", 0, b0 + h), 1024.0, A.mult)
+        rows_of_bases(r, "CB")
+        if r == 2:
+            tower0(3)
             signs(3)
             resets(3)
-        sort_keys(r, [(tbB, "tbB"), (tbT, "tbT")], lambda: None)
-        first_lists(r)
-
-        def e_gap():
-            add_keys(r, 32, "KB", [(tbT, "tbT"), (tbB, "tbB")])
-        make_e(r, lambda t: plane(r, t), ["F%d%d" % (r, t) for t in range(4)], T["CL%d" % r], "CL%d" % r, e_gap)
-        quant(T["QE%dc" % r][:], T["QE%ds" % r][:], "QE%d" % r, T["E%d" % r][:, 0:512], ["E%d%d" % (r, t) for t in range(4)] + ["E%dz" % r])
-        send(T["LE%dc" % r][:, 0:n].bitcast(dt.uint8), T["QE%dc" % r][:, 0:n].bitcast(dt.uint8), "a%dc" % r, ["QE%d" % r], "LE%d" % r)
-        send(T["LE%ds" % r][:, 0:n], T["QE%ds" % r][:, 0:n], "a%ds" % r, ["QE%d" % r], "LE%d" % r)
-        if r == 2:
-            shift_tops(2)
+            pump(f3, 3)
         else:
-            fill(T.DB[:, 9:10], "DBz3", 1, 0.0)
-        extract(r, 32, "KB", T.DB, "DB")
-        upper_bases(r, T.DB, "DB", "DBz%d" % r)
-        rows_of_bases(r)
-        scatter_tops(r)
-        lower(r, T.DB, "DB", T.sl[:, 16:16 + h], "tl")
-        ts(T.SL[:, 0:h], "SL", T.sl[:, 16:16 + h], ["tl"], 1024.0, A.mult)
-        scatter_links(r, T.SL[:, 0:h], "SL")
-        mask_up()
+            vcopy(v("opc", 15, 48, 16), v("opc", 48, 51))
+            quant("QV", 0, 128, v("vb"))
+        scatter_links(r)
+        scatter_tops(r, v("iotaR", P, P + n))
         blend_list()
         if r == 2:
-            lower(2, T.D2, "D2", T.tbB[:, 0:6], "tbB")
-            ts(T.BL[:, 0:6], "BL", T.tbB[:, 0:6], ["tbB"], 1024.0, A.mult)
-            tt(T.tbB[:, 0:6], "tbB", T.tbB[:, 0:6], T.KK[:, 18:24], ["tbB", "KK"], A.add)
             pump(f3)
+            pump(f3c)
         else:
-            op("v", ["opc", "opf"], ["opc"], lambda: g.vector.tensor_copy(T.opc[:, 15:48:16], T.opc[:, 48:51]))
-            op("v", ["opc", "CL3"], ["UP"], lambda: g.vector.tensor_copy(T.UP[:].indirect(T.CL3[:, b0:b0 + h]), T.opc[:, 0:48]))
-            dma("y", T.op[:, :], T.UP[0:128:16, :], ["UP"], ["op"])
-            quant(T.QVc[:], T.QVs[:], "QV", T.vb[:], ["vb"])
-        layer(r, T["LE%dc" % r][:, 0:128], T["LE%ds" % r][:, 0:128], ["LE%d" % r, "LE%dz" % r], 128)
-        blend(r)
+            scatter_tops(3, v("opc", 0, 48))
+            dma("y", T.op[:, :], v("UP", 0, P, rows=slice(0, 128, 16)))
+        first = min(LAND[r], 528 - 128)
+        layer("LB", first, 128)
+        if r == 2:
+            blend(2, 0)
 
-    quant_x(4)
-    for i, (a, n) in enumerate(CH[4]):
-        mm(4 + i, n, T.QVc[:], T.QVs[:], T.QX4c[:, a:a + n], T.QX4s[:, a:a + n], ["QV", QK[4][i]])
-    dma("s", T.oc[:, :], T.QX4c[:].bitcast(dt.uint8), QK[4], ["oc"])
+    off = LAND[3] - first
+    take_h(3, "s", 3, off)
+    for b in (0, 2, 1):
+        take_h(3, "v", b, off)
+    runs = ((0, 256), (256, P))
+    for a, b in runs:
+        for t in (3, 2, 1):
+            fetch(3, t, a, b)
+    for i, (a, b) in enumerate(runs):
+        add_near(3, 0, a, b)
+        for t in (3, 2, 1):
+            add_fetched(3, t, a, b)
+        quant("QX4", a, b, v("X2", 4 * a, 4 * b))
+        mm(4 + i, "QV", 0, "QX4", a, b - a)
+        dma("y", T.oc[:, 4 * a:4 * b], raw(v("QX4c", a, b)))
+    evac("s", v("ysb", 0, 256), v("p4", 0, 256))
+    dma("s", T.y[:, 0:256], v("ysb", 0, 256))
     for k2 in range(4):
-        dma("s" if k2 < 2 else "y", T.osc[4 * k2:4 * k2 + 4, :], T.QX4s[32 * k2:32 * k2 + 4, :], QK[4], ["osc%d" % k2])
-    for i, (a, n) in enumerate(CH[4]):
-        vcopy(T.ysb[:, a:a + n], "ysb%d" % i, T["p%d" % (4 + i)][:, 0:n], ["p%d" % (4 + i)])
-        dma("y", T.y[:, a:a + n], T.ysb[:, a:a + n], ["ysb%d" % i], ["y%d" % i])
+        dma("sy"[k2 % 2], T.osc[4 * k2:4 * k2 + 4, :], v("QX4s", rows=slice(32 * k2, 32 * k2 + 4)))
+    evac("v", v("ysb", 256, P), v("p5", 0, 128))
+    dma("y", T.y[:, 256:P], v("ysb", 256, P))
 
     for sem, val in cnt.items():
         if known["g"].get(sem, 0) < val:

@@ -4,13 +4,14 @@ A = AluOpType
 AF = ActivationFunctionType
 P = 384
 LANES = {1: 24, 2: 12, 3: 6}
-B0 = {1: 14, 2: 8, 3: 6}
+B0 = {1: 14, 2: 14, 3: 8}
 NR = {1: 576, 2: 144, 3: 48}
-NE = {1: 688, 2: 208, 3: 80}
+SPLIT = 15
+SEGS = {1: 14 + SPLIT - 11, 2: 21, 3: 12}
+NE = {r: -(-SEGS[r] * (LANES[r] + 1) // 16) * 16 for r in SEGS}
 K0 = {1: 0, 2: 32, 3: 64}
 VW = 576
 LAND = {1: 96, 2: 0, 3: 480}
-OWN = (P, 96)
 XB = {1: "X1", 2: "X2", 3: "X3", 4: "X2"}
 BF, F32, U16, I32, U8, FP8 = "bfloat16", "float32", "uint16", "int32", "uint8", "float8_e4m3fn_x4"
 SIZE = {BF: 2, F32: 4, U16: 2, I32: 4, U8: 1, FP8: 4}
@@ -27,28 +28,31 @@ for _n, _c in (("QX1", P), ("QX2", P), ("QX3", P), ("QX4", P), ("QU", 128), ("UR
     _buf(_n + "c", _c, FP8)
     _buf(_n + "s", _c, U8)
 for _n, _c, _t in (
-        ("X1", 4 * P, BF), ("X2", 4 * P, BF), ("X3", 4 * P, BF), ("ub", 512, BF), ("vb", 512, BF), ("half", 688, BF),
-        ("zi", 516, BF), ("FP", 4 * P, BF), ("V", 4 * VW, BF), ("FQ", 2 * P, BF), ("E", 768, BF), ("tmp", 832, BF), ("tb", 4 * P, BF),
+        ("X1", 4 * P, BF), ("X2", 4 * P, BF), ("X3", 4 * P, BF), ("ub", 512, BF), ("vb", 512, BF), ("half", 576, BF),
+        ("zi", 516, BF), ("FP", 4 * P, BF), ("V", 4 * VW, BF), ("FQ", P, BF), ("E", 768, BF), ("tmp", 832, BF), ("tb", 4 * P, BF),
         ("m16s", 16, BF), ("m16", P, BF), ("hold", P, BF), ("climb", P, BF), ("C", 576, BF), ("CS", 576, BF),
-        ("tw32", 24, I32), ("ic", 24, I32), ("mi", 16, I32), ("ui", 8, I32), ("ti", 96, I32),
+        ("tw32", 24, I32), ("ic", 26, I32), ("ti", 96, I32),
         ("tw16", 24, U16), ("il", 24, U16), ("ul", 8, U16), ("LL", 26, U16), ("CB", 16, U16), ("BL", 24, U16), ("UL", 24, U16),
+        ("TL", 12, U16), ("RL", 12, U16), ("Z", 208, F32), ("NU", 192, F32),
         ("cols", 8, F32), ("iotaR", 576, F32), ("J", 44, F32), ("KK", 24, F32), ("fe", 24, F32), ("opc", 52, F32),
         ("UP", P + 16, F32), ("ms", P, F32), ("ht", P, F32), ("ysb", P, F32), ("SS", P, F32), ("GM", P, F32), ("SC", P, F32),
-        ("BX", 576, F32), ("M", 688, F32), ("HS", 688, F32), ("tf", 448, F32), ("sl", 24, F32), ("DB", 16, F32),
-        ("VB", 208, F32), ("tbB", 24, F32), ("tbT", 12, F32), ("nB", 12, F32), ("nT", 12, F32), ("KA", 80, F32)):
+        ("BX", 576, F32), ("M", 688, F32), ("HS", 688, F32), ("tf", 448, F32), ("sl", 24, F32),
+        ("VB", 208, F32), ("tbB", 24, F32), ("tbT", 12, F32), ("nB", 12, F32), ("nT", 12, F32), ("KA", 80, F32),
+        ("over", 25 - SPLIT, F32), ("rest", 24 - SPLIT, F32), ("beyond", 24 * (24 - SPLIT), F32)):
     _buf(_n, _c, _t)
 for _r in (1, 2, 3):
     _h = LANES[_r] // 2
     _L = LANES[_r] + 1
-    for _n, _c, _t in (("D0", NR[_r], BF), ("DS", NE[_r], BF), ("T", (B0[_r] + _h + 3) * _L, F32), ("D", 28, F32),
+    for _n, _c, _t in (("D0", NR[_r], BF), ("DS", NE[_r], BF), ("T", (SEGS[_r] + 2) * _L, F32), ("D", 28, F32),
                        ("CL", B0[_r] + _h, U16), ("MN", NR[_r] // 16, U16), ("MX", NR[_r] // 16, U16),
-                       ("KL", NE[_r] // 16, U16), ("KB", NE[_r] // 16, U16)):
+                       ("KL", NE[_r] // 16, U16)):
         _buf(_n + str(_r), _c, _t)
 for _i in range(8):
     _buf("p%d" % _i, 512, F32, "psum")
 
 NDMA = 40
-SEMAPHORES = ["vs", "ss", "ts", "gs", "loc", "axc", "axs", "all1", "a2c", "a2s", "a3c", "a3s"] + ["d%d" % i for i in range(NDMA)]
+SEMAPHORES = (["vs", "ss", "ts", "gs", "loc", "ax0", "ax1", "ax2", "axs", "all1", "a2c", "a2s", "a3c", "a3s"]
+              + ["d%d" % i for i in range(NDMA)])
 
 
 def v(name, a=0, b=None, step=1, rows=None):
@@ -173,14 +177,12 @@ def rank_program(g, core, T, topo):
     def memset(out, k):
         op("v", [], [out], lambda: g.vector.memset(ap(out), k))
 
-    def scan(out, d0, d1, o0, o1):
-        op("v", [d0, d1], [out], lambda: g.vector.tensor_tensor_scan(ap(out), ap(d0), ap(d1), 0.0, o0, o1))
+    def scan(out, d0, d1, o0, o1, first=0.0):
+        op("v", [d0, d1], [out], lambda: g.vector.tensor_tensor_scan(ap(out), ap(d0), ap(d1), first, o0, o1))
 
     def act(out, in_, func=AF.Copy, **kw):
-        op("s", [in_] + list(kw.values()), [out], lambda: g.scalar.activation(ap(out), ap(in_), func, **{k: ap(x) for k, x in kw.items()}))
-
-    def fill(out, n, value):
-        act(out, v("half", 0, n), scale=2.0 * value)
+        op("s", [in_, kw.get("bias")], [out, kw.get("accum_out")],
+           lambda: g.scalar.activation(ap(out), ap(in_), func, **{k: ap(x) for k, x in kw.items()}))
 
     def quant(q, a, b, in_):
         qc, qs = v(q + "c", a, b), v(q + "s", a, b)
@@ -205,52 +207,44 @@ def rank_program(g, core, T, topo):
         else:
             ts(out, in_, scale, A.mult)
 
-    col = {k2: v("cols", i, i + 1) for i, k2 in enumerate(("i", "m0", "minus0", "rise"))}
+    col = {k2: v("cols", i, i + 1) for i, k2 in enumerate(("i", "m0", "minus0", "rise", "before", "slot"))}
 
-    def pair_lists(r):
-        W, n = LANES[r], NR[r] // 16
-        j = v("J", 0, n)
+    todo = []
+
+    width = [2]
+
+    def gap(n=None):
+        for _ in range(min(n or width[0], len(todo))):
+            todo.pop(0)()
+
+    def lists(r):
+        W, n, m, L, b0 = LANES[r], NR[r] // 16, NE[r] // 16, LANES[r] + 1, B0[r]
+        j, i = v("J", 0, n), v("J", 0, m)
         k, kw, kp, mn, mx = v("ti", 0, n), v("tf", 0, n), v("tf", 48, 48 + n), v("tf", 96, 96 + n), v("tf", 144, 144 + n)
-        ts(k, j, 1.0 / W, A.mult, -(W - 1) / (2.0 * W), A.add)
-        yield
-        ts(kw, k, -float(W), A.mult)
-        yield
-        tt(kp, j, kw, A.add)
-        yield
-        tt(mn, k, kp, A.min)
-        tt(mx, k, kp, A.max)
-        yield
-        ts(v("MX%d" % r), mx, 16.0, A.mult, 15.0, A.add)
-        ts(v("MN%d" % r), mn, 16.0, A.mult, 15.0, A.add)
-        yield
+        sg, sl, ps, ad = v("ti", 48, 48 + m), v("tf", 192, 192 + m), v("tf", 240, 240 + m), v("tf", 288, 288 + m)
+        s1 = v("tf", 336, 336 + m)
+        two = r > 1
+        calls = [lambda: ts(k, j, 1.0 / W, A.mult, -(W - 1) / (2.0 * W), A.add),
+                 lambda: ts(sg, i, 1.0 / L, A.mult, -(L - 1) / (2.0 * L), A.add),
+                 lambda: ts(kw, k, -float(W), A.mult),
+                 lambda: ts(sl, sg, -float(L), A.mult),
+                 lambda: tt(kp, j, kw, A.add),
+                 lambda: tt(ps, i, sl, A.add),
+                 two and (lambda: ts(ad, i, float(b0 * L), A.is_ge, float(L), A.mult)),
+                 lambda: tt(mn, k, kp, A.min),
+                 lambda: tt(mx, k, kp, A.max),
+                 two and (lambda: tt(s1, ps, ad, A.add)),
+                 lambda: ts(v("MN%d" % r), mn, 16.0, A.mult, 15.0, A.add),
+                 lambda: ts(v("MX%d" % r), mx, 16.0, A.mult, 15.0, A.add),
+                 lambda: vcopy(v("KL%d" % r), s1 if two else ps)]
+        return [c for c in calls if c]
 
-    def key_lists(r):
-        n, L, b0 = NE[r] // 16, LANES[r] + 1, B0[r]
-        j = v("J", 0, n)
-        sg, sl, ps, ad = v("ti", 48, 48 + n), v("tf", 192, 192 + n), v("tf", 240, 240 + n), v("tf", 288, 288 + n)
-        s1, s2 = v("tf", 304, 304 + n), v("tf", 320, 320 + n)
-        ts(sg, j, 1.0 / L, A.mult, -(L - 1) / (2.0 * L), A.add)
-        yield
-        ts(sl, sg, -float(L), A.mult)
-        if r > 1:
-            ts(ad, j, float(b0 * L), A.is_ge, float(L), A.mult)
-        yield
-        tt(ps, j, sl, A.add)
-        yield
-        if r == 1:
-            vcopy(v("KL1"), ps)
-        else:
-            tt(s1, ps, ad, A.add)
-            tt(s2, ps, ad, A.subtract)
-            yield
-            vcopy(v("KL%d" % r), s1)
-            ts(v("KB%d" % r), s2, float(L), A.add)
-        yield
-
-    def threshold_rows(r):
+    def threshold_rows(r, part):
         L, b0, t = LANES[r] + 1, B0[r], "T%d" % r
-        iota(v(t, 0, b0 * L), [[1, b0], [0, L]], 0)
-        iota(v(t, b0 * L), [[1, LANES[r] // 2 + 3], [0, L]], LANES[r] // 2)
+        if part == 0:
+            iota(v(t, 0, b0 * L), [[1, b0], [0, L]], 0)
+        else:
+            iota(v(t, b0 * L), [[1, SEGS[r] + 2 - b0], [0, L]], LANES[r] // 2)
 
     def tower0(r):
         x = v("T%d" % r, 0, B0[r] * (LANES[r] + 1))
@@ -258,39 +252,25 @@ def rank_program(g, core, T, topo):
 
     def cancels(r):
         W = LANES[r]
-        L, t = W + 1, "T%d" % r
-        ns = B0[r] + W // 2 + 1
-        u = v("tf", 416, 416 + ns)
-        ts(u, v(t, 0, ns * L, L), 0.5, A.mult, -(W - 0.5), A.add)
-        yield
-        tt(v(t, W, ns * L, L), v(t, 0, ns * L, L), u, A.mult)
-        yield
-        ts(v(t, W, W + 1), col["m0"], -P / 1024.0, A.mult)
-        yield
-
-    def together(*gens):
-        gens = list(gens)
-        while gens:
-            gens = [x for x in gens if next(x, 1) is None]
-            yield
+        L, t, ns = W + 1, "T%d" % r, SEGS[r]
+        u, e = v("tf", 416, 416 + ns), (W + 1) * L + W
+        return [lambda: ts(u, v(t, 0, ns * L, L), 0.5, A.mult, -(W - 0.5), A.add),
+                lambda: tt(v(t, W, ns * L, L), v(t, 0, ns * L, L), u, A.mult),
+                (lambda: ts(v(t, W, W + 1), col["m0"], -P / 1024.0, A.mult)) if r == 1 else
+                (lambda: ts(v(t, e, e + 1), col["slot"], W * (1 - W) / 2.0, A.add))]
 
     def signs(r):
         W, d = LANES[r], "D0%d" % r
-        fill(v(d), NR[r], 1.0)
-        fill(v(d, 0, W * W, W), W, 0.0)
-        fill(v(d, 1, (W + 1) * (W - 2) + 2, W + 1), W - 1, -1.0)
-        fill(v(d, W * W - 1, W * W), 1, -1.0)
+        if r > 1:
+            iota(v(d), [[0, NR[r]]], 1)
+        iota(v(d, 0, W * W, W), [[0, W]], 0)
+        iota(v(d, 1, (W + 1) * (W - 2) + 2, W + 1), [[0, W - 1]], -1)
+        iota(v(d, W * W - 1, W * W), [[0, 1]], -1)
 
     def resets(r):
-        W = LANES[r]
-        ns = B0[r] + W // 2 + 1
-        fill(v("DS%d" % r), NE[r], 1.0)
-        fill(v("DS%d" % r, 0, ns * (W + 1), W + 1), ns, 0.0)
-
-    def pump(f, n=99):
-        for _ in range(n):
-            if next(f, 1) is not None:
-                break
+        L = LANES[r] + 1
+        iota(v("DS%d" % r), [[0, NE[r]]], 1)
+        iota(v("DS%d" % r, 0, SEGS[r] * L, L), [[0, SEGS[r]]], 0)
 
     def plane(t, a=0, b=P):
         return v("V", VW * t + a, VW * t + b)
@@ -299,15 +279,15 @@ def rank_program(g, core, T, topo):
         for b in range(4):
             mm(bank + b, "EC", 128 * b, q, a, P)
 
-    def own_planes():
-        for t in range(4):
-            act(plane(t), v("p%d" % t, 0, P))
-            if t < 2:
-                dma("y", v("FQ", P * t, P * t + OWN[t]), plane(t, 0, OWN[t]))
+    def own_plane(t):
+        act(plane(t), v("p%d" % t, 0, P))
+        if t == 0:
+            dma("y", v("FQ"), plane(0))
 
     def gather_scores(r):
         n = 16 * LANES[r]
         tt(v("GM", 0, n), by(v("SS"), v("BL", 0, LANES[r])), v("m16", 0, n), A.mult)
+        gap()
         scan(v("SC", 0, n), v("hold", 0, n), v("GM", 0, n), A.mult, A.add)
 
     def pairs(r, q, a, b):
@@ -320,21 +300,22 @@ def rank_program(g, core, T, topo):
     def keys(r, tables):
         W, n = LANES[r], NR[r]
         scan(v("CS", 0, n), v("D0%d" % r), v("C", 0, n), A.mult, A.add)
+        gap()
         for i, tb in enumerate(tables):
             c = K0[r] + i * (W + 1)
             tt(v("KA", c, c + W), v(tb, 0, W), v("CS", W - 1, W * W, W), A.subtract)
+        gap()
 
-    def extract(r, lst, d):
-        W = LANES[r]
-        L, n = W + 1, NE[r]
-        ns = B0[r] + W // 2 + 1
+    def extract(r, lst, d, between=gap):
+        L, n, ns = LANES[r] + 1, NE[r], SEGS[r]
         tt(v("M", 0, n), by(v("KA", K0[r], K0[r] + (L if r == 1 else 2 * L)), v(lst)), v("T%d" % r, 0, n), A.min)
+        gap()
         scan(v("HS", 0, n), v("DS%d" % r), v("M", 0, n), A.mult, A.add)
+        between()
         tt(v(d, 0, ns - 1), v("HS", 2 * L - 1, ns * L, L), v("HS", L - 1, (ns - 1) * L, L), A.subtract)
 
-    def first_lists(r):
-        extract(r, "KL%d" % r, "D%d" % r)
-        ts(v("CL%d" % r), v("D%d" % r, 0, B0[r] + LANES[r] // 2), 1024.0, A.mult, P - 1.0, A.min)
+    def first_list(r):
+        ts(v("CL%d" % r), v("D%d" % r, 0, B0[r] + LANES[r] // 2), 1024.0, A.mult, P - 1.0 if r == 1 else P + 15.0, A.min)
 
     def next_tables(r):
         h, b0, d = LANES[r] // 2, B0[r], "D%d" % r
@@ -343,13 +324,20 @@ def rank_program(g, core, T, topo):
         dma("y", v("nB", 0, h, rows=slice(0, 128, 16)), v(d, 1, h + 1, rows=slice(0, 128, 16)))
         dma("y", v("nT", 0, h, rows=slice(0, 128, 16)), v(d, b0, b0 + h, rows=slice(15, 128, 16)))
 
-    def rows_of_bases(r, lst):
-        h = LANES[r] // 2
-        act(v("VB", 1, 1 + 16 * h), by(v("iotaR", 0, P), v(lst, B0[r], B0[r] + h)))
+    def partner_list(r):
+        W = LANES[r]
+        return [lambda: ts(v("TL", 0, W), v("nT", 0, W), 1024.0, A.mult),
+                lambda: tt(v("sl", 0, W), v("KK", 24 - W), v("CS", W - 1, W * W, W), A.subtract),
+                lambda: ts(v("RL", 0, W), v("sl", 0, W), 16.0, A.mult, col["before"], A.add)]
 
-    def scatter_links(r):
-        h = LANES[r] // 2
-        vcopy(by(v("UP"), v("CB", 0, h + 1)), v("VB", 0, 16 * h + 16))
+    def upper_bases(r):
+        W = LANES[r]
+        c0 = W // 4 * 2
+        vcopy(v("Z", 96 - 16 * (W - c0), 112), by(v("iotaR", 0, P + 16), v("CL%d" % r, c0, W + 1)))
+
+    def successors(r):
+        W = LANES[r]
+        act(v("NU", 0, 16 * W), by(v("Z", 96 - 8 * W), v("RL", 0, W)))
 
     def scatter_tops(r, values):
         h, b0 = LANES[r] // 2, B0[r]
@@ -357,23 +345,29 @@ def rank_program(g, core, T, topo):
 
     def blend_list():
         scan(v("ht"), v("climb"), v("UP", 0, P), A.add, A.max)
+        gap()
         ts(v("UL"), v("ht", 15, P, 16), col["rise"], A.subtract)
+
+    def bases_of_e(r, win, lst):
+        n = 8 * LANES[r] + 16
+        for t in range(4):
+            act(v("tmp", n * t, n * t + n), by(win(t), v(lst, 0, n // 16)))
 
     def make_e(r, win, lst):
         h, b0 = LANES[r] // 2, B0[r]
         n = 16 * (h + 1)
         for t in range(4):
-            act(v("tmp", n * t, n * t + n), by(win(t), v(lst, 0, h + 1)))
-        for t in range(4):
             tt(v("E", t, 64 * h, 4), by(win(t), v(lst, b0, b0 + h)), v("tmp", n * t + 1, n * t + 1 + 16 * h), A.add)
+        gap()
 
     def layer(q, a, n):
-        for b in (3, 0, 2, 1):
+        for b in (1, 0, 2, 3):
             mm(4 + b, "WW", 128 * b, q, a, n)
 
-    def take_h(r, q, b, off):
+    def take_h(r, off):
         n = 8 * LANES[r]
-        evac(q, plane(b, P, P + n), v("p%d" % (4 + b), off, off + n), 0.015625)
+        for q, b in (("sv"[r > 1], 1), ("v", 0), ("v", 2), ("v", 3)):
+            evac(q, plane(b, P, P + n), v("p%d" % (4 + b), off, off + n), 0.015625)
 
     def near(r, t, a, b):
         return by(plane(t, 0, P + 8 * LANES[r]), v("UL", a // 16, b // 16))
@@ -384,196 +378,213 @@ def rank_program(g, core, T, topo):
     def add_fetched(r, t, a, b):
         tt(v(XB[r + 1], 4 * a + t, 4 * b, 4), v("tb", P * t + a, P * t + b), v("p%d" % t, a, b), A.add)
 
-    def add_near(r, t, a, b):
-        tt(v(XB[r + 1], 4 * a + t, 4 * b, 4), near(r, t, a, b), v("FQ", P * t + a, P * t + b), A.add)
+    def add_near(r, a, b):
+        tt(v(XB[r + 1], 4 * a, 4 * b, 4), near(r, 0, a, b), v("FQ", a, b), A.add)
 
-    def blend(r, off):
-        take_h(r, "s", 3, off)
-        for b in (0, 2, 1):
-            take_h(r, "v", b, off)
-        for t, a, b in ((3, 0, P), (2, 0, P), (1, 96, 256), (1, 256, P)):
+    def blend(r):
+        take_h(r, 0)
+        parts = ((1, 0, P), (2, 0, P), (3, 0, 256), (3, 256, P))
+        for t, a, b in parts:
             fetch(r, t, a, b)
-        add_near(r, 0, 0, P)
-        add_fetched(r, 3, 0, P)
-        add_near(r, 1, 0, 96)
-        for t, a, b in ((2, 0, P), (1, 96, 256), (1, 256, P)):
+        add_near(r, 0, P)
+        for t, a, b in parts:
+            gap()
             add_fetched(r, t, a, b)
+
+    def arrived(t):
+        return v("FP", P * t, P * t + P)
 
     dma("y", v("tw32"), T.tw[:, :])
     dma("s", v("ub"), T.u[:, :])
     for c in range(3):
         dma("y", v("X1", 512 * c, 512 * c + 512), T.x[:, 512 * c:512 * c + 512])
 
-    iota(v("ic"), [[0, 24]], 0, 1)
-    iota(v("mi"), [[1, 16]], 128, -1)
+    iota(v("ic", 0, 24), [[0, 24]], 0, 1)
     iota(v("J"), [[16, 44]], 0)
     iota(v("iotaR", 0, P), [[1, P]], 0)
-    iota(v("ui"), [[16, 8]], 0)
-    iota(v("KK"), [[-1, 24]], 22)
+    threshold_rows(1, 0)
     memset(v("half"), 0.5)
-    ts(v("ic"), v("ic"), 15, A.bitwise_and)
-    ts(v("mi"), v("mi"), 15, A.bitwise_and)
-    vcopy(v("il"), v("ic"))
-    ts(v("m16s"), v("mi"), 0.0, A.is_equal)
+    ts(v("ic", 0, 24), v("ic", 0, 24), 15, A.bitwise_and)
+    vcopy(v("ul"), v("J", 0, 8))
     ts(col["i"], v("ic", 0, 1), 1.0, A.mult)
-    act(v("m16"), by(v("m16s"), v("il")))
-    ts(col["m0"], v("ic", 0, 1), 0.0, A.is_equal)
+    vcopy(v("il"), v("ic", 0, 24))
     ts(v("J"), v("J"), col["i"], A.add)
+    ts(col["m0"], v("ic", 0, 1), 0.0, A.is_equal)
+    todo += lists(1)
+    gap(2)
     ts(col["minus0"], v("ic", 0, 1), 0.0, A.is_equal, -1.0, A.mult)
-    f1 = together(pair_lists(1), key_lists(1))
-    pump(f1, 3)
     vcopy(v("tw16"), v("tw32"))
+    gap(2)
     act(v("ms"), by(v("iotaR", 0, P), v("tw16")))
     dma("y", v("fe"), v("ms", rows=slice(0, 128, 16)))
-    vcopy(v("ul"), v("ui"))
     quant("QU", 0, 128, v("ub"))
-    pump(f1, 1)
-    vcopy(words(v("URc")), by(words(v("QUc")), v("ul")))
-    act(v("URs"), by(v("QUs"), v("ul")))
-    act(v("hold"), v("m16"), AF.Identity, scale=-1.0, bias=1.0)
+    ts(v("m16s"), v("iotaR", 0, 16), col["i"], A.is_equal)
     for c in range(3):
-        quant("QX1", 128 * c, 128 * c + 128, v("X1", 512 * c, 512 * c + 512))
+        a, b = 128 * c, 128 * c + 128
+        quant("QX1", a, b, v("X1", 4 * a, 4 * b))
+        send(raw(v("LBc", LAND[1] + a, LAND[1] + b)), raw(v("QX1c", a, b)), "ax%d" % c)
         if c == 0:
-            pump(f1)
+            vcopy(words(v("URc")), by(words(v("QUc")), v("ul")))
+            act(v("URs"), by(v("QUs"), v("ul")))
+        mm(4 + c, "UR", 0, "QX1", a, 128)
+    send(v("LBs", LAND[1], LAND[1] + P), v("QX1s"), "axs")
+    act(v("m16"), by(v("m16s"), v("il")))
+    act(v("hold"), v("m16"), AF.Identity, scale=-1.0, bias=1.0)
+    tower0(1)
+    act(v("D01"), v("half"), scale=2.0)
     dma("y", raw(v("WWc")), T.wc[:, :])
     dma("y", v("WWs"), T.ws[:, :])
 
-    send(raw(v("LBc", LAND[1], LAND[1] + P)), raw(v("QX1c")), "axc")
-    send(v("LBs", LAND[1], LAND[1] + P), v("QX1s"), "axs")
-    op("g", [v("half", 0, 516)], [v("zi")], lambda: g.affine_select(T.zi[:], T.half[:, 0:516], [[1, 516]], A.is_equal, 0.0, -3, -4))
-    threshold_rows(1)
-    iota(v("iotaR", P), [[1, 576 - P]], P)
-    threshold_rows(2)
-    threshold_rows(3)
-    iota(v("opc", 0, 48), [[1, 3], [3, 16]], P + 3)
-    iota(v("opc", 48, 51), [[1, 3]], P)
-    for c in range(3):
-        mm(4 + c, "UR", 0, "QX1", 128 * c, 128)
-    for c in range(3):
-        evac("sv"[c // 2], v("SS", 128 * c, 128 * c + 128), v("p%d" % (4 + c), 0, 128))
-    memset(v("KK", 23, 24), 1.0)
-    memset(v("KA"), 1e6)
-    vcopy(v("BL"), v("fe"))
-    ts(v("sl"), v("fe"), 1.0 / 1024, A.mult)
+    op("g", [v("half")], [v("zi")], lambda: g.affine_select(T.zi[:], T.half[:, 0:516], [[1, 516]], A.is_equal, 0.0, -3, -4))
+    iota(v("KK"), [[-1, 24]], 22)
+    threshold_rows(1, 1)
     signs(1)
+    iota(v("rest"), [[-1, 24 - SPLIT]], 23 - SPLIT)
+    resets(1)
+    iota(v("iotaR", P), [[1, 576 - P]], P)
+    iota(v("VB"), [[1, 208]], 192)
+    iota(v("ic", 24), [[-13, 2]], 14, 1)
+    gap(4)
+    for c in range(3):
+        evac("v", v("SS", 128 * c, 128 * c + 128), v("p%d" % (4 + c), 0, 128))
+        if c == 1:
+            vcopy(v("BL"), v("fe"))
+    gap(1)
     gather_scores(1)
     thirds = ((0, 192), (192, 384), (384, 576))
     for a, b in thirds:
         pairs(1, "s", a, b)
-    tt(v("tbB"), v("sl"), v("KK"), A.add)
-    for b in range(2):
+    for b in range(4):
         quant("EC", 128 * b, 128 * b + 128, v("zi", 3 - b, 515 - b))
-    tower0(1)
-    resets(1)
-    f1 = cancels(1)
+    unpack("QX1", 0, 0)
+    own_plane(0)
+    own_plane(1)
+    act(v("climb"), v("m16"), AF.Identity, scale=-33792.0, bias=1024.0)
+    c1 = cancels(1)
+    todo += [lambda: ts(v("sl"), v("fe"), 1.0 / 1024, A.mult),
+             lambda: memset(v("KK", 23, 24), 1.0),
+             c1[0],
+             lambda: memset(v("KA"), 1e6),
+             lambda: tt(v("tbB"), v("sl"), v("KK"), A.add),
+             c1[1],
+             lambda: ts(col["rise"], v("ic", 0, 1), -1024.0, A.mult, 15360.0, A.add),
+             c1[2],
+             lambda: memset(v("over", 24 - SPLIT), 0.0)] + lists(2)
     for a, b in thirds:
         compare(1, a, b)
-        if a == 0:
-            for b in range(2, 4):
-                quant("EC", 128 * b, 128 * b + 128, v("zi", 3 - b, 515 - b))
-    unpack("QX1", 0, 0)
-    pump(f1, 2)
+        gap(2 if a else 1)
     keys(1, ["tbB"])
-    pump(f1)
-    own_planes()
-    first_lists(1)
+    for c in range(24 - SPLIT):
+        act(v("beyond", 24 * c, 24 * c + 24), v("KA", 0, 24), AF.Relu, bias=-float(SPLIT + c), accum_out=v("over", c, c + 1))
+    extract(1, "KL1", "D1", lambda: tt(v("sl", 0, 24 - SPLIT), v("over", 0, 24 - SPLIT), v("rest"), A.subtract))
+    tt(v("D1", SEGS[1] - 1, 26), v("sl", 0, 24 - SPLIT), v("over", 1), A.subtract)
+    first_list(1)
     send(v("LL"), v("CL1"), "all1")
 
-    rows_of_bases(1, "CL1")
+    for r in (2, 3):
+        threshold_rows(r, 0)
+        threshold_rows(r, 1)
+        signs(r)
+        resets(r)
+    iota(v("Z", 112), [[1, 96]], P + 17)
+    iota(v("Z", 112, 208, 16), [[16, 6]], P + 1)
+    iota(v("Z", 127, 208, 16), [[16, 6]], P + 16)
+    iota(v("opc", 0, 48), [[1, 3], [3, 16]], P + 3)
+    iota(v("opc", 48, 51), [[1, 3]], P)
     unpack("LB", LAND[1], 4)
     for t in range(4):
-        act(v("FP", P * t, P * t + P), v("p%d" % (4 + t), 0, P))
-    next_tables(1)
+        act(arrived(t), v("p%d" % (4 + t), 0, P))
+        if t == 1:
+            act(v("VB", 1, 193), by(v("iotaR", 0, P), v("CL1", 14, 26)))
     ts(v("CB", 0, 14), v("D1", 0, 14), 1024.0, A.mult)
-    memset(v("VB", 0, 1), 0.0)
-    memset(v("VB", 193), 0.0)
-    ts(col["rise"], v("ic", 0, 1), -1024.0, A.mult, 15360.0, A.add)
-    ts(v("climb"), v("m16"), -33792.0, A.mult, 1024.0, A.add)
-    scatter_links(1)
     scatter_tops(1, v("iotaR", P, P + 192))
-    f2 = together(pair_lists(2), key_lists(2))
-    pump(f2, 2)
-    make_e(1, lambda t: v("FP", P * t, P * t + P), "LL")
+    gap()
+    vcopy(by(v("UP"), v("CB", 0, 13)), v("VB"))
+    bases_of_e(1, arrived, "LL")
+    before("y", touches("y", [v("LL")], [], False))
+    next_tables(1)
+    own_plane(2)
+    own_plane(3)
+    width[0] = 1
+    todo += [lambda: ts(v("ic", 24), v("ic", 24), 15, A.bitwise_and),
+             lambda: ts(col["slot"], v("ic", 0, 1), 0.0, A.not_equal, 1.0 / 1024, A.mult),
+             lambda: ts(col["before"], v("ic", 24, 25), 1.0, A.add),
+             lambda: ts(col["slot"], v("ic", 25), float(P), A.add, col["slot"], A.mult)]
+    gap(1)
+    make_e(1, arrived, "LL")
     quant("QE1", 0, 192, v("E"))
     layer("QE1", 0, 192)
-    tower0(2)
     blend_list()
-    blend(1, 0)
-    signs(2)
-    resets(2)
+    blend(1)
+    tower0(2)
     dma("y", v("vb"), T.v[:, :])
 
-    f2c, f3, f3c = cancels(2), together(pair_lists(3), key_lists(3)), cancels(3)
     for r in (2, 3):
         W = LANES[r]
         h, b0 = W // 2, B0[r]
         n, q = 16 * h, "QX%d" % r
-        quant(q, 0, 256, v(XB[r], 0, 1024))
-        quant(q, 256, P, v(XB[r], 1024))
-        mm(4, "UR", 0, q, 0, 256)
-        mm(5, "UR", 0, q, 256, 128)
+        for c in range(3):
+            quant(q, 128 * c, 128 * c + 128, v(XB[r], 512 * c, 512 * c + 512))
+            mm(4 + c, "UR", 0, q, 128 * c, 128)
         unpack(q, 0, 0)
         ts(v("BL", 0, W), v("nB", 0, W), 1024.0, A.mult)
+        gap(99)
+        for c in range(3):
+            evac(("ssv", "svv")[r - 2][c], v("SS", 128 * c, 128 * c + 128), v("p%d" % (4 + c), 0, 128))
+        for t in range(4):
+            own_plane(t)
+        cr, (tops, ranks, partners) = cancels(r), partner_list(r)
+        todo += [cr[0], lambda W=W: tt(v("tbB", 0, W), v("nB", 0, W), v("KK", 24 - W), A.add),
+                 lambda W=W: tt(v("tbT", 0, W), v("nT", 0, W), v("KK", 24 - W), A.add), cr[1], tops, cr[2]]
         if r == 2:
-            pump(f2)
-        evac("s", v("SS", 0, 256), v("p4", 0, 256))
-        evac("v", v("SS", 256, P), v("p5", 0, 128))
-        own_planes()
-        tt(v("tbB", 0, W), v("nB", 0, W), v("KK", 24 - W), A.add)
+            todo += lists(3)
+        gap()
         gather_scores(r)
-        tt(v("tbT", 0, W), v("nT", 0, W), v("KK", 24 - W), A.add)
+        gap()
         pairs(r, "v", 0, NR[r])
-        if r == 2:
-            pump(f2c, 1)
+        gap()
         compare(r, 0, NR[r])
-        if r == 2:
-            pump(f2c, 1)
+        gap()
         keys(r, ["tbB", "tbT"])
-        if r == 2:
-            pump(f2c)
-        first_lists(r)
+        todo.insert(0, ranks)
+        extract(r, "KL%d" % r, "D%d" % r, partners)
+        gap()
+        first_list(r)
+        bases_of_e(r, plane, "CL%d" % r)
+        gap()
+        upper_bases(r)
+        successors(r)
         make_e(r, plane, "CL%d" % r)
         quant("QE%d" % r, 0, 128, v("E", 0, 512))
         send(raw(v("LBc", LAND[r], LAND[r] + n)), raw(v("QE%dc" % r, 0, n)), "a%dc" % r)
         send(v("LBs", LAND[r], LAND[r] + n), v("QE%ds" % r, 0, n), "a%ds" % r)
         if r == 2:
             next_tables(2)
-        extract(r, "KB%d" % r, "DB")
-        ts(v("CB", 0, b0 + h), v("DB", 0, b0 + h), 1024.0, A.mult)
-        rows_of_bases(r, "CB")
-        if r == 2:
             tower0(3)
-            signs(3)
-            resets(3)
-            pump(f3, 3)
         else:
-            vcopy(v("opc", 15, 48, 16), v("opc", 48, 51))
-            quant("QV", 0, 128, v("vb"))
-        scatter_links(r)
-        scatter_tops(r, v("iotaR", P, P + n))
+            todo += [lambda: vcopy(v("opc", 15, 48, 16), v("opc", 48, 51))]
+        vcopy(by(v("UP"), v("TL", 0, W)), v("NU", 0, 16 * W))
+        gap()
         blend_list()
-        if r == 2:
-            pump(f3)
-            pump(f3c)
-        else:
+        gap(7)
+        if r == 3:
+            quant("QV", 0, 128, v("vb"))
             scatter_tops(3, v("opc", 0, 48))
             dma("y", T.op[:, :], v("UP", 0, P, rows=slice(0, 128, 16)))
         first = min(LAND[r], 528 - 128)
         layer("LB", first, 128)
         if r == 2:
-            blend(2, 0)
+            blend(2)
 
-    off = LAND[3] - first
-    take_h(3, "s", 3, off)
-    for b in (0, 2, 1):
-        take_h(3, "v", b, off)
-    runs = ((0, 256), (256, P))
-    for a, b in runs:
-        for t in (3, 2, 1):
+    take_h(3, LAND[3] - first)
+    for a, b in ((0, 256), (256, P)):
+        for t in (1, 2, 3):
             fetch(3, t, a, b)
-    for i, (a, b) in enumerate(runs):
-        add_near(3, 0, a, b)
-        for t in (3, 2, 1):
+    add_near(3, 0, 256)
+    add_fetched(3, 1, 0, 256)
+    add_near(3, 256, P)
+    for i, (a, b) in enumerate(((0, 256), (256, P))):
+        for t in range(2 - i, 4):
             add_fetched(3, t, a, b)
         quant("QX4", a, b, v("X2", 4 * a, 4 * b))
         mm(4 + i, "QV", 0, "QX4", a, b - a)

@@ -5,12 +5,16 @@ AF = ActivationFunctionType
 P = 384
 LANES = {1: 24, 2: 12, 3: 6}
 B0 = {1: 14, 2: 14, 3: 8}
-NR = {1: 576, 2: 144, 3: 48}
+ROW = {1: 24, 2: 12, 3: 8}
+NR = {r: ROW[r] * LANES[r] for r in ROW}
+SEG = {1: 25, 2: 13, 3: 8}
 SPLIT = 15
 SEGS = {1: 14 + SPLIT - 11, 2: 21, 3: 12}
-NE = {r: -(-SEGS[r] * (LANES[r] + 1) // 16) * 16 for r in SEGS}
+NE = {r: -(-SEGS[r] * SEG[r] // 16) * 16 for r in SEGS}
 K0 = {1: 0, 2: 32, 3: 64}
+TOP = {2: 48, 3: 72}
 VW = 576
+OWN = 128
 LAND = {1: 96, 2: 0, 3: 480}
 XB = {1: "X1", 2: "X2", 3: "X3", 4: "X2"}
 BF, F32, U16, I32, U8, FP8 = "bfloat16", "float32", "uint16", "int32", "uint8", "float8_e4m3fn_x4"
@@ -29,28 +33,27 @@ for _n, _c in (("QX1", P), ("QX2", P), ("QX3", P), ("QX4", P), ("QU", 128), ("UR
     _buf(_n + "s", _c, U8)
 for _n, _c, _t in (
         ("X1", 4 * P, BF), ("X2", 4 * P, BF), ("X3", 4 * P, BF), ("ub", 512, BF), ("vb", 512, BF), ("half", 576, BF),
-        ("zi", 516, BF), ("FP", 4 * P, BF), ("V", 4 * VW, BF), ("FQ", P, BF), ("E", 768, BF), ("tmp", 832, BF), ("tb", 4 * P, BF),
+        ("zi", 516, BF), ("FP", 4 * P, BF), ("V", 4 * VW, BF), ("FQ", P + OWN, BF), ("E", 768, BF), ("tmp", 832, BF), ("tb", 4 * P, BF),
         ("m16s", 16, BF), ("m16", P, BF), ("hold", P, BF), ("climb", P, BF), ("C", 576, BF), ("CS", 576, BF),
-        ("tw32", 24, I32), ("ic", 26, I32), ("ti", 96, I32),
-        ("tw16", 24, U16), ("il", 24, U16), ("ul", 8, U16), ("LL", 26, U16), ("CB", 16, U16), ("BL", 24, U16), ("UL", 24, U16),
-        ("TL", 12, U16), ("RL", 12, U16), ("Z", 208, F32), ("NU", 192, F32),
-        ("cols", 8, F32), ("iotaR", 576, F32), ("J", 44, F32), ("KK", 24, F32), ("fe", 24, F32), ("opc", 52, F32),
-        ("UP", P + 16, F32), ("ms", P, F32), ("ht", P, F32), ("ysb", P, F32), ("SS", P, F32), ("GM", P, F32), ("SC", P, F32),
+        ("tw32", 24, I32), ("ic", 48, I32), ("ti", 96, I32), ("i8", 6, I32), ("l8", 4, U16), ("KL1", NE[1] // 16, U16),
+        ("tw16", 24, U16), ("ms", P, F32), ("il", 24, U16), ("ul", 8, U16), ("LL", 26, U16), ("CB", 16, U16), ("BL", 24, U16), ("UL", 24, U16),
+        ("TL", 12, U16), ("RL", 12, U16), ("Z", 224, F32), ("NU", 192, F32),
+        ("cols", 8, F32), ("iotaR", 576, F32), ("J", 36, F32), ("KK", 24, F32), ("fe", 24, F32), ("opc", 52, F32),
+        ("UP", P + 16, F32), ("ht", P, F32), ("ysb", P, F32), ("SS", P, F32), ("GM", P, F32), ("SC", P, F32),
         ("BX", 576, F32), ("M", 688, F32), ("HS", 688, F32), ("tf", 448, F32), ("sl", 24, F32),
-        ("VB", 208, F32), ("tbB", 24, F32), ("tbT", 12, F32), ("nB", 12, F32), ("nT", 12, F32), ("KA", 80, F32),
+        ("VB", 208, F32), ("tbB", 24, F32), ("KA", 80, F32), ("TT2", 296, F32), ("TT3", NE[3], F32), ("KL2", NE[2] // 16, U16),
+        ("KS2", NE[2] // 16, U16), ("KS3", NE[3] // 16, U16),
         ("over", 25 - SPLIT, F32), ("rest", 24 - SPLIT, F32), ("beyond", 24 * (24 - SPLIT), F32)):
     _buf(_n, _c, _t)
 for _r in (1, 2, 3):
     _h = LANES[_r] // 2
-    _L = LANES[_r] + 1
-    for _n, _c, _t in (("D0", NR[_r], BF), ("DS", NE[_r], BF), ("T", (SEGS[_r] + 2) * _L, F32), ("D", 28, F32),
-                       ("CL", B0[_r] + _h, U16), ("MN", NR[_r] // 16, U16), ("MX", NR[_r] // 16, U16),
-                       ("KL", NE[_r] // 16, U16)):
+    for _n, _c, _t in (("D0", NR[_r], BF), ("DS", NE[_r], BF), ("T", (SEGS[_r] + 2) * SEG[_r], F32), ("D", 28, F32),
+                       ("CL", B0[_r] + _h, U16), ("MN", NR[_r] // 16, U16), ("MX", NR[_r] // 16, U16)):
         _buf(_n + str(_r), _c, _t)
 for _i in range(8):
     _buf("p%d" % _i, 512, F32, "psum")
 
-NDMA = 40
+NDMA = 44
 SEMAPHORES = (["vs", "ss", "ts", "gs", "loc", "ax0", "ax1", "ax2", "axs", "all1", "a2c", "a2s", "a3c", "a3s"]
               + ["d%d" % i for i in range(NDMA)])
 
@@ -82,7 +85,7 @@ def rank_program(g, core, T, topo):
 
     ENG = {"v": g.vector, "s": g.scalar, "t": g.tensor, "g": g, "y": g.sync}
     QSEM = {"v": "vs", "s": "ss", "t": "ts", "g": "gs"}
-    cnt, known, seen, nd = {}, {q: {} for q in ENG}, {}, [0]
+    cnt, known, seen, waited, nd = {}, {q: {} for q in ENG}, {}, {}, [0]
 
     def ap(x):
         if not isinstance(x, dict):
@@ -125,6 +128,7 @@ def rank_program(g, core, T, topo):
         for sem, val, clock in sorted(ev, key=lambda e: -e[1]):
             if known[q].get(sem, 0) < val:
                 ENG[q].wait_ge(T.sem[sem], val)
+                waited[sem] = max(waited.get(sem, 0), val)
                 for k2, v2 in clock.items():
                     if known[q].get(k2, 0) < v2:
                         known[q][k2] = v2
@@ -146,12 +150,12 @@ def rank_program(g, core, T, topo):
         cnt[sem] = cnt.get(sem, 0) + 1
         after(q, sem, acc)
 
-    def dma(q, out, in_):
+    def dma(q, out, in_, add=False):
         acc = touches(q, [in_], [out], True)
         before(q, acc)
         sem = "d%d" % nd[0]
         nd[0] += 1
-        ENG[q].dma_start(ap(out), ap(in_)).then_inc(T.sem[sem], 16)
+        ENG[q].dma_start(ap(out), ap(in_), **({"accum_op": A.add} if add else {})).then_inc(T.sem[sem], 16)
         cnt[sem] = 16
         after(q, sem, acc)
 
@@ -207,37 +211,75 @@ def rank_program(g, core, T, topo):
         else:
             ts(out, in_, scale, A.mult)
 
-    col = {k2: v("cols", i, i + 1) for i, k2 in enumerate(("i", "m0", "minus0", "rise", "before", "slot"))}
+    col = {k2: v("cols", i, i + 1) for i, k2 in enumerate(("i", "m0", "minus0", "rise", "before", "odd", "lane"))}
 
     todo = []
 
     width = [2]
 
     def gap(n=None):
-        for _ in range(min(n or width[0], len(todo))):
+        for _ in range(min(width[0] if n is None else n, len(todo))):
             todo.pop(0)()
 
-    def lists(r):
-        W, n, m, L, b0 = LANES[r], NR[r] // 16, NE[r] // 16, LANES[r] + 1, B0[r]
-        j, i = v("J", 0, n), v("J", 0, m)
+    def pair_lists(r):
+        W, n = LANES[r], NR[r] // 16
+        j = v("J", 0, n)
         k, kw, kp, mn, mx = v("ti", 0, n), v("tf", 0, n), v("tf", 48, 48 + n), v("tf", 96, 96 + n), v("tf", 144, 144 + n)
-        sg, sl, ps, ad = v("ti", 48, 48 + m), v("tf", 192, 192 + m), v("tf", 240, 240 + m), v("tf", 288, 288 + m)
-        s1 = v("tf", 336, 336 + m)
-        two = r > 1
-        calls = [lambda: ts(k, j, 1.0 / W, A.mult, -(W - 1) / (2.0 * W), A.add),
-                 lambda: ts(sg, i, 1.0 / L, A.mult, -(L - 1) / (2.0 * L), A.add),
-                 lambda: ts(kw, k, -float(W), A.mult),
-                 lambda: ts(sl, sg, -float(L), A.mult),
-                 lambda: tt(kp, j, kw, A.add),
-                 lambda: tt(ps, i, sl, A.add),
-                 two and (lambda: ts(ad, i, float(b0 * L), A.is_ge, float(L), A.mult)),
-                 lambda: tt(mn, k, kp, A.min),
-                 lambda: tt(mx, k, kp, A.max),
-                 two and (lambda: tt(s1, ps, ad, A.add)),
-                 lambda: ts(v("MN%d" % r), mn, 16.0, A.mult, 15.0, A.add),
-                 lambda: ts(v("MX%d" % r), mx, 16.0, A.mult, 15.0, A.add),
-                 lambda: vcopy(v("KL%d" % r), s1 if two else ps)]
-        return [c for c in calls if c]
+        return [lambda: ts(k, j, 1.0 / W, A.mult, -(W - 1) / (2.0 * W), A.add),
+                lambda: ts(kw, k, -float(W), A.mult),
+                lambda: tt(kp, j, kw, A.add),
+                lambda: tt(mx, k, kp, A.max),
+                lambda: tt(mn, k, kp, A.min),
+                lambda: ts(v("MX%d" % r), mx, 16.0, A.mult, 15.0, A.add),
+                lambda: ts(v("MN%d" % r), mn, 16.0, A.mult, 15.0, A.add)]
+
+    def key_lists(r):
+        W, L, m = LANES[r], SEG[r], NE[r] // 16
+        j, sg, sl, ps = v("J", 0, m), v("ti", 48, 48 + m), v("tf", 192, 192 + m), v("tf", 240, 240 + m)
+        return [lambda: ts(sg, j, 1.0 / L, A.mult, -(L - 1) / (2.0 * L), A.add),
+                lambda: ts(sl, sg, -float(L), A.mult),
+                lambda: tt(ps, j, sl, A.add),
+                lambda: vcopy(v("KL%d" % r), ps),
+                lambda: ts(v("KS%d" % r), ps, float(W), A.mult, W - 1.0, A.add)]
+
+    def lists_by_eight():
+        rows = v("iotaR", 15, 96, 32)
+        return [lambda: ts(v("i8"), v("ic", 0, 6), 7, A.bitwise_and),
+                lambda: ts(col["odd"], v("ic", 0, 1), 8.0, A.is_ge, 16.0, A.mult),
+                lambda: vcopy(v("l8"), v("i8", 0, 4)),
+                lambda: ts(col["lane"], v("i8", 0, 1), 16.0, A.mult, 15.0, A.add),
+                lambda: ts(v("KS3"), v("i8"), 8.0, A.mult, 5.0, A.add),
+                lambda: ts(v("MX3"), rows, col["odd"], A.add, col["lane"], A.max),
+                lambda: ts(v("MN3"), rows, col["odd"], A.add, col["lane"], A.min)]
+
+    def offsets(r):
+        W, L, b0, t = LANES[r], SEG[r], B0[r], "T%d" % r
+        n, h = SEGS[r] + 2 - b0, W // 2
+        iota(v(t, 0, b0 * L), [[-1, b0], [-1, L]], W - 2)
+        iota(v(t, b0 * L), [[-1, n], [-1, L]], W - 2 - h)
+        iota(v(t, W - 1, b0 * L, L), [[-1, b0]], 1)
+        iota(v(t, b0 * L + W - 1, None, L), [[-1, n]], 1 - h)
+
+    def later_ranks(r):
+        x = v("T%d" % r, SEG[r], B0[r] * SEG[r])
+        act(x, x, AF.Identity, bias=col["m0"])
+        for c in range(LANES[r] + 1, SEG[r]):
+            iota(v("T%d" % r, c, None, SEG[r]), [[0, SEGS[r] + 2]], 64)
+
+    def spread_tables(r):
+        L, a = SEG[r], B0[r] * SEG[r]
+        if r == 2:
+            act(v("TT2", 0, 192), by(v("KA", K0[2], K0[2] + L), v("KL2", 0, 12)))
+            act(v("TT2", a, a + 112), by(v("KA", TOP[2], TOP[2] + L), v("KL2", 0, 7)))
+        else:
+            act(v("TT3", 0, a), by(v("KA", K0[3], K0[3] + L), v("l8")))
+            act(v("TT3", a), by(v("KA", TOP[3], TOP[3] + L), v("l8", 0, 2)))
+        dma("g", v("TT%d" % r, 0, NE[r]), v("T%d" % r, 0, NE[r]), True)
+
+    def ends(r):
+        W, L, ns = LANES[r], SEG[r], SEGS[r]
+        y, u = v("T%d" % r, W, ns * L, L), v("tf", 416, 416 + ns)
+        return [lambda: ts(u, y, -0.5, A.mult, -W - 1.5, A.add), lambda: tt(y, y, u, A.mult)]
 
     def threshold_rows(r, part):
         L, b0, t = LANES[r] + 1, B0[r], "T%d" % r
@@ -253,22 +295,21 @@ def rank_program(g, core, T, topo):
     def cancels(r):
         W = LANES[r]
         L, t, ns = W + 1, "T%d" % r, SEGS[r]
-        u, e = v("tf", 416, 416 + ns), (W + 1) * L + W
-        return [lambda: ts(u, v(t, 0, ns * L, L), 0.5, A.mult, -(W - 0.5), A.add),
-                lambda: tt(v(t, W, ns * L, L), v(t, 0, ns * L, L), u, A.mult),
-                (lambda: ts(v(t, W, W + 1), col["m0"], -P / 1024.0, A.mult)) if r == 1 else
-                (lambda: ts(v(t, e, e + 1), col["slot"], W * (1 - W) / 2.0, A.add))]
+        u = v("tf", 417, 416 + ns)
+        return [lambda: ts(u, v(t, L, ns * L, L), 0.5, A.mult, -(W - 0.5), A.add),
+                lambda: tt(v(t, L + W, ns * L, L), v(t, L, ns * L, L), u, A.mult),
+                lambda: ts(v(t, W, W + 1), col["minus0"], P / 1024.0, A.mult)]
 
     def signs(r):
-        W, d = LANES[r], "D0%d" % r
+        W, R, d = LANES[r], ROW[r], "D0%d" % r
         if r > 1:
             iota(v(d), [[0, NR[r]]], 1)
-        iota(v(d, 0, W * W, W), [[0, W]], 0)
-        iota(v(d, 1, (W + 1) * (W - 2) + 2, W + 1), [[0, W - 1]], -1)
-        iota(v(d, W * W - 1, W * W), [[0, 1]], -1)
+        iota(v(d, 0, None, R), [[0, W]], 0)
+        iota(v(d, 1, (R + 1) * (W - 2) + 2, R + 1), [[0, W - 1]], -1)
+        iota(v(d, (R + 1) * (W - 1), (R + 1) * (W - 1) + 1), [[0, 1]], -1)
 
     def resets(r):
-        L = LANES[r] + 1
+        L = SEG[r]
         iota(v("DS%d" % r), [[0, NE[r]]], 1)
         iota(v("DS%d" % r, 0, SEGS[r] * L, L), [[0, SEGS[r]]], 0)
 
@@ -281,8 +322,8 @@ def rank_program(g, core, T, topo):
 
     def own_plane(t):
         act(plane(t), v("p%d" % t, 0, P))
-        if t == 0:
-            dma("y", v("FQ"), plane(0))
+        if t < 2:
+            dma("y", v("FQ", P * t, P * t + (P, OWN)[t]), plane(t, 0, (P, OWN)[t]))
 
     def gather_scores(r):
         n = 16 * LANES[r]
@@ -297,47 +338,47 @@ def rank_program(g, core, T, topo):
     def compare(r, a, b):
         tt(v("C", a, b), by(v("SC"), v("MN%d" % r, a // 16, b // 16)), v("BX", a, b), A.is_ge)
 
-    def keys(r, tables):
-        W, n = LANES[r], NR[r]
-        scan(v("CS", 0, n), v("D0%d" % r), v("C", 0, n), A.mult, A.add)
-        gap()
-        for i, tb in enumerate(tables):
-            c = K0[r] + i * (W + 1)
-            tt(v("KA", c, c + W), v(tb, 0, W), v("CS", W - 1, W * W, W), A.subtract)
+    def rank_sums(r):
+        scan(v("CS", 0, NR[r]), v("D0%d" % r), v("C", 0, NR[r]), A.mult, A.add)
         gap()
 
-    def extract(r, lst, d, between=gap):
-        L, n, ns = LANES[r] + 1, NE[r], SEGS[r]
-        tt(v("M", 0, n), by(v("KA", K0[r], K0[r] + (L if r == 1 else 2 * L)), v(lst)), v("T%d" % r, 0, n), A.min)
+    def extract(r, between):
+        L, n, ns = SEG[r], NE[r], SEGS[r]
+        if r == 1:
+            tt(v("M", 0, n), by(v("KA", 0, L), v("KL1")), v("T1", 0, n), A.min)
+        else:
+            tt(v("M", 0, n), by(v("CS"), v("KS%d" % r)), v("TT%d" % r, 0, n), A.max)
         gap()
         scan(v("HS", 0, n), v("DS%d" % r), v("M", 0, n), A.mult, A.add)
         between()
-        tt(v(d, 0, ns - 1), v("HS", 2 * L - 1, ns * L, L), v("HS", L - 1, (ns - 1) * L, L), A.subtract)
+        later, earlier = v("HS", 2 * L - 1, ns * L, L), v("HS", L - 1, (ns - 1) * L, L)
+        tt(v("D%d" % r, 0, ns - 1), *((later, earlier) if r == 1 else (earlier, later)), A.subtract)
 
     def first_list(r):
-        ts(v("CL%d" % r), v("D%d" % r, 0, B0[r] + LANES[r] // 2), 1024.0, A.mult, P - 1.0 if r == 1 else P + 15.0, A.min)
+        ts(v("CL%d" % r), v("D%d" % r, 0, B0[r] + LANES[r] // 2), 1024.0, A.mult, P - 1.0, A.min)
 
     def next_tables(r):
-        h, b0, d = LANES[r] // 2, B0[r], "D%d" % r
-        dma("y", v("nB", 0, h), v(d, 0, h))
-        dma("y", v("nT", 0, h, rows=slice(1, 128)), v(d, b0, b0 + h, rows=slice(0, 127)))
-        dma("y", v("nB", 0, h, rows=slice(0, 128, 16)), v(d, 1, h + 1, rows=slice(0, 128, 16)))
-        dma("y", v("nT", 0, h, rows=slice(0, 128, 16)), v(d, b0, b0 + h, rows=slice(15, 128, 16)))
+        h, b0, d, nb, nt = LANES[r] // 2, B0[r], "D%d" % r, K0[r + 1], TOP[r + 1]
+        dma("y", v("KA", nb, nb + h), v(d, 0, h))
+        dma("y", v("KA", nt, nt + h, rows=slice(1, 128)), v(d, b0, b0 + h, rows=slice(0, 127)))
+        dma("y", v("KA", nb, nb + h, rows=slice(0, 128, 16)), v(d, 1, h + 1, rows=slice(0, 128, 16)))
+        dma("y", v("KA", nt, nt + h, rows=slice(0, 128, 16)), v(d, b0, b0 + h, rows=slice(15, 128, 16)))
 
     def partner_list(r):
         W = LANES[r]
-        return [lambda: ts(v("TL", 0, W), v("nT", 0, W), 1024.0, A.mult),
-                lambda: tt(v("sl", 0, W), v("KK", 24 - W), v("CS", W - 1, W * W, W), A.subtract),
+        return [lambda: ts(v("TL", 0, W), v("KA", TOP[r], TOP[r] + W), 1024.0, A.mult),
+                lambda: tt(v("sl", 0, W), v("KK", 24 - W), v("CS", W - 1, NR[r], ROW[r]), A.subtract),
                 lambda: ts(v("RL", 0, W), v("sl", 0, W), 16.0, A.mult, col["before"], A.add)]
 
     def upper_bases(r):
         W = LANES[r]
         c0 = W // 4 * 2
-        vcopy(v("Z", 96 - 16 * (W - c0), 112), by(v("iotaR", 0, P + 16), v("CL%d" % r, c0, W + 1)))
+        vcopy(v("Z", 96 - 16 * (W - c0), 112), by(v("iotaR", 0, P), v("CL%d" % r, c0, W + 1)))
 
     def successors(r):
         W = LANES[r]
-        act(v("NU", 0, 16 * W), by(v("Z", 96 - 8 * W), v("RL", 0, W)))
+        act(v("Z", 97, 112), v("Z", 209))
+        act(v("NU", 0, 16 * W), by(v("Z", 96 - 8 * W, 208), v("RL", 0, W)))
 
     def scatter_tops(r, values):
         h, b0 = LANES[r] // 2, B0[r]
@@ -348,10 +389,10 @@ def rank_program(g, core, T, topo):
         gap()
         ts(v("UL"), v("ht", 15, P, 16), col["rise"], A.subtract)
 
-    def bases_of_e(r, win, lst):
+    def bases_of_e(r, win, lst, planes, copy=act):
         n = 8 * LANES[r] + 16
-        for t in range(4):
-            act(v("tmp", n * t, n * t + n), by(win(t), v(lst, 0, n // 16)))
+        for t in planes:
+            copy(v("tmp", n * t, n * t + n), by(win(t), v(lst, 0, n // 16)))
 
     def make_e(r, win, lst):
         h, b0 = LANES[r] // 2, B0[r]
@@ -378,18 +419,20 @@ def rank_program(g, core, T, topo):
     def add_fetched(r, t, a, b):
         tt(v(XB[r + 1], 4 * a + t, 4 * b, 4), v("tb", P * t + a, P * t + b), v("p%d" % t, a, b), A.add)
 
-    def add_near(r, a, b):
-        tt(v(XB[r + 1], 4 * a, 4 * b, 4), near(r, 0, a, b), v("FQ", a, b), A.add)
+    def add_near(r, t, a, b):
+        tt(v(XB[r + 1], 4 * a + t, 4 * b, 4), near(r, t, a, b), v("FQ", P * t + a, P * t + b), A.add)
 
     def blend(r):
         take_h(r, 0)
-        parts = ((1, 0, P), (2, 0, P), (3, 0, 256), (3, 256, P))
+        own = OWN // (2 if r == 1 else 1)
+        parts = ((1, own, P), (2, 0, P), (3, 0, 256), (3, 256, P))
         for t, a, b in parts:
             fetch(r, t, a, b)
-        add_near(r, 0, P)
+        add_near(r, 0, 0, P)
         for t, a, b in parts:
-            gap()
             add_fetched(r, t, a, b)
+            if t == 1:
+                add_near(r, 1, 0, own)
 
     def arrived(t):
         return v("FP", P * t, P * t + P)
@@ -397,28 +440,31 @@ def rank_program(g, core, T, topo):
     dma("y", v("tw32"), T.tw[:, :])
     dma("s", v("ub"), T.u[:, :])
     for c in range(3):
-        dma("y", v("X1", 512 * c, 512 * c + 512), T.x[:, 512 * c:512 * c + 512])
+        dma("ysy"[c], v("X1", 512 * c, 512 * c + 512), T.x[:, 512 * c:512 * c + 512])
 
-    iota(v("ic", 0, 24), [[0, 24]], 0, 1)
-    iota(v("J"), [[16, 44]], 0)
-    iota(v("iotaR", 0, P), [[1, P]], 0)
-    threshold_rows(1, 0)
+    iota(v("ic"), [[14, 2], [0, 24]], 0, 1)
+    iota(v("J"), [[16, 36]], 0)
     memset(v("half"), 0.5)
-    ts(v("ic", 0, 24), v("ic", 0, 24), 15, A.bitwise_and)
-    vcopy(v("ul"), v("J", 0, 8))
+    op("g", [v("half")], [v("zi")], lambda: g.affine_select(T.zi[:], T.half[:, 0:516], [[1, 516]], A.is_equal, 0.0, -3, -4))
+    threshold_rows(1, 0)
+    ts(v("ic"), v("ic"), 15, A.bitwise_and)
+    scan(v("iotaR", 0, P), v("half", 0, P), v("half", 0, P), A.add, A.add, -1.0)
     ts(col["i"], v("ic", 0, 1), 1.0, A.mult)
+    vcopy(v("ul"), v("J", 0, 8))
     vcopy(v("il"), v("ic", 0, 24))
-    ts(v("J"), v("J"), col["i"], A.add)
-    ts(col["m0"], v("ic", 0, 1), 0.0, A.is_equal)
-    todo += lists(1)
-    gap(2)
-    ts(col["minus0"], v("ic", 0, 1), 0.0, A.is_equal, -1.0, A.mult)
     vcopy(v("tw16"), v("tw32"))
-    gap(2)
+    ts(v("m16s"), v("iotaR", 0, 16), col["i"], A.is_equal)
+    ts(v("J"), v("J"), col["i"], A.add)
     act(v("ms"), by(v("iotaR", 0, P), v("tw16")))
     dma("y", v("fe"), v("ms", rows=slice(0, 128, 16)))
+    p1, k1 = pair_lists(1), key_lists(1)
+    todo += [lambda: ts(col["minus0"], v("ic", 0, 1), 0.0, A.is_equal, -1.0, A.mult), k1[0],
+             p1[0], k1[1], lambda: memset(v("KA"), 0.0),
+             p1[1], k1[2], p1[2], k1[3],
+             lambda: ts(v("sl"), v("fe"), 1.0 / 1024, A.mult)] + p1[3:]
+    gap(2)
     quant("QU", 0, 128, v("ub"))
-    ts(v("m16s"), v("iotaR", 0, 16), col["i"], A.is_equal)
+    gap(3)
     for c in range(3):
         a, b = 128 * c, 128 * c + 128
         quant("QX1", a, b, v("X1", 4 * a, 4 * b))
@@ -426,98 +472,106 @@ def rank_program(g, core, T, topo):
         if c == 0:
             vcopy(words(v("URc")), by(words(v("QUc")), v("ul")))
             act(v("URs"), by(v("QUs"), v("ul")))
+        if c == 1:
+            gap(2)
         mm(4 + c, "UR", 0, "QX1", a, 128)
     send(v("LBs", LAND[1], LAND[1] + P), v("QX1s"), "axs")
     act(v("m16"), by(v("m16s"), v("il")))
+
+    iota(v("KK"), [[-1, 24]], 22)
+    iota(v("KK", 23), [[0, 1]], 1)
+    threshold_rows(1, 1)
+    for c in range(3):
+        gap((2, 0, 0)[c])
+        evac("v", v("SS", 128 * c, 128 * c + 128), v("p%d" % (4 + c), 0, 128))
+        if c == 1:
+            vcopy(v("BL"), v("fe"))
+    gap(2)
     act(v("hold"), v("m16"), AF.Identity, scale=-1.0, bias=1.0)
     tower0(1)
     act(v("D01"), v("half"), scale=2.0)
-    dma("y", raw(v("WWc")), T.wc[:, :])
-    dma("y", v("WWs"), T.ws[:, :])
-
-    op("g", [v("half")], [v("zi")], lambda: g.affine_select(T.zi[:], T.half[:, 0:516], [[1, 516]], A.is_equal, 0.0, -3, -4))
-    iota(v("KK"), [[-1, 24]], 22)
-    threshold_rows(1, 1)
     signs(1)
     iota(v("rest"), [[-1, 24 - SPLIT]], 23 - SPLIT)
     resets(1)
     iota(v("iotaR", P), [[1, 576 - P]], P)
-    iota(v("VB"), [[1, 208]], 192)
-    iota(v("ic", 24), [[-13, 2]], 14, 1)
-    gap(4)
-    for c in range(3):
-        evac("v", v("SS", 128 * c, 128 * c + 128), v("p%d" % (4 + c), 0, 128))
-        if c == 1:
-            vcopy(v("BL"), v("fe"))
-    gap(1)
+    iota(v("VB", 0, 1), [[0, 1]], 0)
+    iota(v("VB", 193), [[1, 15]], P + 1)
     gather_scores(1)
     thirds = ((0, 192), (192, 384), (384, 576))
     for a, b in thirds:
         pairs(1, "s", a, b)
+    gap(1)
     for b in range(4):
         quant("EC", 128 * b, 128 * b + 128, v("zi", 3 - b, 515 - b))
     unpack("QX1", 0, 0)
     own_plane(0)
     own_plane(1)
-    act(v("climb"), v("m16"), AF.Identity, scale=-33792.0, bias=1024.0)
+    dma("y", raw(v("WWc")), T.wc[:, :])
+    dma("y", v("WWs"), T.ws[:, :])
     c1 = cancels(1)
-    todo += [lambda: ts(v("sl"), v("fe"), 1.0 / 1024, A.mult),
-             lambda: memset(v("KK", 23, 24), 1.0),
-             c1[0],
-             lambda: memset(v("KA"), 1e6),
-             lambda: tt(v("tbB"), v("sl"), v("KK"), A.add),
-             c1[1],
-             lambda: ts(col["rise"], v("ic", 0, 1), -1024.0, A.mult, 15360.0, A.add),
-             c1[2],
-             lambda: memset(v("over", 24 - SPLIT), 0.0)] + lists(2)
+    k2 = key_lists(2)
+    climb = [lambda a=a: ts(v("climb", a, a + 128), v("m16", a, a + 128), -33792.0, A.mult, 1024.0, A.add) for a in (0, 128, 256)]
+    todo += [c1[0], lambda: tt(v("tbB"), v("sl"), v("KK"), A.add),
+             c1[1], c1[2],
+             k2[0], lambda: memset(v("over", 24 - SPLIT), 0.0),
+             k2[1], climb[0],
+             k2[2], lambda: ts(col["m0"], v("ic", 0, 1), 0.0, A.is_equal),
+             climb[1],
+             k2[3], climb[2]]
     for a, b in thirds:
         compare(1, a, b)
-        gap(2 if a else 1)
-    keys(1, ["tbB"])
+    gap()
+    rank_sums(1)
+    tt(v("KA", 0, 24), v("tbB"), v("CS", 23, 576, 24), A.subtract)
+    gap()
     for c in range(24 - SPLIT):
         act(v("beyond", 24 * c, 24 * c + 24), v("KA", 0, 24), AF.Relu, bias=-float(SPLIT + c), accum_out=v("over", c, c + 1))
-    extract(1, "KL1", "D1", lambda: tt(v("sl", 0, 24 - SPLIT), v("over", 0, 24 - SPLIT), v("rest"), A.subtract))
+    extract(1, lambda: tt(v("sl", 0, 24 - SPLIT), v("over", 0, 24 - SPLIT), v("rest"), A.subtract))
     tt(v("D1", SEGS[1] - 1, 26), v("sl", 0, 24 - SPLIT), v("over", 1), A.subtract)
+    gap()
     first_list(1)
     send(v("LL"), v("CL1"), "all1")
 
-    for r in (2, 3):
-        threshold_rows(r, 0)
-        threshold_rows(r, 1)
-        signs(r)
-        resets(r)
-    iota(v("Z", 112), [[1, 96]], P + 17)
-    iota(v("Z", 112, 208, 16), [[16, 6]], P + 1)
-    iota(v("Z", 127, 208, 16), [[16, 6]], P + 16)
-    iota(v("opc", 0, 48), [[1, 3], [3, 16]], P + 3)
-    iota(v("opc", 48, 51), [[1, 3]], P)
+    offsets(2)
+    dma("g", v("vb"), T.v[:, :])
     unpack("LB", LAND[1], 4)
     for t in range(4):
         act(arrived(t), v("p%d" % (4 + t), 0, P))
         if t == 1:
             act(v("VB", 1, 193), by(v("iotaR", 0, P), v("CL1", 14, 26)))
     ts(v("CB", 0, 14), v("D1", 0, 14), 1024.0, A.mult)
+    gap(1)
     scatter_tops(1, v("iotaR", P, P + 192))
     gap()
     vcopy(by(v("UP"), v("CB", 0, 13)), v("VB"))
-    bases_of_e(1, arrived, "LL")
+    bases_of_e(1, arrived, "LL", range(4))
     before("y", touches("y", [v("LL")], [], False))
     next_tables(1)
+    later_ranks(2)
+    signs(2)
+    resets(2)
     own_plane(2)
     own_plane(3)
-    width[0] = 1
-    todo += [lambda: ts(v("ic", 24), v("ic", 24), 15, A.bitwise_and),
-             lambda: ts(col["slot"], v("ic", 0, 1), 0.0, A.not_equal, 1.0 / 1024, A.mult),
-             lambda: ts(col["before"], v("ic", 24, 25), 1.0, A.add),
-             lambda: ts(col["slot"], v("ic", 25), float(P), A.add, col["slot"], A.mult)]
-    gap(1)
+    e2 = ends(2)
+    p2 = pair_lists(2)
+    ts(col["rise"], v("ic", 0, 1), -1024.0, A.mult, 15360.0, A.add)
+    todo += [e2[0], p2[0], e2[1], p2[1], p2[2], k2[4]] + p2[3:] + [lambda: ts(col["before"], v("ic", 24, 25), 1.0, A.add)]
     make_e(1, arrived, "LL")
     quant("QE1", 0, 192, v("E"))
     layer("QE1", 0, 192)
     blend_list()
     blend(1)
-    tower0(2)
-    dma("y", v("vb"), T.v[:, :])
+    spread_tables(2)
+    iota(v("Z", 112, 208), [[1, 96]], P + 17)
+    iota(v("Z", 209, 223), [[1, 14]], P + 2)
+    iota(v("Z", 223), [[0, 1]], P)
+    iota(v("Z", 112, 208, 16), [[16, 6]], P + 1)
+    iota(v("Z", 127, 208, 16), [[16, 6]], P + 16)
+    offsets(3)
+    signs(3)
+    resets(3)
+    iota(v("opc", 0, 48), [[1, 3], [3, 16]], P + 3)
+    iota(v("opc", 48, 51), [[1, 3]], P)
 
     for r in (2, 3):
         W = LANES[r]
@@ -527,32 +581,36 @@ def rank_program(g, core, T, topo):
             quant(q, 128 * c, 128 * c + 128, v(XB[r], 512 * c, 512 * c + 512))
             mm(4 + c, "UR", 0, q, 128 * c, 128)
         unpack(q, 0, 0)
-        ts(v("BL", 0, W), v("nB", 0, W), 1024.0, A.mult)
-        gap(99)
+        ts(v("BL", 0, W), v("KA", K0[r], K0[r] + W), 1024.0, A.mult)
+        gap(2)
         for c in range(3):
-            evac(("ssv", "svv")[r - 2][c], v("SS", 128 * c, 128 * c + 128), v("p%d" % (4 + c), 0, 128))
+            evac("svv"[c], v("SS", 128 * c, 128 * c + 128), v("p%d" % (4 + c), 0, 128))
         for t in range(4):
             own_plane(t)
-        cr, (tops, ranks, partners) = cancels(r), partner_list(r)
-        todo += [cr[0], lambda W=W: tt(v("tbB", 0, W), v("nB", 0, W), v("KK", 24 - W), A.add),
-                 lambda W=W: tt(v("tbT", 0, W), v("nT", 0, W), v("KK", 24 - W), A.add), cr[1], tops, cr[2]]
+        tops, ranks, partners = partner_list(r)
+        todo += [tops]
         if r == 2:
-            todo += lists(3)
+            later_ranks(3)
+            todo += lists_by_eight() + ends(3)
+        else:
+            todo += [lambda: quant("QV", 0, 128, v("vb")), lambda: vcopy(v("opc", 15, 48, 16), v("opc", 48, 51))]
         gap()
         gather_scores(r)
+        width[0] = 1
         gap()
         pairs(r, "v", 0, NR[r])
         gap()
         compare(r, 0, NR[r])
         gap()
-        keys(r, ["tbB", "tbT"])
+        rank_sums(r)
         todo.insert(0, ranks)
-        extract(r, "KL%d" % r, "D%d" % r, partners)
+        extract(r, partners)
         gap()
         first_list(r)
-        bases_of_e(r, plane, "CL%d" % r)
+        bases_of_e(r, plane, "CL%d" % r, range(3))
         gap()
         upper_bases(r)
+        bases_of_e(r, plane, "CL%d" % r, [3], vcopy)
         successors(r)
         make_e(r, plane, "CL%d" % r)
         quant("QE%d" % r, 0, 128, v("E", 0, 512))
@@ -560,15 +618,13 @@ def rank_program(g, core, T, topo):
         send(v("LBs", LAND[r], LAND[r] + n), v("QE%ds" % r, 0, n), "a%ds" % r)
         if r == 2:
             next_tables(2)
-            tower0(3)
-        else:
-            todo += [lambda: vcopy(v("opc", 15, 48, 16), v("opc", 48, 51))]
         vcopy(by(v("UP"), v("TL", 0, W)), v("NU", 0, 16 * W))
-        gap()
+        gap(2)
         blend_list()
-        gap(7)
+        gap(99)
+        if r == 2:
+            spread_tables(3)
         if r == 3:
-            quant("QV", 0, 128, v("vb"))
             scatter_tops(3, v("opc", 0, 48))
             dma("y", T.op[:, :], v("UP", 0, P, rows=slice(0, 128, 16)))
         first = min(LAND[r], 528 - 128)
@@ -579,13 +635,15 @@ def rank_program(g, core, T, topo):
     take_h(3, LAND[3] - first)
     for a, b in ((0, 256), (256, P)):
         for t in (1, 2, 3):
-            fetch(3, t, a, b)
-    add_near(3, 0, 256)
-    add_fetched(3, 1, 0, 256)
-    add_near(3, 256, P)
+            fetch(3, t, max(a, OWN) if t == 1 else a, b)
+    add_near(3, 0, 0, P)
+    add_fetched(3, 1, OWN, 256)
+    add_near(3, 1, 0, OWN)
     for i, (a, b) in enumerate(((0, 256), (256, P))):
-        for t in range(2 - i, 4):
+        for t in (2, 3):
             add_fetched(3, t, a, b)
+        if i == 0:
+            add_fetched(3, 1, 256, P)
         quant("QX4", a, b, v("X2", 4 * a, 4 * b))
         mm(4 + i, "QV", 0, "QX4", a, b - a)
         dma("y", T.oc[:, 4 * a:4 * b], raw(v("QX4c", a, b)))
@@ -597,5 +655,5 @@ def rank_program(g, core, T, topo):
     dma("y", T.y[:, 256:P], v("ysb", 256, P))
 
     for sem, val in cnt.items():
-        if known["g"].get(sem, 0) < val:
+        if waited.get(sem, 0) < val:
             g.wait_ge(T.sem[sem], val)

@@ -4,21 +4,16 @@ A = AluOpType
 AF = ActivationFunctionType
 P = 384
 LANES = {1: 24, 2: 12, 3: 6}
-B0 = {1: 14, 2: 14, 3: 8}
-ROW = {1: 24, 2: 12, 3: 8}
-NR = {r: ROW[r] * LANES[r] for r in ROW}
-SEG = {1: 25, 2: 13, 3: 8}
-SPLIT = 15
-SEGS = {1: 14 + SPLIT - 11, 2: 21, 3: 12}
-NE = {r: -(-SEGS[r] * SEG[r] // 16) * 16 for r in SEGS}
-K0 = {1: 0, 2: 32, 3: 64}
-TOP = {2: 48, 3: 72}
+NR = {1: 576, 2: 144, 3: 48}
+NE = {1: 608, 2: 160, 3: 48}
+UPC = {1: 0, 2: 0, 3: 4}
+LOC = {1: 12, 2: 6, 3: 0}
+SECOND = 320
 VW = 576
-OWN = 128
-LAND = {1: 96, 2: 0, 3: 480}
+OWN = {1: 256, 2: 256, 3: 128}
 XB = {1: "X1", 2: "X2", 3: "X3", 4: "X2"}
-BF, F32, U16, I32, U8, FP8 = "bfloat16", "float32", "uint16", "int32", "uint8", "float8_e4m3fn_x4"
-SIZE = {BF: 2, F32: 4, U16: 2, I32: 4, U8: 1, FP8: 4}
+BF, F32, F16, U16, I32, U8, FP8 = "bfloat16", "float32", "float16", "uint16", "int32", "uint8", "float8_e4m3fn_x4"
+SIZE = {BF: 2, F32: 4, F16: 2, U16: 2, I32: 4, U8: 1, FP8: 4}
 
 SCRATCH = {}
 
@@ -28,33 +23,34 @@ def _buf(name, cols, dtype, where="sbuf"):
 
 
 for _n, _c in (("QX1", P), ("QX2", P), ("QX3", P), ("QX4", P), ("QU", 128), ("UR", 128), ("QV", 128), ("WW", 512),
-               ("EC", 512), ("LB", 528), ("QE1", 192), ("QE2", 128), ("QE3", 128)):
+               ("EC", 512), ("LB1", P + 64), ("LB2", P), ("QE1", 192), ("QE2", 128), ("QE3", 128)):
     _buf(_n + "c", _c, FP8)
     _buf(_n + "s", _c, U8)
 for _n, _c, _t in (
         ("X1", 4 * P, BF), ("X2", 4 * P, BF), ("X3", 4 * P, BF), ("ub", 512, BF), ("vb", 512, BF), ("half", 576, BF),
-        ("zi", 516, BF), ("FP", 4 * P, BF), ("V", 4 * VW, BF), ("FQ", P + OWN, BF), ("E", 768, BF), ("tmp", 832, BF), ("tb", 4 * P, BF),
-        ("m16s", 16, BF), ("m16", P, BF), ("hold", P, BF), ("climb", P, BF), ("C", 576, BF), ("CS", 576, BF),
-        ("tw32", 24, I32), ("ic", 48, I32), ("ti", 96, I32), ("i8", 6, I32), ("l8", 4, U16), ("KL1", NE[1] // 16, U16),
-        ("tw16", 24, U16), ("ms", P, F32), ("il", 24, U16), ("ul", 8, U16), ("LL", 26, U16), ("CB", 16, U16), ("BL", 24, U16), ("UL", 24, U16),
-        ("TL", 12, U16), ("RL", 12, U16), ("Z", 224, F32), ("NU", 192, F32),
-        ("cols", 8, F32), ("iotaR", 576, F32), ("J", 36, F32), ("KK", 24, F32), ("fe", 24, F32), ("opc", 52, F32),
-        ("UP", P + 16, F32), ("ht", P, F32), ("ysb", P, F32), ("SS", P, F32), ("GM", P, F32), ("SC", P, F32),
-        ("BX", 576, F32), ("M", 688, F32), ("HS", 688, F32), ("tf", 448, F32), ("sl", 24, F32),
-        ("VB", 208, F32), ("tbB", 24, F32), ("KA", 80, F32), ("TT2", 296, F32), ("TT3", NE[3], F32), ("KL2", NE[2] // 16, U16),
-        ("KS2", NE[2] // 16, U16), ("KS3", NE[3] // 16, U16),
-        ("over", 25 - SPLIT, F32), ("rest", 24 - SPLIT, F32), ("beyond", 24 * (24 - SPLIT), F32)):
+        ("zi", 516, BF), ("FP", 4 * P, BF), ("V", 4 * VW, BF), ("FQ", 2 * P, BF), ("E", 768, BF), ("tmp", 832, BF),
+        ("tb", 4 * P, BF), ("m16s", 16, BF), ("m16", P, BF), ("hold", P, BF), ("climb", P, BF), ("C", 576, BF),
+        ("CS", 576, BF), ("miss", 608, BF), ("AT", 608, F16), ("HS", 608, F16),
+        ("tw32", 48, I32), ("ic", 24, I32), ("i16", 24, I32), ("ti", 96, I32), ("W2", 48, F32), ("MT", 96, F32), ("TT", 96, F32),
+        ("ml", 6, U16), ("fl", 2, U16), ("il", 24, U16), ("ul", 8, U16), ("BL", 32, U16), ("UL", 24, U16), ("NX", 64, U16), ("PL", 12, U16),
+        ("PF", 36, F32), ("AD", 48, F32), ("cols", 12, F32), ("iotaR", 576, F32), ("J0", 38, F32), ("J", 38, F32),
+        ("opc", 52, F32), ("UP", P, F32), ("ht", P, F32), ("ysb", P, F32), ("SS", P, F32), ("GM", P, F32), ("SC", P, F32),
+        ("BX", 576, F32), ("tf", 448, F32)):
     _buf(_n, _c, _t)
 for _r in (1, 2, 3):
-    _h = LANES[_r] // 2
-    for _n, _c, _t in (("D0", NR[_r], BF), ("DS", NE[_r], BF), ("T", (SEGS[_r] + 2) * SEG[_r], F32), ("D", 28, F32),
-                       ("CL", B0[_r] + _h, U16), ("MN", NR[_r] // 16, U16), ("MX", NR[_r] // 16, U16)):
+    _w = LANES[_r]
+    for _n, _c, _t in (("D0", NR[_r], BF), ("TH", (_w + 2) * _w, BF), ("CL", _w + 1, U16), ("VB", 8 * _w + 16, F32),
+                       ("MN", NR[_r] // 16, U16), ("MX", NR[_r] // 16, U16), ("KS", NE[_r] // 16, U16), ("KL", NE[_r] // 16, U16)):
         _buf(_n + str(_r), _c, _t)
+    if _r > 1:
+        _buf("CM%d" % _r, _w + 1, U16)
+    if _r < 3:
+        _buf("LL%d" % _r, _w + 1, U16)
 for _i in range(8):
     _buf("p%d" % _i, 512, F32, "psum")
 
-NDMA = 44
-SEMAPHORES = (["vs", "ss", "ts", "gs", "loc", "ax0", "ax1", "ax2", "axs", "all1", "a2c", "a2s", "a3c", "a3s"]
+NDMA = 48
+SEMAPHORES = (["vs", "ss", "ts", "gs", "loc", "a3c", "a3s"] + ["a%d%s" % (r, k) for r in (1, 2) for k in ("c0", "c1", "c2", "s1", "s2", "l")]
               + ["d%d" % i for i in range(NDMA)])
 
 
@@ -150,12 +146,12 @@ def rank_program(g, core, T, topo):
         cnt[sem] = cnt.get(sem, 0) + 1
         after(q, sem, acc)
 
-    def dma(q, out, in_, add=False):
+    def dma(q, out, in_):
         acc = touches(q, [in_], [out], True)
         before(q, acc)
         sem = "d%d" % nd[0]
         nd[0] += 1
-        ENG[q].dma_start(ap(out), ap(in_), **({"accum_op": A.add} if add else {})).then_inc(T.sem[sem], 16)
+        ENG[q].dma_start(ap(out), ap(in_)).then_inc(T.sem[sem], 16)
         cnt[sem] = 16
         after(q, sem, acc)
 
@@ -185,7 +181,7 @@ def rank_program(g, core, T, topo):
         op("v", [d0, d1], [out], lambda: g.vector.tensor_tensor_scan(ap(out), ap(d0), ap(d1), first, o0, o1))
 
     def act(out, in_, func=AF.Copy, **kw):
-        op("s", [in_, kw.get("bias")], [out, kw.get("accum_out")],
+        op("s", [in_, kw.get("bias")], [out],
            lambda: g.scalar.activation(ap(out), ap(in_), func, **{k: ap(x) for k, x in kw.items()}))
 
     def quant(q, a, b, in_):
@@ -211,15 +207,20 @@ def rank_program(g, core, T, topo):
         else:
             ts(out, in_, scale, A.mult)
 
-    col = {k2: v("cols", i, i + 1) for i, k2 in enumerate(("i", "m0", "minus0", "rise", "before", "odd", "lane"))}
+    col = {k2: v("cols", i, i + 1) for i, k2 in enumerate(("i", "m0", "oct", "rise", 1, 2, 3))}
+    tower = v("i16", 0, 1)
 
     todo = []
 
-    width = [2]
+    def gap(n=2):
+        for chain in [c for c in todo if c][:n]:
+            chain.pop(0)()
 
-    def gap(n=None):
-        for _ in range(min(width[0] if n is None else n, len(todo))):
-            todo.pop(0)()
+    def finish(*chains):
+        while any(chains):
+            for chain in chains:
+                if chain:
+                    chain.pop(0)()
 
     def pair_lists(r):
         W, n = LANES[r], NR[r] // 16
@@ -233,426 +234,435 @@ def rank_program(g, core, T, topo):
                 lambda: ts(v("MX%d" % r), mx, 16.0, A.mult, 15.0, A.add),
                 lambda: ts(v("MN%d" % r), mn, 16.0, A.mult, 15.0, A.add)]
 
-    def key_lists(r):
-        W, L, m = LANES[r], SEG[r], NE[r] // 16
-        j, sg, sl, ps = v("J", 0, m), v("ti", 48, 48 + m), v("tf", 192, 192 + m), v("tf", 240, 240 + m)
-        return [lambda: ts(sg, j, 1.0 / L, A.mult, -(L - 1) / (2.0 * L), A.add),
-                lambda: ts(sl, sg, -float(L), A.mult),
-                lambda: tt(ps, j, sl, A.add),
-                lambda: vcopy(v("KL%d" % r), ps),
-                lambda: ts(v("KS%d" % r), ps, float(W), A.mult, W - 1.0, A.add)]
+    def lane_lists(r):
+        W, m = LANES[r], NE[r] // 16
+        j, sg, sl, ps, far = v("J", 0, m), v("ti", 48, 48 + m), v("tf", 192, 192 + m), v("tf", 240, 240 + m), v("tf", 288, 288 + m)
+        calls = [lambda: ts(sg, j, 1.0 / W, A.mult, -(W - 1) / (2.0 * W), A.add),
+                 lambda: ts(sl, sg, -float(W), A.mult),
+                 lambda: tt(ps, j, sl, A.add),
+                 lambda: ts(v("KS%d" % r), ps, float(W), A.mult, W - 1.0, A.add)]
+        if r == 1:
+            return calls + [lambda: vcopy(v("KL1"), ps)]
+        return calls + [lambda: ts(far, j, float(W * max(UPC[r], LOC[r])), A.is_ge, 16.0, A.mult),
+                        lambda: tt(far, far, ps, A.add),
+                        lambda: vcopy(v("KL%d" % r), far)]
 
-    def lists_by_eight():
-        rows = v("iotaR", 15, 96, 32)
-        return [lambda: ts(v("i8"), v("ic", 0, 6), 7, A.bitwise_and),
-                lambda: ts(col["odd"], v("ic", 0, 1), 8.0, A.is_ge, 16.0, A.mult),
-                lambda: vcopy(v("l8"), v("i8", 0, 4)),
-                lambda: ts(col["lane"], v("i8", 0, 1), 16.0, A.mult, 15.0, A.add),
-                lambda: ts(v("KS3"), v("i8"), 8.0, A.mult, 5.0, A.add),
-                lambda: ts(v("MX3"), rows, col["odd"], A.add, col["lane"], A.max),
-                lambda: ts(v("MN3"), rows, col["odd"], A.add, col["lane"], A.min)]
-
-    def offsets(r):
-        W, L, b0, t = LANES[r], SEG[r], B0[r], "T%d" % r
-        n, h = SEGS[r] + 2 - b0, W // 2
-        iota(v(t, 0, b0 * L), [[-1, b0], [-1, L]], W - 2)
-        iota(v(t, b0 * L), [[-1, n], [-1, L]], W - 2 - h)
-        iota(v(t, W - 1, b0 * L, L), [[-1, b0]], 1)
-        iota(v(t, b0 * L + W - 1, None, L), [[-1, n]], 1 - h)
-
-    def later_ranks(r):
-        x = v("T%d" % r, SEG[r], B0[r] * SEG[r])
-        act(x, x, AF.Identity, bias=col["m0"])
-        for c in range(LANES[r] + 1, SEG[r]):
-            iota(v("T%d" % r, c, None, SEG[r]), [[0, SEGS[r] + 2]], 64)
-
-    def spread_tables(r):
-        L, a = SEG[r], B0[r] * SEG[r]
-        if r == 2:
-            act(v("TT2", 0, 192), by(v("KA", K0[2], K0[2] + L), v("KL2", 0, 12)))
-            act(v("TT2", a, a + 112), by(v("KA", TOP[2], TOP[2] + L), v("KL2", 0, 7)))
-        else:
-            act(v("TT3", 0, a), by(v("KA", K0[3], K0[3] + L), v("l8")))
-            act(v("TT3", a), by(v("KA", TOP[3], TOP[3] + L), v("l8", 0, 2)))
-        dma("g", v("TT%d" % r, 0, NE[r]), v("T%d" % r, 0, NE[r]), True)
-
-    def ends(r):
-        W, L, ns = LANES[r], SEG[r], SEGS[r]
-        y, u = v("T%d" % r, W, ns * L, L), v("tf", 416, 416 + ns)
-        return [lambda: ts(u, y, -0.5, A.mult, -W - 1.5, A.add), lambda: tt(y, y, u, A.mult)]
-
-    def threshold_rows(r, part):
-        L, b0, t = LANES[r] + 1, B0[r], "T%d" % r
-        if part == 0:
-            iota(v(t, 0, b0 * L), [[1, b0], [0, L]], 0)
-        else:
-            iota(v(t, b0 * L), [[1, SEGS[r] + 2 - b0], [0, L]], LANES[r] // 2)
+    def thresholds(r, upper):
+        W, t = LANES[r], "TH%d" % r
+        h = W // 2
+        s0, first = (UPC[r], h) if upper else (LOC[r], 0)
+        n = W + 2 - s0 if s0 else max(UPC[r], LOC[r])
+        iota(v(t, s0 * W, (s0 + n) * W), [[-1, n], [-1, W]], W - 2 - first)
+        iota(v(t, s0 * W + W - 1, (s0 + n) * W, W), [[-1, n]], 1 - first)
 
     def tower0(r):
-        x = v("T%d" % r, 0, B0[r] * (LANES[r] + 1))
-        act(x, x, AF.Relu, bias=col["minus0"])
-
-    def cancels(r):
-        W = LANES[r]
-        L, t, ns = W + 1, "T%d" % r, SEGS[r]
-        u = v("tf", 417, 416 + ns)
-        return [lambda: ts(u, v(t, L, ns * L, L), 0.5, A.mult, -(W - 0.5), A.add),
-                lambda: tt(v(t, L + W, ns * L, L), v(t, L, ns * L, L), u, A.mult),
-                lambda: ts(v(t, W, W + 1), col["minus0"], P / 1024.0, A.mult)]
+        W, t = LANES[r], "TH%d" % r
+        a = LOC[r] * W
+        act(v(t, a + W, a + W * (W // 2 + 1)), v(t, a + W, a + W * (W // 2 + 1)), AF.Identity, bias=col["m0"])
+        act(v(t, a, a + W), v(t, a, a + W), AF.Identity, bias=col[r])
 
     def signs(r):
-        W, R, d = LANES[r], ROW[r], "D0%d" % r
+        W, d = LANES[r], "D0%d" % r
         if r > 1:
             iota(v(d), [[0, NR[r]]], 1)
-        iota(v(d, 0, None, R), [[0, W]], 0)
-        iota(v(d, 1, (R + 1) * (W - 2) + 2, R + 1), [[0, W - 1]], -1)
-        iota(v(d, (R + 1) * (W - 1), (R + 1) * (W - 1) + 1), [[0, 1]], -1)
+        iota(v(d, 0, W * W, W), [[0, W]], 0)
+        iota(v(d, 1, (W + 1) * (W - 2) + 2, W + 1), [[0, W - 1]], -1)
+        iota(v(d, W * W - 1, W * W), [[0, 1]], -1)
 
-    def resets(r):
-        L = SEG[r]
-        iota(v("DS%d" % r), [[0, NE[r]]], 1)
-        iota(v("DS%d" % r, 0, SEGS[r] * L, L), [[0, SEGS[r]]], 0)
+    def slots(r):
+        n, k = 8 * LANES[r], (1, 1, 3)[r - 1]
+        iota(v("VB%d" % r, 0, 1), [[0, 1]], P + k // 3 * 3)
+        iota(v("VB%d" % r, n + 1), [[k, 15]], P + k + k // 3 * 3)
+        if r == 3:
+            iota(v("VB3", n + 15), [[0, 1]], P)
+
+    def table(r, kind):
+        if r == 1:
+            return v("BL", 0, 24)
+        a = 32 * (r - 2) + (16 if (kind == "tops") == (UPC[r] > LOC[r]) else 0)
+        return v("NX", a, a + LANES[r])
+
+    def steps(r):
+        W = LANES[r]
+        if r == 1:
+            return [lambda: vcopy(v("PF", 0, W), table(1, "bases")), lambda: tt(v("AD", 0, W), v("PF", 0, W), v("PF", 1, W + 1), A.subtract)]
+        return [lambda: vcopy(v("PF", 0, 32), v("NX", 32 * (r - 2), 32 * (r - 1))),
+                lambda: tt(v("AD", 0, 32), v("PF", 0, 32), v("PF", 1, 33), A.subtract),
+                lambda: tt(v("AD", 32, 32 + W), v("PF", 0, W), v("PF", 1, W + 1), A.subtract)]
+
+    def spread(r):
+        act(v("AT", 0, NE[r]), by(v("AD", 0, 32), v("KL%d" % r)))
+        if r > 1:
+            act(v("AT", SECOND, SECOND + NE[r]), by(v("AD", 16, 48), v("KL%d" % r)))
 
     def plane(t, a=0, b=P):
         return v("V", VW * t + a, VW * t + b)
 
-    def unpack(q, a, bank):
-        for b in range(4):
-            mm(bank + b, "EC", 128 * b, q, a, P)
+    def arrived(t, a=0, b=P):
+        return v("FP", P * t + a, P * t + b)
 
-    def own_plane(t):
+    def unpack(q, bank, a=0, b=P):
+        for t in range(4):
+            mm(bank + t, "EC", 128 * t, q, a, b - a)
+
+    def unpack_arrived(r, a, b):
+        unpack("LB%d" % r, 4, a, b)
+        for t in range(4):
+            act(arrived(t, a, b), v("p%d" % (4 + t), 0, b - a))
+
+    def own_plane(r, t):
         act(plane(t), v("p%d" % t, 0, P))
         if t < 2:
-            dma("y", v("FQ", P * t, P * t + (P, OWN)[t]), plane(t, 0, (P, OWN)[t]))
+            a = (0, OWN[r])[t]
+            dma("y", v("FQ", P * t, P * t + P - a), plane(t, a, P))
 
-    def gather_scores(r):
-        n = 16 * LANES[r]
-        tt(v("GM", 0, n), by(v("SS"), v("BL", 0, LANES[r])), v("m16", 0, n), A.mult)
-        gap()
-        scan(v("SC", 0, n), v("hold", 0, n), v("GM", 0, n), A.mult, A.add)
+    def quantise_and_score(r, c):
+        q, a, b = "QX%d" % r, 128 * c, 128 * c + 128
+        quant(q, a, b, v(XB[r], 4 * a, 4 * b))
+        if r < 3:
+            send(raw(v("LB%dc" % r, a, b)), raw(v(q + "c", a, b)), "a%dc%d" % (r, c))
+            if c > 0:
+                a0 = (0, 0, a)[c]
+                send(v("LB%ds" % r, a0, b), v(q + "s", a0, b), "a%ds%d" % (r, c))
+        if r > 1:
+            mm(4 + c, "UR" if r < 4 else "QV", 0, q, a, 128)
+
+    def take_scores(q, c, a=0, b=128):
+        evac(q, v("SS", 128 * c + a, 128 * c + b), v("p%d" % (4 + c), a, b))
+
+    def gather_scores(r, cuts):
+        runs = list(zip(cuts, cuts[1:]))
+        base = table(r, "bases")
+        for a, b in runs:
+            tt(v("GM", a, b), by(v("SS"), v(base["n"], base["a"] + a // 16, base["a"] + b // 16)), v("m16", a, b), A.mult)
+        gap(2 - len(runs))
+        for a, b in runs:
+            scan(v("SC", a, b), v("hold", a, b), v("GM", a, b), A.mult, A.add)
 
     def pairs(r, q, a, b):
-        src = by(v("SC"), v("MX%d" % r, a // 16, b // 16))
-        (act if q == "s" else vcopy)(v("BX", a, b), src)
+        (act if q == "s" else vcopy)(v("BX", a, b), by(v("SC"), v("MX%d" % r, a // 16, b // 16)))
 
     def compare(r, a, b):
         tt(v("C", a, b), by(v("SC"), v("MN%d" % r, a // 16, b // 16)), v("BX", a, b), A.is_ge)
 
-    def rank_sums(r):
-        scan(v("CS", 0, NR[r]), v("D0%d" % r), v("C", 0, NR[r]), A.mult, A.add)
-        gap()
+    def rank_sums(r, a, b):
+        scan(v("CS", a, b), v("D0%d" % r, a, b), v("C", a, b), A.mult, A.add)
 
-    def extract(r, between):
-        L, n, ns = SEG[r], NE[r], SEGS[r]
-        if r == 1:
-            tt(v("M", 0, n), by(v("KA", 0, L), v("KL1")), v("T1", 0, n), A.min)
-        else:
-            tt(v("M", 0, n), by(v("CS"), v("KS%d" % r)), v("TT%d" % r, 0, n), A.max)
-        gap()
-        scan(v("HS", 0, n), v("DS%d" % r), v("M", 0, n), A.mult, A.add)
-        between()
-        later, earlier = v("HS", 2 * L - 1, ns * L, L), v("HS", L - 1, (ns - 1) * L, L)
-        tt(v("D%d" % r, 0, ns - 1), *((later, earlier) if r == 1 else (earlier, later)), A.subtract)
+    def misses(r, a, b, at=0):
+        tt(v("miss", at + a, at + b), by(v("CS"), v("KS%d" % r, a // 16, b // 16)), v("TH%d" % r, a, b), A.not_equal)
 
-    def first_list(r):
-        ts(v("CL%d" % r), v("D%d" % r, 0, B0[r] + LANES[r] // 2), 1024.0, A.mult, P - 1.0, A.min)
+    def places(r, s0, s1, at=0):
+        a, b = at + s0 * LANES[r], at + s1 * LANES[r]
+        scan(v("HS", a, b), v("miss", a, b), v("AT", a, b), A.mult, A.add)
+
+    def listed(name, r, s0, s1, at=0):
+        W = LANES[r]
+        vcopy(v(name + str(r), s0, s1), v("HS", at + s0 * W + W - 1, at + s1 * W, W))
+
+    def upper(name, r):
+        return v(name + str(r), UPC[r], UPC[r] + LANES[r] // 2)
+
+    def lower(name, r):
+        return v(name + str(r), LOC[r], LOC[r] + LANES[r] // 2 + 1)
 
     def next_tables(r):
-        h, b0, d, nb, nt = LANES[r] // 2, B0[r], "D%d" % r, K0[r + 1], TOP[r + 1]
-        dma("y", v("KA", nb, nb + h), v(d, 0, h))
-        dma("y", v("KA", nt, nt + h, rows=slice(1, 128)), v(d, b0, b0 + h, rows=slice(0, 127)))
-        dma("y", v("KA", nb, nb + h, rows=slice(0, 128, 16)), v(d, 1, h + 1, rows=slice(0, 128, 16)))
-        dma("y", v("KA", nt, nt + h, rows=slice(0, 128, 16)), v(d, b0, b0 + h, rows=slice(15, 128, 16)))
+        h, cl = LANES[r] // 2, "CL%d" % r
+        nb, nt, lo, up = table(r + 1, "bases")["a"], table(r + 1, "tops")["a"], LOC[r], UPC[r]
+        dma("y", v("NX", nb, nb + h), v(cl, lo, lo + h))
+        dma("y", v("NX", nt, nt + h, rows=slice(1, 128)), v(cl, up, up + h, rows=slice(0, 127)))
+        dma("y", v("NX", nb, nb + h, rows=slice(0, 128, 16)), v(cl, lo + 1, lo + h + 1, rows=slice(0, 128, 16)))
+        dma("y", v("NX", nt, nt + h, rows=slice(0, 128, 16)), v(cl, up, up + h, rows=slice(15, 128, 16)))
 
-    def partner_list(r):
-        W = LANES[r]
-        return [lambda: ts(v("TL", 0, W), v("KA", TOP[r], TOP[r] + W), 1024.0, A.mult),
-                lambda: tt(v("sl", 0, W), v("KK", 24 - W), v("CS", W - 1, NR[r], ROW[r]), A.subtract),
-                lambda: ts(v("RL", 0, W), v("sl", 0, W), 16.0, A.mult, col["before"], A.add)]
+    def upper_bases(r, copy=act):
+        copy(v("VB%d" % r, 1, 8 * LANES[r] + 1), by(v("iotaR", 0, P), upper("CL" if r == 1 else "CM", r)))
 
-    def upper_bases(r):
-        W = LANES[r]
-        c0 = W // 4 * 2
-        vcopy(v("Z", 96 - 16 * (W - c0), 112), by(v("iotaR", 0, P), v("CL%d" % r, c0, W + 1)))
+    def new_tops(r, values):
+        vcopy(by(v("UP"), upper("CL", r)), values)
 
-    def successors(r):
-        W = LANES[r]
-        act(v("Z", 97, 112), v("Z", 209))
-        act(v("NU", 0, 16 * W), by(v("Z", 96 - 8 * W, 208), v("RL", 0, W)))
-
-    def scatter_tops(r, values):
-        h, b0 = LANES[r] // 2, B0[r]
-        vcopy(by(v("UP"), v("CL%d" % r, b0, b0 + h)), values)
+    def links(r):
+        vcopy(by(v("UP"), lower("CL" if r == 1 else "CM", r)), v("VB%d" % r))
 
     def blend_list():
-        scan(v("ht"), v("climb"), v("UP", 0, P), A.add, A.max)
+        scan(v("ht"), v("climb"), v("UP"), A.add, A.max)
         gap()
         ts(v("UL"), v("ht", 15, P, 16), col["rise"], A.subtract)
 
-    def bases_of_e(r, win, lst, planes, copy=act):
-        n = 8 * LANES[r] + 16
-        for t in planes:
-            copy(v("tmp", n * t, n * t + n), by(win(t), v(lst, 0, n // 16)))
-
-    def make_e(r, win, lst):
-        h, b0 = LANES[r] // 2, B0[r]
-        n = 16 * (h + 1)
+    def make_e(r, win, lst, between):
+        n = 8 * LANES[r]
         for t in range(4):
-            tt(v("E", t, 64 * h, 4), by(win(t), v(lst, b0, b0 + h)), v("tmp", n * t + 1, n * t + 1 + 16 * h), A.add)
-        gap()
+            (vcopy if t == 0 else act)(v("tmp", (n + 16) * t, (n + 16) * (t + 1)), by(win(t), lower(lst, r)))
+        between()
+        for t in range(4):
+            a = (n + 16) * t + 1
+            tt(v("E", t, 4 * n, 4), by(win(t), upper(lst, r)), v("tmp", a, a + n), A.add)
 
-    def layer(q, a, n):
-        for b in (1, 0, 2, 3):
+    def layer(q, a, n, order=(1, 0, 2, 3)):
+        for b in order:
             mm(4 + b, "WW", 128 * b, q, a, n)
 
-    def take_h(r, off):
+    def blend(r, off):
         n = 8 * LANES[r]
-        for q, b in (("sv"[r > 1], 1), ("v", 0), ("v", 2), ("v", 3)):
+
+        def take_h(q, b):
             evac(q, plane(b, P, P + n), v("p%d" % (4 + b), off, off + n), 0.015625)
 
-    def near(r, t, a, b):
-        return by(plane(t, 0, P + 8 * LANES[r]), v("UL", a // 16, b // 16))
+        def near(t, a, b):
+            return by(plane(t, 0, P + n), v("UL", a // 16, b // 16))
 
-    def fetch(r, t, a, b):
-        act(v("tb", P * t + a, P * t + b), near(r, t, a, b))
+        def x(t, a, b):
+            return v(XB[r + 1], 4 * a + t, 4 * b, 4)
 
-    def add_fetched(r, t, a, b):
-        tt(v(XB[r + 1], 4 * a + t, 4 * b, 4), v("tb", P * t + a, P * t + b), v("p%d" % t, a, b), A.add)
+        def fetch(t, a, b):
+            act(v("tb", P * t + a, P * t + b), near(t, a, b))
 
-    def add_near(r, t, a, b):
-        tt(v(XB[r + 1], 4 * a + t, 4 * b, 4), near(r, t, a, b), v("FQ", P * t + a, P * t + b), A.add)
+        def add(t, a, b):
+            tt(x(t, a, b), v("tb", P * t + a, P * t + b), v("p%d" % t, a, b), A.add)
 
-    def blend(r):
-        take_h(r, 0)
-        own = OWN // (2 if r == 1 else 1)
-        parts = ((1, own, P), (2, 0, P), (3, 0, 256), (3, 256, P))
-        for t, a, b in parts:
-            fetch(r, t, a, b)
-        add_near(r, 0, 0, P)
-        for t, a, b in parts:
-            add_fetched(r, t, a, b)
-            if t == 1:
-                add_near(r, 1, 0, own)
+        own = OWN[r]
+        parts = [(1, 0, own), (2, 0, 256), (3, 0, 256), (2, 256, P), (3, 256, P)]
+        if r < 3:
+            for q, t in (("s", 1), ("v", 0), ("v", 2), ("v", 3)):
+                take_h(q, t)
+        else:
+            parts = [(1, 0, own), (2, 0, P), (3, 0, 256), (3, 256, P)]
+        for part in parts:
+            fetch(*part)
+        tt(x(0, 0, P), near(0, 0, P), v("FQ", 0, P), A.add)
+        tt(x(1, own, P), near(1, own, P), v("FQ", P, 2 * P - own), A.add)
+        for part in parts:
+            add(*part)
+        if r < 3:
+            for c in range(3):
+                quantise_and_score(r + 1, c)
 
-    def arrived(t):
-        return v("FP", P * t, P * t + P)
+    def mend(off):
+        n = 8 * LANES[3]
+        for t in range(4):
+            evac("s", v("tmp", n * t, n * t + n), v("p%d" % (4 + t), off, off + n), 0.015625)
+            tt(v("E", n * t, n * t + n), by(plane(t), upper("CL", 3)), v("tmp", n * t, n * t + n), A.add)
+        vcopy(by(v(XB[4]), v("PL")), v("E", 0, 4 * n))
 
-    dma("y", v("tw32"), T.tw[:, :])
-    dma("s", v("ub"), T.u[:, :])
+    dma("y", v("ub"), T.u[:, :])
+    dma("s", v("tw32", 0, 24), T.tw[:, :])
+    dma("s", v("tw32", 24, 48, rows=slice(0, 120)), T.tw[8:128, :])
     for c in range(3):
-        dma("ysy"[c], v("X1", 512 * c, 512 * c + 512), T.x[:, 512 * c:512 * c + 512])
+        dma("yys"[c], v("X1", 512 * c, 512 * c + 512), T.x[:, 512 * c:512 * c + 512])
 
-    iota(v("ic"), [[14, 2], [0, 24]], 0, 1)
-    iota(v("J"), [[16, 36]], 0)
+    iota(v("ic"), [[0, 24]], 0, 1)
+    iota(v("J0"), [[16, 38]], 0)
     memset(v("half"), 0.5)
     op("g", [v("half")], [v("zi")], lambda: g.affine_select(T.zi[:], T.half[:, 0:516], [[1, 516]], A.is_equal, 0.0, -3, -4))
-    threshold_rows(1, 0)
-    ts(v("ic"), v("ic"), 15, A.bitwise_and)
-    scan(v("iotaR", 0, P), v("half", 0, P), v("half", 0, P), A.add, A.add, -1.0)
-    ts(col["i"], v("ic", 0, 1), 1.0, A.mult)
-    vcopy(v("ul"), v("J", 0, 8))
-    vcopy(v("il"), v("ic", 0, 24))
-    vcopy(v("tw16"), v("tw32"))
-    ts(v("m16s"), v("iotaR", 0, 16), col["i"], A.is_equal)
-    ts(v("J"), v("J"), col["i"], A.add)
-    act(v("ms"), by(v("iotaR", 0, P), v("tw16")))
-    dma("y", v("fe"), v("ms", rows=slice(0, 128, 16)))
-    p1, k1 = pair_lists(1), key_lists(1)
-    todo += [lambda: ts(col["minus0"], v("ic", 0, 1), 0.0, A.is_equal, -1.0, A.mult), k1[0],
-             p1[0], k1[1], lambda: memset(v("KA"), 0.0),
-             p1[1], k1[2], p1[2], k1[3],
-             lambda: ts(v("sl"), v("fe"), 1.0 / 1024, A.mult)] + p1[3:]
-    gap(2)
-    quant("QU", 0, 128, v("ub"))
-    gap(3)
-    for c in range(3):
-        a, b = 128 * c, 128 * c + 128
-        quant("QX1", a, b, v("X1", 4 * a, 4 * b))
-        send(raw(v("LBc", LAND[1] + a, LAND[1] + b)), raw(v("QX1c", a, b)), "ax%d" % c)
-        if c == 0:
-            vcopy(words(v("URc")), by(words(v("QUc")), v("ul")))
-            act(v("URs"), by(v("QUs"), v("ul")))
-        if c == 1:
-            gap(2)
-        mm(4 + c, "UR", 0, "QX1", a, 128)
-    send(v("LBs", LAND[1], LAND[1] + P), v("QX1s"), "axs")
+    thresholds(1, False)
+    ts(v("i16"), v("ic"), 15, A.bitwise_and)
+    ts(v("ti", 0, 1), v("ic", 0, 1), 23, A.bitwise_and)
+    ts(v("ti", 2, 3), v("ic", 0, 1), 8, A.bitwise_and)
+    memset(v("W2"), 0.0)
+    vcopy(v("ul"), v("J0", 0, 8))
+    ts(col["i"], tower, 1.0, A.mult)
+    ts(col["oct"], v("ti", 2, 3), 4.0, A.mult)
+    vcopy(v("il"), v("i16", 0, 24))
+    for o in range(3):
+        ts(v("ml", 2 * o, 2 * o + 2), v("i16", 0, 2), 3.0, A.mult, float(o), A.add)
+    ts(v("J"), v("J0"), col["i"], A.add)
+    ts(v("m16s"), v("J0", 0, 16), 1.0 / 16, A.mult, col["i"], A.is_equal)
+    ts(v("fl", 0, 1), v("ti", 0, 1), col["oct"], A.add)
+    ts(v("fl", 1, 2), v("ti", 0, 1), 64.0, A.add)
     act(v("m16"), by(v("m16s"), v("il")))
+    p1, k1 = pair_lists(1), lane_lists(1)
+    c1 = [lambda: memset(v("PF"), 0.0), lambda: memset(v("AD"), 0.0),
+          lambda: ts(col["m0"], tower, 0.0, A.is_equal), lambda: ts(col[1], tower, 0.0, A.is_equal, -12.0, A.mult)]
+    unpackers = [lambda b=b: quant("EC", 128 * b, 128 * b + 128, v("zi", 3 - b, 515 - b)) for b in range(4)]
+    todo += [k1, p1, c1]
+    gap(3)
 
-    iota(v("KK"), [[-1, 24]], 22)
-    iota(v("KK", 23), [[0, 1]], 1)
-    threshold_rows(1, 1)
-    for c in range(3):
-        gap((2, 0, 0)[c])
-        evac("v", v("SS", 128 * c, 128 * c + 128), v("p%d" % (4 + c), 0, 128))
-        if c == 1:
-            vcopy(v("BL"), v("fe"))
-    gap(2)
+    vcopy(v("W2", 0, 48, 2), v("tw32", 0, 24))
+    vcopy(v("W2", 1, 48, 2, rows=slice(0, 120)), v("tw32", 24, 48, rows=slice(0, 120)))
+    gap(3)
+    quant("QU", 0, 128, v("ub"))
+    act(v("MT"), by(v("W2"), v("ml")))
+    gap(3)
+    vcopy(words(v("URc")), by(words(v("QUc")), v("ul")))
+    act(v("URs"), by(v("QUs"), v("ul")))
+    op("v", [v("MT")], [v("TT")], lambda: g.vector.transpose(T.TT[:, :], T.MT[:, :]))
+    gap(3)
+    quantise_and_score(1, 0)
+    vcopy(v("BL"), by(v("TT"), v("fl")))
     act(v("hold"), v("m16"), AF.Identity, scale=-1.0, bias=1.0)
-    tower0(1)
     act(v("D01"), v("half"), scale=2.0)
+    gap(3)
+    quantise_and_score(1, 1)
+    todo.insert(0, steps(1))
+    gap(3)
+    unpackers[0]()
+    gap(3)
+    quantise_and_score(1, 2)
+    for c in range(3):
+        mm(4 + c, "UR", 0, "QX1", 128 * c, 128)
+    take_scores("v", 0)
+    take_scores("v", 1)
+    finish(*todo)
+    unpackers[1]()
+    take_scores("v", 2)
+    unpackers[2]()
+    spread(1)
     signs(1)
-    iota(v("rest"), [[-1, 24 - SPLIT]], 23 - SPLIT)
-    resets(1)
-    iota(v("iotaR", P), [[1, 576 - P]], P)
-    iota(v("VB", 0, 1), [[0, 1]], 0)
-    iota(v("VB", 193), [[1, 15]], P + 1)
-    gather_scores(1)
-    thirds = ((0, 192), (192, 384), (384, 576))
-    for a, b in thirds:
-        pairs(1, "s", a, b)
-    gap(1)
-    for b in range(4):
-        quant("EC", 128 * b, 128 * b + 128, v("zi", 3 - b, 515 - b))
-    unpack("QX1", 0, 0)
-    own_plane(0)
-    own_plane(1)
+    iota(v("iotaR"), [[1, 576]], 0)
+    slots(1)
+
+    gather_scores(1, (0, 256, 384))
+    unpackers[3]()
+    unpack("QX1", 0)
+    pairs(1, "s", 0, 96)
+    pairs(1, "s", 288, 576)
+    pairs(1, "v", 96, 288)
+    act(v("TH1", 0, 288), v("TH1", 288, 576), AF.Identity, bias=-12.0)
+    tower0(1)
+    own_plane(1, 0)
+    own_plane(1, 1)
     dma("y", raw(v("WWc")), T.wc[:, :])
     dma("y", v("WWs"), T.ws[:, :])
-    c1 = cancels(1)
-    k2 = key_lists(2)
-    climb = [lambda a=a: ts(v("climb", a, a + 128), v("m16", a, a + 128), -33792.0, A.mult, 1024.0, A.add) for a in (0, 128, 256)]
-    todo += [c1[0], lambda: tt(v("tbB"), v("sl"), v("KK"), A.add),
-             c1[1], c1[2],
-             k2[0], lambda: memset(v("over", 24 - SPLIT), 0.0),
-             k2[1], climb[0],
-             k2[2], lambda: ts(col["m0"], v("ic", 0, 1), 0.0, A.is_equal),
-             climb[1],
-             k2[3], climb[2]]
-    for a, b in thirds:
-        compare(1, a, b)
-    gap()
-    rank_sums(1)
-    tt(v("KA", 0, 24), v("tbB"), v("CS", 23, 576, 24), A.subtract)
-    gap()
-    for c in range(24 - SPLIT):
-        act(v("beyond", 24 * c, 24 * c + 24), v("KA", 0, 24), AF.Relu, bias=-float(SPLIT + c), accum_out=v("over", c, c + 1))
-    extract(1, lambda: tt(v("sl", 0, 24 - SPLIT), v("over", 0, 24 - SPLIT), v("rest"), A.subtract))
-    tt(v("D1", SEGS[1] - 1, 26), v("sl", 0, 24 - SPLIT), v("over", 1), A.subtract)
-    gap()
-    first_list(1)
-    send(v("LL"), v("CL1"), "all1")
+    climb = [lambda a=a: ts(v("climb", a, a + 192), v("m16", a, a + 192), -33792.0, A.mult, 1024.0, A.add) for a in (0, 192)]
+    p2, k2 = pair_lists(2), lane_lists(2)
+    c2 = climb + [lambda: memset(v("NX"), 0), lambda: ts(col["rise"], tower, -1024.0, A.mult, 15360.0, A.add),
+                  lambda: ts(col[2], tower, 0.0, A.is_equal, -6.0, A.mult), lambda: ts(col[3], tower, 0.0, A.is_equal, -3.0, A.mult)]
+    todo += [c2, k2, p2]
+    compare(1, 0, 96)
+    compare(1, 96, 288)
+    compare(1, 288, 576)
+    rank_sums(1, 0, 288)
+    rank_sums(1, 288, 576)
+    gap(2)
+    misses(1, 0, 288)
+    misses(1, 288, 608)
+    places(1, 0, 12)
+    places(1, 12, 25)
+    listed("CL", 1, 0, 12)
+    gap(2)
+    listed("CL", 1, 12, 25)
+    send(v("LL1"), v("CL1"), "a1l")
 
-    offsets(2)
     dma("g", v("vb"), T.v[:, :])
-    unpack("LB", LAND[1], 4)
-    for t in range(4):
-        act(arrived(t), v("p%d" % (4 + t), 0, P))
-        if t == 1:
-            act(v("VB", 1, 193), by(v("iotaR", 0, P), v("CL1", 14, 26)))
-    ts(v("CB", 0, 14), v("D1", 0, 14), 1024.0, A.mult)
-    gap(1)
-    scatter_tops(1, v("iotaR", P, P + 192))
-    gap()
-    vcopy(by(v("UP"), v("CB", 0, 13)), v("VB"))
-    bases_of_e(1, arrived, "LL", range(4))
-    before("y", touches("y", [v("LL")], [], False))
+    for r in (2, 3):
+        thresholds(r, False)
+        thresholds(r, True)
+        signs(r)
+        slots(r)
+    iota(v("opc", 0, 48), [[1, 3], [3, 16]], P + 3)
+    iota(v("opc", 48, 51), [[1, 3]], P)
+    unpack_arrived(1, 0, 256)
+    upper_bases(1)
+    unpack_arrived(1, 256, P)
+    own_plane(1, 2)
+    new_tops(1, v("iotaR", P, P + 192))
+    gap(3)
+    links(1)
+    gap(3)
+    finish(c2)
+    before("y", touches("y", [v("LL1")], [], False))
     next_tables(1)
-    later_ranks(2)
-    signs(2)
-    resets(2)
-    own_plane(2)
-    own_plane(3)
-    e2 = ends(2)
-    p2 = pair_lists(2)
-    ts(col["rise"], v("ic", 0, 1), -1024.0, A.mult, 15360.0, A.add)
-    todo += [e2[0], p2[0], e2[1], p2[1], p2[2], k2[4]] + p2[3:] + [lambda: ts(col["before"], v("ic", 24, 25), 1.0, A.add)]
-    make_e(1, arrived, "LL")
+    make_e(1, arrived, "LL", lambda: gap(3))
+    own_plane(1, 3)
+    tower0(2)
+    gap(3)
     quant("QE1", 0, 192, v("E"))
     layer("QE1", 0, 192)
     blend_list()
-    blend(1)
-    spread_tables(2)
-    iota(v("Z", 112, 208), [[1, 96]], P + 17)
-    iota(v("Z", 209, 223), [[1, 14]], P + 2)
-    iota(v("Z", 223), [[0, 1]], P)
-    iota(v("Z", 112, 208, 16), [[16, 6]], P + 1)
-    iota(v("Z", 127, 208, 16), [[16, 6]], P + 16)
-    offsets(3)
-    signs(3)
-    resets(3)
-    iota(v("opc", 0, 48), [[1, 3], [3, 16]], P + 3)
-    iota(v("opc", 48, 51), [[1, 3]], P)
+    gap(2)
+    blend(1, 0)
 
     for r in (2, 3):
         W = LANES[r]
-        h, b0 = W // 2, B0[r]
-        n, q = 16 * h, "QX%d" % r
+        n = 8 * W
+        unpack("QX%d" % r, 0)
+        todo.insert(0, steps(r))
         for c in range(3):
-            quant(q, 128 * c, 128 * c + 128, v(XB[r], 512 * c, 512 * c + 512))
-            mm(4 + c, "UR", 0, q, 128 * c, 128)
-        unpack(q, 0, 0)
-        ts(v("BL", 0, W), v("KA", K0[r], K0[r] + W), 1024.0, A.mult)
-        gap(2)
-        for c in range(3):
-            evac("svv"[c], v("SS", 128 * c, 128 * c + 128), v("p%d" % (4 + c), 0, 128))
+            gap(1)
+            take_scores("v", c)
+        finish(*todo)
+        spread(r)
         for t in range(4):
-            own_plane(t)
-        tops, ranks, partners = partner_list(r)
-        todo += [tops]
+            own_plane(r, t)
         if r == 2:
-            later_ranks(3)
-            todo += lists_by_eight() + ends(3)
-        else:
-            todo += [lambda: quant("QV", 0, 128, v("vb")), lambda: vcopy(v("opc", 15, 48, 16), v("opc", 48, 51))]
-        gap()
-        gather_scores(r)
-        width[0] = 1
-        gap()
-        pairs(r, "v", 0, NR[r])
-        gap()
-        compare(r, 0, NR[r])
-        gap()
-        rank_sums(r)
-        todo.insert(0, ranks)
-        extract(r, partners)
-        gap()
-        first_list(r)
-        bases_of_e(r, plane, "CL%d" % r, range(3))
-        gap()
-        upper_bases(r)
-        bases_of_e(r, plane, "CL%d" % r, [3], vcopy)
-        successors(r)
-        make_e(r, plane, "CL%d" % r)
-        quant("QE%d" % r, 0, 128, v("E", 0, 512))
-        send(raw(v("LBc", LAND[r], LAND[r] + n)), raw(v("QE%dc" % r, 0, n)), "a%dc" % r)
-        send(v("LBs", LAND[r], LAND[r] + n), v("QE%ds" % r, 0, n), "a%ds" % r)
-        if r == 2:
+            tower0(3)
+            unpack_arrived(2, 0, 256)
+            unpack_arrived(2, 256, P)
+            todo += [lane_lists(3), pair_lists(3)]
+            gather_scores(2, (0, 128, 192))
+            gap(2)
+            pairs(2, "v", 0, 96)
+            pairs(2, "v", 96, 144)
+            gap(1)
+            compare(2, 0, 96)
+            compare(2, 96, 144)
+            gap(3)
+            rank_sums(2, 0, 144)
+            gap(3)
+            misses(2, 0, 160)
+            misses(2, 0, 96, SECOND)
+            places(2, 0, 13)
+            misses(2, 96, 160, SECOND)
+            listed("CL", 2, 0, 13)
+            send(v("LL2"), v("CL2"), "a2l")
+            gap(1)
+            places(2, 0, 13, SECOND)
+            gap(3)
+            listed("CM", 2, 0, 13, SECOND)
+            new_tops(2, v("iotaR", P, P + n))
+            upper_bases(2, vcopy)
+            gap(2)
+            links(2)
+            finish(*todo)
+            before("y", touches("y", [v("LL2")], [], False))
             next_tables(2)
-        vcopy(by(v("UP"), v("TL", 0, W)), v("NU", 0, 16 * W))
-        gap(2)
-        blend_list()
-        gap(99)
-        if r == 2:
-            spread_tables(3)
-        if r == 3:
-            scatter_tops(3, v("opc", 0, 48))
-            dma("y", T.op[:, :], v("UP", 0, P, rows=slice(0, 128, 16)))
-        first = min(LAND[r], 528 - 128)
-        layer("LB", first, 128)
-        if r == 2:
-            blend(2)
+            make_e(2, arrived, "LL", gap)
+            quant("QE2", 0, 128, v("E", 0, 512))
+            layer("QE2", 0, 128)
+            blend_list()
+            blend(2, 0)
+        else:
+            todo += [[lambda: quant("QV", 0, 128, v("vb")), lambda: vcopy(v("opc", 15, 48, 16), v("opc", 48, 51))]]
+            gap(1)
+            gather_scores(3, (0, 96))
+            pairs(3, "v", 0, 48)
+            compare(3, 0, 48)
+            rank_sums(3, 0, 36)
+            misses(3, 0, 48)
+            misses(3, 0, 48, SECOND)
+            places(3, 0, 7)
+            places(3, 0, 7, SECOND)
+            listed("CL", 3, 0, 7)
+            listed("CM", 3, 0, 7, SECOND)
+            make_e(3, plane, "CL", lambda: (new_tops(3, v("opc", 0, n)), upper_bases(3)))
+            links(3)
+            quant("QE3", 0, 128, v("E", 0, 512))
+            send(raw(v("LB1c", P, P + n)), raw(v("QE3c", 0, n)), "a3c")
+            send(v("LB1s", P, P + n), v("QE3s", 0, n), "a3s")
+            todo += [[lambda t=t: ts(v("PL", 3 * t, 3 * t + 3), v("HS", 29, 42, 6), 4.0, A.mult, float(t), A.add)] for t in range(4)]
+            blend_list()
+            gap(2)
+            dma("y", T.op[:, :], v("UP", rows=slice(0, 128, 16)))
+            blend(3, 0)
+            layer("LB1", P + n - 128, 128, range(4))
+            mend(128 - n)
 
-    take_h(3, LAND[3] - first)
-    for a, b in ((0, 256), (256, P)):
-        for t in (1, 2, 3):
-            fetch(3, t, max(a, OWN) if t == 1 else a, b)
-    add_near(3, 0, 0, P)
-    add_fetched(3, 1, OWN, 256)
-    add_near(3, 1, 0, OWN)
-    for i, (a, b) in enumerate(((0, 256), (256, P))):
-        for t in (2, 3):
-            add_fetched(3, t, a, b)
-        if i == 0:
-            add_fetched(3, 1, 256, P)
-        quant("QX4", a, b, v("X2", 4 * a, 4 * b))
-        mm(4 + i, "QV", 0, "QX4", a, b - a)
-        dma("y", T.oc[:, 4 * a:4 * b], raw(v("QX4c", a, b)))
-    evac("s", v("ysb", 0, 256), v("p4", 0, 256))
-    dma("s", T.y[:, 0:256], v("ysb", 0, 256))
-    for k2 in range(4):
-        dma("sy"[k2 % 2], T.osc[4 * k2:4 * k2 + 4, :], v("QX4s", rows=slice(32 * k2, 32 * k2 + 4)))
-    evac("v", v("ysb", 256, P), v("p5", 0, 128))
-    dma("y", T.y[:, 256:P], v("ysb", 256, P))
+    def store(c):
+        a, b = 128 * c, 128 * c + 128
+        if c > 0:
+            a0 = (0, 0, a)[c]
+            dma("y", T.oc[:, 4 * a0:4 * b], raw(v("QX4c", a0, b)))
+        if c < 2:
+            evac("s", v("ysb", a, b), v("p%d" % (4 + c), 0, 128))
+        if c == 1:
+            dma("s", T.y[:, 0:b], v("ysb", 0, b))
+        if c == 2:
+            for k2 in range(4):
+                dma("sy"[k2 % 2], T.osc[4 * k2:4 * k2 + 4, :], v("QX4s", rows=slice(32 * k2, 32 * k2 + 4)))
+            evac("v", v("ysb", a, b), v("p6", 0, 128))
+            dma("y", T.y[:, a:b], v("ysb", a, b))
+
+    for c in range(3):
+        quantise_and_score(4, c)
+        store(c)
 
     for sem, val in cnt.items():
         if waited.get(sem, 0) < val:

@@ -10,7 +10,7 @@ UPC = {1: 0, 2: 0, 3: 4}
 LOC = {1: 12, 2: 6, 3: 0}
 SECOND = 320
 VW = 576
-OWN = {1: 256, 2: 256, 3: 128}
+OWN = 160
 XB = {1: "X1", 2: "X2", 3: "X3", 4: "X2"}
 BF, F32, F16, U16, I32, U8, FP8 = "bfloat16", "float32", "float16", "uint16", "int32", "uint8", "float8_e4m3fn_x4"
 SIZE = {BF: 2, F32: 4, F16: 2, U16: 2, I32: 4, U8: 1, FP8: 4}
@@ -28,14 +28,16 @@ for _n, _c in (("QX1", P), ("QX2", P), ("QX3", P), ("QX4", P), ("QU", 128), ("UR
     _buf(_n + "s", _c, U8)
 for _n, _c, _t in (
         ("X1", 4 * P, BF), ("X2", 4 * P, BF), ("X3", 4 * P, BF), ("ub", 512, BF), ("vb", 512, BF), ("half", 576, BF),
-        ("zi", 516, BF), ("FP", 4 * P, BF), ("V", 4 * VW, BF), ("FQ", 2 * P, BF), ("E", 768, BF), ("tmp", 832, BF),
-        ("tb", 4 * P, BF), ("m16s", 16, BF), ("m16", P, BF), ("hold", P, BF), ("climb", P, BF), ("C", 576, BF),
+        ("zi", 516, BF), ("FP", 4 * P, BF), ("V", 4 * VW, BF), ("FQ", 2 * P - OWN, BF), ("E", 768, BF), ("tmp", 832, BF),
+        ("tb", 4 * P, BF), ("m16s", 16, BF), ("pair", 96, BF), ("c16", 16, BF), ("climb", P, BF), ("C", 576, BF),
         ("CS", 576, BF), ("miss", 608, BF), ("AT", 608, F16), ("HS", 608, F16),
-        ("tw32", 48, I32), ("ic", 24, I32), ("i16", 24, I32), ("ti", 96, I32), ("W2", 48, F32), ("MT", 96, F32), ("TT", 96, F32),
-        ("ml", 6, U16), ("fl", 2, U16), ("il", 24, U16), ("ul", 8, U16), ("BL", 32, U16), ("UL", 24, U16), ("NX", 64, U16), ("PL", 12, U16),
-        ("PF", 36, F32), ("AD", 48, F32), ("cols", 12, F32), ("iotaR", 576, F32), ("J0", 38, F32), ("J", 38, F32),
-        ("opc", 52, F32), ("UP", P, F32), ("ht", P, F32), ("ysb", P, F32), ("SS", P, F32), ("GM", P, F32), ("SC", P, F32),
-        ("BX", 576, F32), ("tf", 448, F32)):
+        ("tw32", 48, I32), ("ic", 24, I32), ("i16", 24, I32), ("ti", 96, I32),
+        ("ml", 6, U16), ("fl", 2, U16), ("il", 24, U16), ("ul", 8, U16), ("xl", 2, U16), ("xn", 2, U16),
+        ("XL", 32, U16), ("UL", 24, U16), ("PL", 12, U16),
+        ("W2", 48, F32), ("MT", 96, F32), ("TT", 120, F32), ("NX", 128, F32), ("U0", 8, F32), ("PF", 32, F32),
+        ("AD", 32, F32), ("cols", 16, F32), ("iotaR", 576, F32), ("J0", 38, F32), ("J", 38, F32), ("opc", 52, F32),
+        ("UP", P, F32), ("ht", P, F32), ("ysb", P, F32), ("SS", P, F32), ("GM", P, F32), ("SC", P, F32),
+        ("BX", 576, F32), ("tf", 192, F32)):
     _buf(_n, _c, _t)
 for _r in (1, 2, 3):
     _w = LANES[_r]
@@ -46,6 +48,7 @@ for _r in (1, 2, 3):
         _buf("CM%d" % _r, _w + 1, U16)
     if _r < 3:
         _buf("LL%d" % _r, _w + 1, U16)
+        _buf("CF%d" % _r, _w + 1, F32)
 for _i in range(8):
     _buf("p%d" % _i, 512, F32, "psum")
 
@@ -81,7 +84,7 @@ def rank_program(g, core, T, topo):
 
     ENG = {"v": g.vector, "s": g.scalar, "t": g.tensor, "g": g, "y": g.sync}
     QSEM = {"v": "vs", "s": "ss", "t": "ts", "g": "gs"}
-    cnt, known, seen, waited, nd = {}, {q: {} for q in ENG}, {}, {}, [0]
+    cnt, known, seen, waited, nd, probe = {}, {q: {} for q in ENG}, {}, {}, [0], []
 
     def ap(x):
         if not isinstance(x, dict):
@@ -140,6 +143,9 @@ def rank_program(g, core, T, topo):
 
     def op(q, reads, writes, fn):
         acc = touches(q, reads, writes, False)
+        if probe:
+            probe[0] = acc
+            return
         before(q, acc)
         sem = QSEM[q]
         fn().then_inc(T.sem[sem], 1)
@@ -177,6 +183,9 @@ def rank_program(g, core, T, topo):
     def memset(out, k):
         op("v", [], [out], lambda: g.vector.memset(ap(out), k))
 
+    def turn(out, in_):
+        op("v", [in_], [out], lambda: g.vector.transpose(ap(out), ap(in_)))
+
     def scan(out, d0, d1, o0, o1, first=0.0):
         op("v", [d0, d1], [out], lambda: g.vector.tensor_tensor_scan(ap(out), ap(d0), ap(d1), first, o0, o1))
 
@@ -207,67 +216,78 @@ def rank_program(g, core, T, topo):
         else:
             ts(out, in_, scale, A.mult)
 
-    col = {k2: v("cols", i, i + 1) for i, k2 in enumerate(("i", "m0", "oct", "rise", 1, 2, 3))}
+    col = {k2: v("cols", i, i + 1) for i, k2 in enumerate(("i", "m0", "oct", "rise", 1, 2, 3, "own", "a", "b", "c", "d", "e", "f"))}
     tower = v("i16", 0, 1)
 
     todo = []
 
     def gap(n=2):
-        for chain in [c for c in todo if c][:n]:
-            chain.pop(0)()
+        held = []
+        for call in list(todo):
+            probe.append(None)
+            call()
+            acc = probe.pop()
+            if n and not any(a == b and m & m2 and (w or w2) for a, m, w in acc for b, m2, w2 in held):
+                todo.remove(call)
+                call()
+                n -= 1
+            held += acc
 
-    def finish(*chains):
-        while any(chains):
-            for chain in chains:
-                if chain:
-                    chain.pop(0)()
+    def finish():
+        while todo:
+            gap(9)
 
-    def pair_lists(r):
-        W, n = LANES[r], NR[r] // 16
-        j = v("J", 0, n)
-        k, kw, kp, mn, mx = v("ti", 0, n), v("tf", 0, n), v("tf", 48, 48 + n), v("tf", 96, 96 + n), v("tf", 144, 144 + n)
-        return [lambda: ts(k, j, 1.0 / W, A.mult, -(W - 1) / (2.0 * W), A.add),
-                lambda: ts(kw, k, -float(W), A.mult),
-                lambda: tt(kp, j, kw, A.add),
-                lambda: tt(mx, k, kp, A.max),
-                lambda: tt(mn, k, kp, A.min),
-                lambda: ts(v("MX%d" % r), mx, 16.0, A.mult, 15.0, A.add),
-                lambda: ts(v("MN%d" % r), mn, 16.0, A.mult, 15.0, A.add)]
-
-    def lane_lists(r):
-        W, m = LANES[r], NE[r] // 16
-        j, sg, sl, ps, far = v("J", 0, m), v("ti", 48, 48 + m), v("tf", 192, 192 + m), v("tf", 240, 240 + m), v("tf", 288, 288 + m)
-        calls = [lambda: ts(sg, j, 1.0 / W, A.mult, -(W - 1) / (2.0 * W), A.add),
-                 lambda: ts(sl, sg, -float(W), A.mult),
-                 lambda: tt(ps, j, sl, A.add),
-                 lambda: ts(v("KS%d" % r), ps, float(W), A.mult, W - 1.0, A.add)]
+    def lists(r):
+        W, n, m = LANES[r], NR[r] // 16, NE[r] // 16
+        j, k = v("J", 0, m), v("ti", 0, m)
+        c, s, t, low = (v("tf", 48 * i, 48 * i + m) for i in range(4))
+        calls = [lambda: ts(k, j, 1.0 / W, A.mult, -(W - 1) / (2.0 * W), A.add),
+                 lambda: ts(t, k, -float(W), A.mult),
+                 lambda: tt(c, j, t, A.add)]
         if r == 1:
-            return calls + [lambda: vcopy(v("KL1"), ps)]
-        return calls + [lambda: ts(far, j, float(W * max(UPC[r], LOC[r])), A.is_ge, 16.0, A.mult),
-                        lambda: tt(far, far, ps, A.add),
-                        lambda: vcopy(v("KL%d" % r), far)]
+            calls += [lambda: ts(s, j, float(W), A.is_lt),
+                      lambda: tt(s, s, k, A.add),
+                      lambda: tt(s, s, c, A.add),
+                      lambda: ts(t, s, float(W), A.is_ge, -float(W), A.mult),
+                      lambda: tt(s, s, t, A.add)]
+        else:
+            s = c
+        return calls + [lambda: vcopy(v("KL%d" % r), c), lambda: tt(t, k, s, A.max),
+                        lambda: tt(low, k, s, A.min),
+                        lambda: ts(v("MN%d" % r), v("tf", 144, 144 + n), 16.0, A.mult, col["own"], A.add),
+                        lambda: ts(v("MX%d" % r), v("tf", 96, 96 + n), 16.0, A.mult, col["own"], A.add),
+                        lambda: ts(v("KS%d" % r), c, float(W), A.mult, W - 1.0, A.add)]
 
     def thresholds(r, upper):
         W, t = LANES[r], "TH%d" % r
         h = W // 2
         s0, first = (UPC[r], h) if upper else (LOC[r], 0)
         n = W + 2 - s0 if s0 else max(UPC[r], LOC[r])
-        iota(v(t, s0 * W, (s0 + n) * W), [[-1, n], [-1, W]], W - 2 - first)
-        iota(v(t, s0 * W + W - 1, (s0 + n) * W, W), [[-1, n]], 1 - first)
+        if r == 1:
+            iota(v(t, s0 * W, (s0 + n) * W), [[1, n], [0, W]], first)
+        else:
+            iota(v(t, s0 * W, (s0 + n) * W), [[-1, n], [-1, W]], W - 2 - first)
+            iota(v(t, s0 * W + W - 1, (s0 + n) * W, W), [[-1, n]], 1 - first)
 
     def tower0(r):
         W, t = LANES[r], "TH%d" % r
         a = LOC[r] * W
-        act(v(t, a + W, a + W * (W // 2 + 1)), v(t, a + W, a + W * (W // 2 + 1)), AF.Identity, bias=col["m0"])
+        act(v(t, a + W, a + W * (W // 2 + 1)), v(t, a + W, a + W * (W // 2 + 1)), AF.Identity,
+            bias=col["m0"] if r == 1 else v("m16s", 0, 1))
         act(v(t, a, a + W), v(t, a, a + W), AF.Identity, bias=col[r])
 
     def signs(r):
         W, d = LANES[r], "D0%d" % r
-        if r > 1:
+        if r == 1:
+            iota(v(d, W, W * W, W), [[0, W - 1]], 0)
+            iota(v(d, W + 1, W * W, W), [[1, W - 1]], 2 - W)
+            iota(v(d, 2 * W - 1, (W - 1) * W, W - 1), [[0, W - 2]], -1)
+            iota(v(d, W - 1, W), [[0, 1]], -1)
+        else:
             iota(v(d), [[0, NR[r]]], 1)
-        iota(v(d, 0, W * W, W), [[0, W]], 0)
-        iota(v(d, 1, (W + 1) * (W - 2) + 2, W + 1), [[0, W - 1]], -1)
-        iota(v(d, W * W - 1, W * W), [[0, 1]], -1)
+            iota(v(d, 0, W * W, W), [[0, W]], 0)
+            iota(v(d, 1, (W + 1) * (W - 2) + 2, W + 1), [[0, W - 1]], -1)
+            iota(v(d, W * W - 1, W * W), [[0, 1]], -1)
 
     def slots(r):
         n, k = 8 * LANES[r], (1, 1, 3)[r - 1]
@@ -276,24 +296,29 @@ def rank_program(g, core, T, topo):
         if r == 3:
             iota(v("VB3", n + 15), [[0, 1]], P)
 
+    def tables(r):
+        thresholds(r, False)
+        thresholds(r, True)
+        signs(r)
+        slots(r)
+
     def table(r, kind):
-        if r == 1:
-            return v("BL", 0, 24)
-        a = 32 * (r - 2) + (16 if (kind == "tops") == (UPC[r] > LOC[r]) else 0)
-        return v("NX", a, a + LANES[r])
+        return 64 * (r - 2) + 16 * ("tops", "bases", "below", "above").index(kind)
 
     def steps(r):
         W = LANES[r]
         if r == 1:
-            return [lambda: vcopy(v("PF", 0, W), table(1, "bases")), lambda: tt(v("AD", 0, W), v("PF", 0, W), v("PF", 1, W + 1), A.subtract)]
-        return [lambda: vcopy(v("PF", 0, 32), v("NX", 32 * (r - 2), 32 * (r - 1))),
-                lambda: tt(v("AD", 0, 32), v("PF", 0, 32), v("PF", 1, 33), A.subtract),
-                lambda: tt(v("AD", 32, 32 + W), v("PF", 0, W), v("PF", 1, W + 1), A.subtract)]
+            return [lambda: tt(v("AD", 0, W), v("PF", 0, W), v("PF", 1, W + 1), A.subtract)]
+        a = table(r, "tops")
+        return [lambda: vcopy(v("XL", 0, 16), by(v("NX", a + 16, a + 64), v("xn", 0, 1))),
+                lambda: tt(v("AD", 0, 32), v("NX", a, a + 32), v("NX", a + 1, a + 33), A.subtract)]
 
-    def spread(r):
-        act(v("AT", 0, NE[r]), by(v("AD", 0, 32), v("KL%d" % r)))
-        if r > 1:
-            act(v("AT", SECOND, SECOND + NE[r]), by(v("AD", 16, 48), v("KL%d" % r)))
+    def spread(r, first=0, last=2):
+        W = LANES[r]
+        cut = W * max(UPC[r], LOC[r])
+        for a, n in ((0, -(-cut // 16)), (cut, -(-(W * W + W - cut) // 16)))[first:last]:
+            for at, tab in ((0, 16 * ((a > 0) == (r == 2))), (SECOND, 16 * ((a > 0) != (r == 2)))):
+                act(v("AT", at + a, at + a + 16 * n), by(v("AD", tab, tab + W), v("KL%d" % r, 0, n)))
 
     def plane(t, a=0, b=P):
         return v("V", VW * t + a, VW * t + b)
@@ -301,63 +326,73 @@ def rank_program(g, core, T, topo):
     def arrived(t, a=0, b=P):
         return v("FP", P * t + a, P * t + b)
 
-    def unpack(q, bank, a=0, b=P):
-        for t in range(4):
+    def unpack(q, bank, a=0, b=P, planes=range(4)):
+        for t in planes:
             mm(bank + t, "EC", 128 * t, q, a, b - a)
 
-    def unpack_arrived(r, a, b):
+    def unpack_arrived(r, a, b, between=lambda: None):
         unpack("LB%d" % r, 4, a, b)
         for t in range(4):
+            if t == 3:
+                between()
             act(arrived(t, a, b), v("p%d" % (4 + t), 0, b - a))
 
-    def own_plane(r, t):
+    def own_plane(t):
         act(plane(t), v("p%d" % t, 0, P))
         if t < 2:
-            a = (0, OWN[r])[t]
+            a = (0, OWN)[t]
             dma("y", v("FQ", P * t, P * t + P - a), plane(t, a, P))
 
     def quantise_and_score(r, c):
         q, a, b = "QX%d" % r, 128 * c, 128 * c + 128
         quant(q, a, b, v(XB[r], 4 * a, 4 * b))
-        if r < 3:
-            send(raw(v("LB%dc" % r, a, b)), raw(v(q + "c", a, b)), "a%dc%d" % (r, c))
-            if c > 0:
-                a0 = (0, 0, a)[c]
-                send(v("LB%ds" % r, a0, b), v(q + "s", a0, b), "a%ds%d" % (r, c))
+        if r == 1 or r == 2 and c > 0:
+            a0 = 0 if (r, c) == (2, 1) else a
+            send(raw(v("LB%dc" % r, a0, b)), raw(v(q + "c", a0, b)), "a%dc%d" % (r, c))
+        if r < 3 and c > 0:
+            a0 = (0, 0, a)[c]
+            send(v("LB%ds" % r, a0, b), v(q + "s", a0, b), "a%ds%d" % (r, c))
         if r > 1:
             mm(4 + c, "UR" if r < 4 else "QV", 0, q, a, 128)
 
-    def take_scores(q, c, a=0, b=128):
-        evac(q, v("SS", 128 * c + a, 128 * c + b), v("p%d" % (4 + c), a, b))
+    def take_scores(q, c):
+        evac(q, v("SS", 128 * c, 128 * c + 128), v("p%d" % (4 + c), 0, 128))
 
-    def gather_scores(r, cuts):
-        runs = list(zip(cuts, cuts[1:]))
-        base = table(r, "bases")
-        for a, b in runs:
-            tt(v("GM", a, b), by(v("SS"), v(base["n"], base["a"] + a // 16, base["a"] + b // 16)), v("m16", a, b), A.mult)
-        gap(2 - len(runs))
-        for a, b in runs:
-            scan(v("SC", a, b), v("hold", a, b), v("GM", a, b), A.mult, A.add)
+    def gather_scores(r, cut):
+        n = 16 * LANES[r]
+        vcopy(v("GM", 0, cut), by(v("SS"), v("XL", 0, cut // 16)))
+        act(v("GM", cut, n), by(v("SS"), v("XL", cut // 16, n // 16)))
+        gap(3)
+        for a, b in ((0, cut), (cut, n)):
+            turn(v("SC", a, b), v("GM", a, b))
 
     def pairs(r, q, a, b):
-        (act if q == "s" else vcopy)(v("BX", a, b), by(v("SC"), v("MX%d" % r, a // 16, b // 16)))
+        lanes = -(-b // LANES[r])
+        (act if q == "s" else vcopy)(v("BX", a, b), by(v("SC", 0, 16 * lanes), v("MN%d" % r, a // 16, b // 16)))
 
     def compare(r, a, b):
-        tt(v("C", a, b), by(v("SC"), v("MN%d" % r, a // 16, b // 16)), v("BX", a, b), A.is_ge)
+        tt(v("C", a, b), by(v("SC"), v("MX%d" % r, a // 16, b // 16)), v("BX", a, b), A.is_le)
 
     def rank_sums(r, a, b):
-        scan(v("CS", a, b), v("D0%d" % r, a, b), v("C", a, b), A.mult, A.add)
+        scan(v("CS", a, b), v("D0%d" % r, a, b), v("C", a, b), A.mult, A.add, 2.0 - LANES[r])
 
     def misses(r, a, b, at=0):
         tt(v("miss", at + a, at + b), by(v("CS"), v("KS%d" % r, a // 16, b // 16)), v("TH%d" % r, a, b), A.not_equal)
 
-    def places(r, s0, s1, at=0):
-        a, b = at + s0 * LANES[r], at + s1 * LANES[r]
-        scan(v("HS", a, b), v("miss", a, b), v("AT", a, b), A.mult, A.add)
+    def distances(s):
+        act(v("miss", 24 * s, 24 * s + 24), v("CS", 23, 576, 24), AF.Abs, bias=-12.0 - s)
 
-    def listed(name, r, s0, s1, at=0):
+    def places(r, s0, s1, at=0, clear=A.mult):
+        a, b = at + s0 * LANES[r], at + s1 * LANES[r]
+        scan(v("HS", a, b), v("miss", a, b), v("AT", a, b), clear, A.add, P / 2048.0)
+
+    def listed(name, r, at=0):
         W = LANES[r]
-        vcopy(v(name + str(r), s0, s1), v("HS", at + s0 * W + W - 1, at + s1 * W, W))
+        ends = v("HS", at + W - 1, at + (W + 1) * W, W)
+        if r == 1:
+            ts(v(name + "1"), ends, 2048.0, A.mult, -float(P), A.add)
+        else:
+            vcopy(v(name + str(r)), ends)
 
     def upper(name, r):
         return v(name + str(r), UPC[r], UPC[r] + LANES[r] // 2)
@@ -366,15 +401,18 @@ def rank_program(g, core, T, topo):
         return v(name + str(r), LOC[r], LOC[r] + LANES[r] // 2 + 1)
 
     def next_tables(r):
-        h, cl = LANES[r] // 2, "CL%d" % r
-        nb, nt, lo, up = table(r + 1, "bases")["a"], table(r + 1, "tops")["a"], LOC[r], UPC[r]
-        dma("y", v("NX", nb, nb + h), v(cl, lo, lo + h))
-        dma("y", v("NX", nt, nt + h, rows=slice(1, 128)), v(cl, up, up + h, rows=slice(0, 127)))
-        dma("y", v("NX", nb, nb + h, rows=slice(0, 128, 16)), v(cl, lo + 1, lo + h + 1, rows=slice(0, 128, 16)))
-        dma("y", v("NX", nt, nt + h, rows=slice(0, 128, 16)), v(cl, up, up + h, rows=slice(15, 128, 16)))
+        h, cl, lo, up = LANES[r] // 2, "CF%d" % r, LOC[r], UPC[r]
+        for kind, c, to, of in (("bases", lo, slice(0, 128), slice(0, 128)), ("below", lo, slice(0, 112), slice(16, 128)),
+                                ("above", lo, slice(16, 128), slice(0, 112)), ("tops", up, slice(1, 128), slice(0, 127)),
+                                ("bases", lo + 1, slice(0, 128, 16), slice(0, 128, 16)),
+                                ("below", lo + 1, slice(0, 128, 32), slice(16, 128, 32)),
+                                ("above", lo + 1, slice(16, 128, 32), slice(0, 128, 32)),
+                                ("tops", up, slice(0, 128, 16), slice(15, 128, 16))):
+            a = table(r + 1, kind)
+            dma("y", v("NX", a, a + h, rows=to), v(cl, c, c + h, rows=of))
 
-    def upper_bases(r, copy=act):
-        copy(v("VB%d" % r, 1, 8 * LANES[r] + 1), by(v("iotaR", 0, P), upper("CL" if r == 1 else "CM", r)))
+    def upper_bases(r):
+        act(v("VB%d" % r, 1, 8 * LANES[r] + 1), by(v("iotaR", 0, P), upper("CL" if r == 1 else "CM", r)))
 
     def new_tops(r, values):
         vcopy(by(v("UP"), upper("CL", r)), values)
@@ -387,24 +425,40 @@ def rank_program(g, core, T, topo):
         gap()
         ts(v("UL"), v("ht", 15, P, 16), col["rise"], A.subtract)
 
-    def make_e(r, win, lst, between):
-        n = 8 * LANES[r]
-        for t in range(4):
-            (vcopy if t == 0 else act)(v("tmp", (n + 16) * t, (n + 16) * (t + 1)), by(win(t), lower(lst, r)))
+    def make_e(r, win, lst, between=lambda: None):
+        n, name = 8 * LANES[r], lst + str(r)
+
+        def bases(copy, t, a=0, b=n + 16):
+            copy(v("tmp", (n + 16) * t + a, (n + 16) * t + b), by(win(t), v(name, LOC[r] + a // 16, LOC[r] + b // 16)))
+
+        def tops(t, a=0, b=n):
+            c = (n + 16) * t + 1
+            tt(v("E", 4 * a + t, 4 * b, 4), by(win(t), v(name, UPC[r] + a // 16, UPC[r] + b // 16)), v("tmp", c + a, c + b), A.add)
+
+        bases(vcopy, 0)
+        if r == 1:
+            bases(act, 1, 0, 96)
+            bases(act, 1, 96)
+            tops(1, 0, 64)
+        else:
+            bases(act, 1)
+        bases(act, 2)
+        bases(act, 3)
         between()
-        for t in range(4):
-            a = (n + 16) * t + 1
-            tt(v("E", t, 4 * n, 4), by(win(t), upper(lst, r)), v("tmp", a, a + n), A.add)
+        tops(0)
+        tops(1, 64 if r == 1 else 0)
+        tops(2)
+        tops(3)
 
     def layer(q, a, n, order=(1, 0, 2, 3)):
         for b in order:
             mm(4 + b, "WW", 128 * b, q, a, n)
 
-    def blend(r, off):
+    def blend(r):
         n = 8 * LANES[r]
 
         def take_h(q, b):
-            evac(q, plane(b, P, P + n), v("p%d" % (4 + b), off, off + n), 0.015625)
+            evac(q, plane(b, P, P + n), v("p%d" % (4 + b), 0, n), 0.015625)
 
         def near(t, a, b):
             return by(plane(t, 0, P + n), v("UL", a // 16, b // 16))
@@ -412,257 +466,255 @@ def rank_program(g, core, T, topo):
         def x(t, a, b):
             return v(XB[r + 1], 4 * a + t, 4 * b, 4)
 
-        def fetch(t, a, b):
-            act(v("tb", P * t + a, P * t + b), near(t, a, b))
-
-        def add(t, a, b):
-            tt(x(t, a, b), v("tb", P * t + a, P * t + b), v("p%d" % t, a, b), A.add)
-
-        own = OWN[r]
-        parts = [(1, 0, own), (2, 0, 256), (3, 0, 256), (2, 256, P), (3, 256, P)]
+        parts = [(1, 0, OWN), (2, 0, P), (3, 0, 192), (3, 192, 320), (3, 320, P)]
         if r < 3:
-            for q, t in (("s", 1), ("v", 0), ("v", 2), ("v", 3)):
+            for q, t in (("s", 1), ("v", 0), ("v", 2)):
                 take_h(q, t)
-        else:
-            parts = [(1, 0, own), (2, 0, P), (3, 0, 256), (3, 256, P)]
-        for part in parts:
-            fetch(*part)
+        for t, a, b in parts:
+            act(v("tb", P * t + a, P * t + b), near(t, a, b))
+            if r < 3 and t == 1:
+                take_h("s", 3)
         tt(x(0, 0, P), near(0, 0, P), v("FQ", 0, P), A.add)
-        tt(x(1, own, P), near(1, own, P), v("FQ", P, 2 * P - own), A.add)
-        for part in parts:
-            add(*part)
+        tt(x(1, OWN, P), near(1, OWN, P), v("FQ", P), A.add)
+        for t, a, b in parts:
+            tt(x(t, a, b), v("tb", P * t + a, P * t + b), v("p%d" % t, a, b), A.add)
         if r < 3:
             for c in range(3):
                 quantise_and_score(r + 1, c)
 
     def mend(off):
-        n = 8 * LANES[3]
+        n = 16 * LANES[3]
         for t in range(4):
-            evac("s", v("tmp", n * t, n * t + n), v("p%d" % (4 + t), off, off + n), 0.015625)
-            tt(v("E", n * t, n * t + n), by(plane(t), upper("CL", 3)), v("tmp", n * t, n * t + n), A.add)
-        vcopy(by(v(XB[4]), v("PL")), v("E", 0, 4 * n))
+            evac("s", v("FP", n * t + 1, n * t + n, 2), v("p%d" % (4 + t), off, off + n // 2), 0.015625)
+            scan(v("E", n * t, n * t + n), v("pair"), v("FP", n * t, n * t + n), A.mult, A.add)
+        vcopy(by(v(XB[4]), v("PL")), v("E", 1, 4 * n, 2))
 
     dma("y", v("ub"), T.u[:, :])
     dma("s", v("tw32", 0, 24), T.tw[:, :])
     dma("s", v("tw32", 24, 48, rows=slice(0, 120)), T.tw[8:128, :])
     for c in range(3):
-        dma("yys"[c], v("X1", 512 * c, 512 * c + 512), T.x[:, 512 * c:512 * c + 512])
+        dma("y", v("X1", 512 * c, 512 * c + 512), T.x[:, 512 * c:512 * c + 512])
 
     iota(v("ic"), [[0, 24]], 0, 1)
     iota(v("J0"), [[16, 38]], 0)
+    iota(v("U0"), [[64, 4], [0, 2]], 0)
     memset(v("half"), 0.5)
     op("g", [v("half")], [v("zi")], lambda: g.affine_select(T.zi[:], T.half[:, 0:516], [[1, 516]], A.is_equal, 0.0, -3, -4))
+    unpackers = [lambda b=b: quant("EC", 128 * b, 128 * b + 128, v("zi", 3 - b, 515 - b)) for b in range(4)]
+    act(v("D01"), v("half"), scale=2.0)
     thresholds(1, False)
+    act(v("W2"), v("half", 0, 48))
+    act(v("TT", 96), v("half", 0, 24), scale=-2.0 * P)
+    bit = {k2: v("ti", 60 + 2 * i, 61 + 2 * i) for i, k2 in enumerate((8, 23, 1, 16))}
     ts(v("i16"), v("ic"), 15, A.bitwise_and)
-    ts(v("ti", 0, 1), v("ic", 0, 1), 23, A.bitwise_and)
-    ts(v("ti", 2, 3), v("ic", 0, 1), 8, A.bitwise_and)
-    memset(v("W2"), 0.0)
-    vcopy(v("ul"), v("J0", 0, 8))
+    for k2 in (8, 23, 1, 16):
+        ts(bit[k2], v("ic", 0, 1), k2, A.bitwise_and)
     ts(col["i"], tower, 1.0, A.mult)
-    ts(col["oct"], v("ti", 2, 3), 4.0, A.mult)
-    vcopy(v("il"), v("i16", 0, 24))
+    ts(col["oct"], bit[8], 4.0, A.mult)
     for o in range(3):
         ts(v("ml", 2 * o, 2 * o + 2), v("i16", 0, 2), 3.0, A.mult, float(o), A.add)
     ts(v("J"), v("J0"), col["i"], A.add)
     ts(v("m16s"), v("J0", 0, 16), 1.0 / 16, A.mult, col["i"], A.is_equal)
-    ts(v("fl", 0, 1), v("ti", 0, 1), col["oct"], A.add)
-    ts(v("fl", 1, 2), v("ti", 0, 1), 64.0, A.add)
-    act(v("m16"), by(v("m16s"), v("il")))
-    p1, k1 = pair_lists(1), lane_lists(1)
-    c1 = [lambda: memset(v("PF"), 0.0), lambda: memset(v("AD"), 0.0),
-          lambda: ts(col["m0"], tower, 0.0, A.is_equal), lambda: ts(col[1], tower, 0.0, A.is_equal, -12.0, A.mult)]
-    unpackers = [lambda b=b: quant("EC", 128 * b, 128 * b + 128, v("zi", 3 - b, 515 - b)) for b in range(4)]
-    todo += [k1, p1, c1]
-    gap(3)
+    ts(col["a"], bit[23], col["oct"], A.add)
+    vcopy(v("il"), v("i16", 0, 24))
+    ts(v("ul"), v("U0"), col["oct"], A.add, 0.5, A.mult)
+    ts(col["own"], bit[16], 0.5, A.mult)
+    ts(col["d"], bit[1], -1.0, A.add)
+    act(v("c16"), v("m16s"), AF.Identity, scale=-33792.0, bias=1024.0)
+    for k2, x in (("m0", -1.0), (1, 12.0), (2, -6.0), (3, -3.0)):
+        act(col[k2], v("m16s", 0, 1), scale=x)
+    act(v("climb"), by(v("c16"), v("il")))
+    act(col["e"], col["own"], AF.Relu, scale=1.0 / 8, bias=col["d"])
+    act(col["f"], col["own"], AF.Identity, scale=33.0 / 8, bias=col["i"])
+    todo += lists(1)
+    gap(1)
+    ts(col["b"], bit[1], 15.0, A.mult, col["a"], A.add)
+    vcopy(v("fl", 0, 1), col["a"])
+    ts(v("fl", 1, 2), col["a"], 64.0, A.add)
 
     vcopy(v("W2", 0, 48, 2), v("tw32", 0, 24))
-    vcopy(v("W2", 1, 48, 2, rows=slice(0, 120)), v("tw32", 24, 48, rows=slice(0, 120)))
-    gap(3)
+    gap(2)
+    ts(col["c"], bit[16], -15.0 / 16, A.mult, col["b"], A.add)
+    gap(2)
     quant("QU", 0, 128, v("ub"))
-    act(v("MT"), by(v("W2"), v("ml")))
-    gap(3)
+    vcopy(v("W2", 1, 48, 2, rows=slice(0, 120)), v("tw32", 24, 48, rows=slice(0, 120)))
+    gap(2)
     vcopy(words(v("URc")), by(words(v("QUc")), v("ul")))
+    act(v("MT"), by(v("W2"), v("ml")))
     act(v("URs"), by(v("QUs"), v("ul")))
-    op("v", [v("MT")], [v("TT")], lambda: g.vector.transpose(T.TT[:, :], T.MT[:, :]))
-    gap(3)
+    act(v("TH1", 192, 288), v("TH1", 288, 384), AF.Identity, bias=20.0)
+    act(col["rise"], col["i"], AF.Identity, scale=-1024.0, bias=15360.0)
+    act(col["e"], col["e"], AF.Identity, scale=-48.0, bias=col["f"])
+    tower0(1)
     quantise_and_score(1, 0)
-    vcopy(v("BL"), by(v("TT"), v("fl")))
-    act(v("hold"), v("m16"), AF.Identity, scale=-1.0, bias=1.0)
-    act(v("D01"), v("half"), scale=2.0)
-    gap(3)
+    gap(1)
+    vcopy(v("xl", 0, 1), col["c"])
+    ts(v("xl", 1, 2), col["c"], 64.0, A.add, 95.0, A.min)
     quantise_and_score(1, 1)
-    todo.insert(0, steps(1))
-    gap(3)
-    unpackers[0]()
-    gap(3)
+    turn(v("TT", 0, 96), v("MT"))
+    gap(1)
     quantise_and_score(1, 2)
+    signs(1)
     for c in range(3):
         mm(4 + c, "UR", 0, "QX1", 128 * c, 128)
-    take_scores("v", 0)
-    take_scores("v", 1)
-    finish(*todo)
-    unpackers[1]()
+    take_scores("s", 0)
+    take_scores("s", 1)
+    vcopy(v("XL"), by(v("TT"), v("xl")))
+    ts(v("PF"), by(v("TT"), v("fl")), 1 / 2048.0, A.mult)
+    act(col["e"], col["d"], AF.Identity, scale=15.0, bias=col["e"])
+    gap(2)
+    unpackers[0]()
     take_scores("v", 2)
-    unpackers[2]()
-    spread(1)
-    signs(1)
+    todo[:0] = steps(1)
+    gap(3)
     iota(v("iotaR"), [[1, 576]], 0)
     slots(1)
 
-    gather_scores(1, (0, 256, 384))
-    unpackers[3]()
-    unpack("QX1", 0)
+    todo += [lambda: memset(v("NX"), 0.0)]
+    gather_scores(1, 160)
+    act(v("AT", 0, 288), by(v("AD", 0, 24), v("KL1", 0, 18)))
+    unpackers[1]()
+    unpack("QX1", 0, planes=(0, 1))
     pairs(1, "s", 0, 96)
-    pairs(1, "s", 288, 576)
-    pairs(1, "v", 96, 288)
-    act(v("TH1", 0, 288), v("TH1", 288, 576), AF.Identity, bias=-12.0)
-    tower0(1)
-    own_plane(1, 0)
-    own_plane(1, 1)
+    pairs(1, "s", 96, 384)
+    pairs(1, "v", 384, 576)
+    act(v("AT", 288), by(v("AD", 0, 24), v("KL1", 18)))
+    before("y", touches("y", [v("BX")], [], False))
     dma("y", raw(v("WWc")), T.wc[:, :])
     dma("y", v("WWs"), T.ws[:, :])
-    climb = [lambda a=a: ts(v("climb", a, a + 192), v("m16", a, a + 192), -33792.0, A.mult, 1024.0, A.add) for a in (0, 192)]
-    p2, k2 = pair_lists(2), lane_lists(2)
-    c2 = climb + [lambda: memset(v("NX"), 0), lambda: ts(col["rise"], tower, -1024.0, A.mult, 15360.0, A.add),
-                  lambda: ts(col[2], tower, 0.0, A.is_equal, -6.0, A.mult), lambda: ts(col[3], tower, 0.0, A.is_equal, -3.0, A.mult)]
-    todo += [c2, k2, p2]
-    compare(1, 0, 96)
-    compare(1, 96, 288)
-    compare(1, 288, 576)
-    rank_sums(1, 0, 288)
-    rank_sums(1, 288, 576)
-    gap(2)
-    misses(1, 0, 288)
+    own_plane(0)
+    own_plane(1)
+    todo += [lambda: ts(v("xn", 0, 1), col["e"], 15.0, A.add)] + lists(2)
+    for a, b in ((0, 96), (384, 576), (96, 384)):
+        compare(1, a, b)
+    for a, b in ((0, 96), (384, 576), (96, 384)):
+        rank_sums(1, a, b)
+    unpackers[2]()
+    for s in range(8):
+        distances(s)
     misses(1, 288, 608)
-    places(1, 0, 12)
+    misses(1, 192, 288)
+    places(1, 0, 8, clear=A.min)
     places(1, 12, 25)
-    listed("CL", 1, 0, 12)
-    gap(2)
-    listed("CL", 1, 12, 25)
+    places(1, 8, 12)
+    unpackers[3]()
+    listed("CL", 1)
     send(v("LL1"), v("CL1"), "a1l")
+    listed("CF", 1)
 
-    dma("g", v("vb"), T.v[:, :])
-    for r in (2, 3):
-        thresholds(r, False)
-        thresholds(r, True)
-        signs(r)
-        slots(r)
-    iota(v("opc", 0, 48), [[1, 3], [3, 16]], P + 3)
-    iota(v("opc", 48, 51), [[1, 3]], P)
-    unpack_arrived(1, 0, 256)
-    upper_bases(1)
+    tables(2)
+    unpack_arrived(1, 0, 256, lambda: upper_bases(1))
     unpack_arrived(1, 256, P)
-    own_plane(1, 2)
+    unpack("QX1", 0, planes=(2, 3))
+    gap(2)
     new_tops(1, v("iotaR", P, P + 192))
-    gap(3)
+    gap(1)
     links(1)
-    gap(3)
-    finish(c2)
     before("y", touches("y", [v("LL1")], [], False))
     next_tables(1)
-    make_e(1, arrived, "LL", lambda: gap(3))
-    own_plane(1, 3)
+    dma("y", v("vb"), T.v[:, :])
+    make_e(1, arrived, "LL")
+    own_plane(2)
+    own_plane(3)
     tower0(2)
     gap(3)
     quant("QE1", 0, 192, v("E"))
     layer("QE1", 0, 192)
     blend_list()
     gap(2)
-    blend(1, 0)
+    blend(1)
 
-    for r in (2, 3):
-        W = LANES[r]
-        n = 8 * W
+    def scores(r):
         unpack("QX%d" % r, 0)
-        todo.insert(0, steps(r))
+        todo[:0] = steps(r)
         for c in range(3):
-            gap(1)
-            take_scores("v", c)
-        finish(*todo)
-        spread(r)
-        for t in range(4):
-            own_plane(r, t)
-        if r == 2:
-            tower0(3)
-            unpack_arrived(2, 0, 256)
-            unpack_arrived(2, 256, P)
-            todo += [lane_lists(3), pair_lists(3)]
-            gather_scores(2, (0, 128, 192))
-            gap(2)
-            pairs(2, "v", 0, 96)
-            pairs(2, "v", 96, 144)
-            gap(1)
-            compare(2, 0, 96)
-            compare(2, 96, 144)
-            gap(3)
-            rank_sums(2, 0, 144)
-            gap(3)
-            misses(2, 0, 160)
-            misses(2, 0, 96, SECOND)
-            places(2, 0, 13)
-            misses(2, 96, 160, SECOND)
-            listed("CL", 2, 0, 13)
-            send(v("LL2"), v("CL2"), "a2l")
-            gap(1)
-            places(2, 0, 13, SECOND)
-            gap(3)
-            listed("CM", 2, 0, 13, SECOND)
-            new_tops(2, v("iotaR", P, P + n))
-            upper_bases(2, vcopy)
-            gap(2)
-            links(2)
-            finish(*todo)
-            before("y", touches("y", [v("LL2")], [], False))
-            next_tables(2)
-            make_e(2, arrived, "LL", gap)
-            quant("QE2", 0, 128, v("E", 0, 512))
-            layer("QE2", 0, 128)
-            blend_list()
-            blend(2, 0)
-        else:
-            todo += [[lambda: quant("QV", 0, 128, v("vb")), lambda: vcopy(v("opc", 15, 48, 16), v("opc", 48, 51))]]
-            gap(1)
-            gather_scores(3, (0, 96))
-            pairs(3, "v", 0, 48)
-            compare(3, 0, 48)
-            rank_sums(3, 0, 36)
-            misses(3, 0, 48)
-            misses(3, 0, 48, SECOND)
-            places(3, 0, 7)
-            places(3, 0, 7, SECOND)
-            listed("CL", 3, 0, 7)
-            listed("CM", 3, 0, 7, SECOND)
-            make_e(3, plane, "CL", lambda: (new_tops(3, v("opc", 0, n)), upper_bases(3)))
-            links(3)
-            quant("QE3", 0, 128, v("E", 0, 512))
-            send(raw(v("LB1c", P, P + n)), raw(v("QE3c", 0, n)), "a3c")
-            send(v("LB1s", P, P + n), v("QE3s", 0, n), "a3s")
-            todo += [[lambda t=t: ts(v("PL", 3 * t, 3 * t + 3), v("HS", 29, 42, 6), 4.0, A.mult, float(t), A.add)] for t in range(4)]
-            blend_list()
-            gap(2)
-            dma("y", T.op[:, :], v("UP", rows=slice(0, 128, 16)))
-            blend(3, 0)
-            layer("LB1", P + n - 128, 128, range(4))
-            mend(128 - n)
+            gap((3, 3, 0)[c])
+            take_scores("ssv"[c], c)
+        finish()
 
-    def store(c):
-        a, b = 128 * c, 128 * c + 128
-        if c > 0:
-            a0 = (0, 0, a)[c]
-            dma("y", T.oc[:, 4 * a0:4 * b], raw(v("QX4c", a0, b)))
-        if c < 2:
-            evac("s", v("ysb", a, b), v("p%d" % (4 + c), 0, 128))
-        if c == 1:
-            dma("s", T.y[:, 0:b], v("ysb", 0, b))
-        if c == 2:
-            for k2 in range(4):
-                dma("sy"[k2 % 2], T.osc[4 * k2:4 * k2 + 4, :], v("QX4s", rows=slice(32 * k2, 32 * k2 + 4)))
-            evac("v", v("ysb", a, b), v("p6", 0, 128))
-            dma("y", T.y[:, a:b], v("ysb", a, b))
+    scores(2)
+    todo += lists(3)
+    gather_scores(2, 96)
+    spread(2)
+    own_plane(0)
+    own_plane(1)
+    gap(1)
+    pairs(2, "v", 0, 64)
+    pairs(2, "v", 64, 144)
+    compare(2, 0, 64)
+    compare(2, 64, 144)
+    gap(3)
+    rank_sums(2, 0, 144)
+    misses(2, 0, 160)
+    misses(2, 0, 96, SECOND)
+    places(2, 0, 13)
+    misses(2, 96, 160, SECOND)
+    listed("CL", 2)
+    send(v("LL2"), v("CL2"), "a2l")
+    tables(3)
+    iota(v("opc", 0, 48), [[1, 3], [3, 16]], P + 3)
+    iota(v("opc", 48, 51), [[1, 3]], P)
+    iota(v("pair"), [[0, 48], [1, 2]], 0)
+    listed("CF", 2)
+    places(2, 0, 13, SECOND)
+    gap(2)
+    listed("CM", 2, SECOND)
+    unpack_arrived(2, 0, 256, lambda: upper_bases(2))
+    unpack_arrived(2, 256, P)
+    new_tops(2, v("iotaR", P, P + 96))
+    gap(3)
+    links(2)
+    before("y", touches("y", [v("LL2")], [], False))
+    next_tables(2)
+    make_e(2, arrived, "LL")
+    own_plane(2)
+    own_plane(3)
+    tower0(3)
+    quant("QE2", 0, 128, v("E", 0, 512))
+    layer("QE2", 0, 128)
+    blend_list()
+    blend(2)
+
+    scores(3)
+    spread(3, 0, 1)
+    gather_scores(3, 64)
+    spread(3, 1, 2)
+    for t in range(4):
+        own_plane(t)
+    quant("QV", 0, 128, v("vb"))
+    pairs(3, "v", 0, 48)
+    vcopy(v("opc", 15, 48, 16), v("opc", 48, 51))
+    compare(3, 0, 48)
+    rank_sums(3, 0, 36)
+    misses(3, 0, 48)
+    misses(3, 0, 48, SECOND)
+    places(3, 0, 7)
+    places(3, 0, 7, SECOND)
+    listed("CL", 3)
+    listed("CM", 3, SECOND)
+    make_e(3, plane, "CL", lambda: (new_tops(3, v("opc", 0, 48)), upper_bases(3)))
+    for t in range(4):
+        act(v("FP", 96 * t, 96 * t + 96, 2), by(plane(t), upper("CL", 3)))
+    links(3)
+    quant("QE3", 0, 128, v("E", 0, 512))
+    send(raw(v("LB1c", P, P + 48)), raw(v("QE3c", 0, 48)), "a3c")
+    send(v("LB1s", P, P + 48), v("QE3s", 0, 48), "a3s")
+    todo += [lambda t=t: ts(v("PL", 3 * t, 3 * t + 3), v("HS", 29, 42, 6), 4.0, A.mult, float(t), A.add) for t in range(4)]
+    blend_list()
+    gap(2)
+    dma("y", T.op[:, :], v("UP", rows=slice(0, 128, 16)))
+    blend(3)
+    layer("LB1", P + 48 - 128, 128, range(4))
+    mend(128 - 48)
 
     for c in range(3):
         quantise_and_score(4, c)
-        store(c)
+        dma("sys"[c], T.oc[:, 512 * c:512 * c + 512], raw(v("QX4c", 128 * c, 128 * c + 128)))
+    for k2 in range(4):
+        dma("yyss"[k2], T.osc[4 * k2:4 * k2 + 4, :], v("QX4s", rows=slice(32 * k2, 32 * k2 + 4)))
+    for c in range(3):
+        evac("v", v("ysb", 128 * c, 128 * c + 128), v("p%d" % (4 + c), 0, 128))
+        dma("ysy"[c], T.y[:, 128 * c:128 * c + 128], v("ysb", 128 * c, 128 * c + 128))
 
     for sem, val in cnt.items():
         if waited.get(sem, 0) < val:

from concourse.mybir import dt, AluOpType, ActivationFunctionType

A = AluOpType
AF = ActivationFunctionType
P = 384
LANES = {1: 24, 2: 12, 3: 6}
NR = {1: 576, 2: 144, 3: 48}
NE = {1: 608, 2: 160, 3: 48}
UPC = {1: 0, 2: 0, 3: 4}
LOC = {1: 12, 2: 6, 3: 0}
SECOND = 320
VW = 576
OWN = 160
XB = {1: "X1", 2: "X2", 3: "X3", 4: "X2"}
BF, F32, F16, U16, I32, U8, FP8 = "bfloat16", "float32", "float16", "uint16", "int32", "uint8", "float8_e4m3fn_x4"
SIZE = {BF: 2, F32: 4, F16: 2, U16: 2, I32: 4, U8: 1, FP8: 4}

SCRATCH = {}


def _buf(name, cols, dtype, where="sbuf"):
    SCRATCH[name] = (where, [128, cols], dtype)


for _n, _c in (("QX1", P), ("QX2", P), ("QX3", P), ("QX4", P), ("QU", 128), ("UR", 128), ("QV", 128), ("WW", 512),
               ("EC", 512), ("LB1", P + 64), ("LB2", P), ("QE1", 192), ("QE2", 128), ("QE3", 128)):
    _buf(_n + "c", _c, FP8)
    _buf(_n + "s", _c, U8)
for _n, _c, _t in (
        ("X1", 4 * P, BF), ("X2", 4 * P, BF), ("X3", 4 * P, BF), ("ub", 512, BF), ("vb", 512, BF), ("half", 576, BF),
        ("zi", 516, BF), ("FP", 4 * P, BF), ("V", 4 * VW, BF), ("FQ", 2 * P - OWN, BF), ("E", 768, BF), ("tmp", 832, BF),
        ("tb", 4 * P, BF), ("m16s", 16, BF), ("pair", 96, BF), ("c16", 16, BF), ("climb", P, BF), ("C", 576, BF),
        ("CS", 576, BF), ("miss", 608, BF), ("AT", 608, F16), ("HS", 608, F16),
        ("tw32", 48, I32), ("ic", 24, I32), ("i16", 24, I32), ("ti", 96, I32),
        ("ml", 6, U16), ("fl", 2, U16), ("il", 24, U16), ("ul", 8, U16), ("xl", 2, U16), ("xn", 2, U16),
        ("XL", 32, U16), ("UL", 24, U16), ("PL", 12, U16),
        ("W2", 48, F32), ("MT", 96, F32), ("TT", 120, F32), ("NX", 128, F32), ("U0", 8, F32), ("PF", 32, F32),
        ("AD", 32, F32), ("cols", 16, F32), ("iotaR", 576, F32), ("J0", 38, F32), ("J", 38, F32), ("opc", 52, F32),
        ("UP", P, F32), ("ht", P, F32), ("ysb", P, F32), ("SS", P, F32), ("GM", P, F32), ("SC", P, F32),
        ("BX", 576, F32), ("tf", 192, F32)):
    _buf(_n, _c, _t)
for _r in (1, 2, 3):
    _w = LANES[_r]
    for _n, _c, _t in (("D0", NR[_r], BF), ("TH", (_w + 2) * _w, BF), ("CL", _w + 1, U16), ("VB", 8 * _w + 16, F32),
                       ("MN", NR[_r] // 16, U16), ("MX", NR[_r] // 16, U16), ("KS", NE[_r] // 16, U16), ("KL", NE[_r] // 16, U16)):
        _buf(_n + str(_r), _c, _t)
    if _r > 1:
        _buf("CM%d" % _r, _w + 1, U16)
    if _r < 3:
        _buf("LL%d" % _r, _w + 1, U16)
        _buf("CF%d" % _r, _w + 1, F32)
for _i in range(8):
    _buf("p%d" % _i, 512, F32, "psum")

NDMA = 48
SEMAPHORES = (["vs", "ss", "ts", "gs", "loc", "a3c", "a3s"] + ["a%d%s" % (r, k) for r in (1, 2) for k in ("c0", "c1", "c2", "s1", "s2", "l")]
              + ["d%d" % i for i in range(NDMA)])


def v(name, a=0, b=None, step=1, rows=None):
    return {"n": name, "a": a, "b": SCRATCH[name][1][1] if b is None else b, "s": step, "rows": rows, "by": None, "as": None}


def by(win, lst):
    return dict(win, by=lst)


def words(x):
    return dict(x, **{"as": dt.uint32})


def raw(x):
    return dict(x, **{"as": dt.uint8})


def rank_program(g, core, T, topo):
    rank = T.rank_of(core)
    if rank is None:
        return
    nxt = T.cores[(rank + 1) % len(T.cores)]
    rid, pid = topo.addr(nxt)[:2]
    mask = topo.mask(core, nxt)
    neng = len(topo.engines(core, nxt))

    ENG = {"v": g.vector, "s": g.scalar, "t": g.tensor, "g": g, "y": g.sync}
    QSEM = {"v": "vs", "s": "ss", "t": "ts", "g": "gs"}
    cnt, known, seen, waited, nd, probe = {}, {q: {} for q in ENG}, {}, {}, [0], []

    def ap(x):
        if not isinstance(x, dict):
            return x
        a = T[x["n"]][x["rows"] if x["rows"] is not None else slice(None), x["a"]:x["b"]:x["s"]]
        if x["as"] is not None:
            a = a.bitcast(x["as"])
        return a if x["by"] is None else a.indirect(ap(x["by"]))

    def bits(x, blocks=False):
        where, shape, dtype = SCRATCH[x["n"]]
        if where == "psum":
            return 1
        m = 0
        k = 16 // SIZE[dtype] if blocks else 1
        for c in range(x["a"], x["b"], x["s"]):
            m |= ((1 << k) - 1) << (c - c % k)
        return m

    def touches(q, reads, writes, dma_):
        acc = []
        for x in reads:
            if isinstance(x, dict):
                acc.append((x["n"], bits(x), False))
                if x["by"] is not None:
                    acc.append((x["by"]["n"], bits(x["by"]), False))
        for x in writes:
            if isinstance(x, dict):
                acc.append((x["n"], bits(x, dma_), True))
                if x["by"] is not None:
                    acc.append((x["by"]["n"], bits(x["by"]), False))
        return acc

    def before(q, acc):
        ev = []
        for n, m, w in acc:
            for m2, w2, q2, e in seen.get(n, []):
                if m & m2 and (w or w2 or (SCRATCH[n][0] == "psum" and q != q2)):
                    ev.append(e)
        for sem, val, clock in sorted(ev, key=lambda e: -e[1]):
            if known[q].get(sem, 0) < val:
                ENG[q].wait_ge(T.sem[sem], val)
                waited[sem] = max(waited.get(sem, 0), val)
                for k2, v2 in clock.items():
                    if known[q].get(k2, 0) < v2:
                        known[q][k2] = v2

    def after(q, sem, acc):
        clock = dict(known[q])
        clock[sem] = cnt[sem]
        for n, m, w in acc:
            old = seen.get(n, [])
            if w:
                old = [e for e in old if e[0] & ~m]
            seen[n] = old + [(m, w, q, (sem, cnt[sem], clock))]

    def op(q, reads, writes, fn):
        acc = touches(q, reads, writes, False)
        if probe:
            probe[0] = acc
            return
        before(q, acc)
        sem = QSEM[q]
        fn().then_inc(T.sem[sem], 1)
        cnt[sem] = cnt.get(sem, 0) + 1
        after(q, sem, acc)

    def dma(q, out, in_):
        acc = touches(q, [in_], [out], True)
        before(q, acc)
        sem = "d%d" % nd[0]
        nd[0] += 1
        ENG[q].dma_start(ap(out), ap(in_)).then_inc(T.sem[sem], 16)
        cnt[sem] = 16
        after(q, sem, acc)

    def send(out, in_, sem):
        before("g", touches("g", [in_], [], False))
        g.remote_dma(ap(out), ap(in_), T.sem[sem], T.sem.loc, pid, rid, mask)
        cnt["loc"] = cnt.get("loc", 0) + neng
        cnt[sem] = neng
        seen.setdefault(out["n"], []).append((bits(out), True, "r", (sem, neng, {sem: neng})))

    def ts(out, in0, s1, op0, s2=None, op1=None):
        if op1 is None:
            op("v", [in0, s1], [out], lambda: g.vector.tensor_scalar(ap(out), ap(in0), ap(s1), None, op0))
        else:
            op("v", [in0, s1, s2], [out], lambda: g.vector.tensor_scalar(ap(out), ap(in0), ap(s1), ap(s2), op0, op1))

    def tt(out, in0, in1, o):
        op("v", [in0, in1], [out], lambda: g.vector.tensor_tensor(ap(out), ap(in0), ap(in1), o))

    def vcopy(out, in_):
        op("v", [in_], [out], lambda: g.vector.tensor_copy(ap(out), ap(in_)))

    def memset(out, k):
        op("v", [], [out], lambda: g.vector.memset(ap(out), k))

    def turn(out, in_):
        op("v", [in_], [out], lambda: g.vector.transpose(ap(out), ap(in_)))

    def scan(out, d0, d1, o0, o1, first=0.0):
        op("v", [d0, d1], [out], lambda: g.vector.tensor_tensor_scan(ap(out), ap(d0), ap(d1), first, o0, o1))

    def act(out, in_, func=AF.Copy, **kw):
        op("s", [in_, kw.get("bias")], [out],
           lambda: g.scalar.activation(ap(out), ap(in_), func, **{k: ap(x) for k, x in kw.items()}))

    def quant(q, a, b, in_):
        qc, qs = v(q + "c", a, b), v(q + "s", a, b)
        op("v", [in_], [qc, qs], lambda: g.vector.quantize_mx(ap(qc), ap(qs), ap(in_)))

    def mm(bank, l, la, r, ra, n):
        sides = [v(l + "c", la, la + 128), v(l + "s", la, la + 128), v(r + "c", ra, ra + n), v(r + "s", ra, ra + n)]
        out = v("p%d" % bank, 0, n)
        op("t", sides, [out], lambda: g.tensor.matmul_mx(ap(out), *[ap(x) for x in sides], True, True))

    def iota(out, pattern, base, cm=0):
        if SCRATCH[out["n"]][2] == I32:
            op("g", [], [out], lambda: g.iota(ap(out), pattern, base, cm))
        else:
            op("g", [], [out], lambda: g.iota(ap(out), pattern, base, cm, allow_small_or_imprecise_dtypes=True))

    def evac(q, out, in_, scale=None):
        if q == "s":
            act(out, in_, **({} if scale is None else {"scale": scale}))
        elif scale is None:
            vcopy(out, in_)
        else:
            ts(out, in_, scale, A.mult)

    col = {k2: v("cols", i, i + 1) for i, k2 in enumerate(("i", "m0", "oct", "rise", 1, 2, 3, "own", "a", "b", "c", "d", "e", "f"))}
    tower = v("i16", 0, 1)

    todo = []

    def gap(n=2):
        held = []
        for call in list(todo):
            probe.append(None)
            call()
            acc = probe.pop()
            if n and not any(a == b and m & m2 and (w or w2) for a, m, w in acc for b, m2, w2 in held):
                todo.remove(call)
                call()
                n -= 1
            held += acc

    def finish():
        while todo:
            gap(9)

    def lists(r):
        W, n, m = LANES[r], NR[r] // 16, NE[r] // 16
        j, k = v("J", 0, m), v("ti", 0, m)
        c, s, t, low = (v("tf", 48 * i, 48 * i + m) for i in range(4))
        calls = [lambda: ts(k, j, 1.0 / W, A.mult, -(W - 1) / (2.0 * W), A.add),
                 lambda: ts(t, k, -float(W), A.mult),
                 lambda: tt(c, j, t, A.add)]
        if r == 1:
            calls += [lambda: ts(s, j, float(W), A.is_lt),
                      lambda: tt(s, s, k, A.add),
                      lambda: tt(s, s, c, A.add),
                      lambda: ts(t, s, float(W), A.is_ge, -float(W), A.mult),
                      lambda: tt(s, s, t, A.add)]
        else:
            s = c
        return calls + [lambda: vcopy(v("KL%d" % r), c), lambda: tt(t, k, s, A.max),
                        lambda: tt(low, k, s, A.min),
                        lambda: ts(v("MN%d" % r), v("tf", 144, 144 + n), 16.0, A.mult, col["own"], A.add),
                        lambda: ts(v("MX%d" % r), v("tf", 96, 96 + n), 16.0, A.mult, col["own"], A.add),
                        lambda: ts(v("KS%d" % r), c, float(W), A.mult, W - 1.0, A.add)]

    def thresholds(r, upper):
        W, t = LANES[r], "TH%d" % r
        h = W // 2
        s0, first = (UPC[r], h) if upper else (LOC[r], 0)
        n = W + 2 - s0 if s0 else max(UPC[r], LOC[r])
        if r == 1:
            iota(v(t, s0 * W, (s0 + n) * W), [[1, n], [0, W]], first)
        else:
            iota(v(t, s0 * W, (s0 + n) * W), [[-1, n], [-1, W]], W - 2 - first)
            iota(v(t, s0 * W + W - 1, (s0 + n) * W, W), [[-1, n]], 1 - first)

    def tower0(r):
        W, t = LANES[r], "TH%d" % r
        a = LOC[r] * W
        act(v(t, a + W, a + W * (W // 2 + 1)), v(t, a + W, a + W * (W // 2 + 1)), AF.Identity,
            bias=col["m0"] if r == 1 else v("m16s", 0, 1))
        act(v(t, a, a + W), v(t, a, a + W), AF.Identity, bias=col[r])

    def signs(r):
        W, d = LANES[r], "D0%d" % r
        if r == 1:
            iota(v(d, W, W * W, W), [[0, W - 1]], 0)
            iota(v(d, W + 1, W * W, W), [[1, W - 1]], 2 - W)
            iota(v(d, 2 * W - 1, (W - 1) * W, W - 1), [[0, W - 2]], -1)
            iota(v(d, W - 1, W), [[0, 1]], -1)
        else:
            iota(v(d), [[0, NR[r]]], 1)
            iota(v(d, 0, W * W, W), [[0, W]], 0)
            iota(v(d, 1, (W + 1) * (W - 2) + 2, W + 1), [[0, W - 1]], -1)
            iota(v(d, W * W - 1, W * W), [[0, 1]], -1)

    def slots(r):
        n, k = 8 * LANES[r], (1, 1, 3)[r - 1]
        iota(v("VB%d" % r, 0, 1), [[0, 1]], P + k // 3 * 3)
        iota(v("VB%d" % r, n + 1), [[k, 15]], P + k + k // 3 * 3)
        if r == 3:
            iota(v("VB3", n + 15), [[0, 1]], P)

    def tables(r):
        thresholds(r, False)
        thresholds(r, True)
        signs(r)
        slots(r)

    def table(r, kind):
        return 64 * (r - 2) + 16 * ("tops", "bases", "below", "above").index(kind)

    def steps(r):
        W = LANES[r]
        if r == 1:
            return [lambda: tt(v("AD", 0, W), v("PF", 0, W), v("PF", 1, W + 1), A.subtract)]
        a = table(r, "tops")
        return [lambda: vcopy(v("XL", 0, 16), by(v("NX", a + 16, a + 64), v("xn", 0, 1))),
                lambda: tt(v("AD", 0, 32), v("NX", a, a + 32), v("NX", a + 1, a + 33), A.subtract)]

    def spread(r, first=0, last=2):
        W = LANES[r]
        cut = W * max(UPC[r], LOC[r])
        for a, n in ((0, -(-cut // 16)), (cut, -(-(W * W + W - cut) // 16)))[first:last]:
            for at, tab in ((0, 16 * ((a > 0) == (r == 2))), (SECOND, 16 * ((a > 0) != (r == 2)))):
                act(v("AT", at + a, at + a + 16 * n), by(v("AD", tab, tab + W), v("KL%d" % r, 0, n)))

    def plane(t, a=0, b=P):
        return v("V", VW * t + a, VW * t + b)

    def arrived(t, a=0, b=P):
        return v("FP", P * t + a, P * t + b)

    def unpack(q, bank, a=0, b=P, planes=range(4)):
        for t in planes:
            mm(bank + t, "EC", 128 * t, q, a, b - a)

    def unpack_arrived(r, a, b, between=lambda: None):
        unpack("LB%d" % r, 4, a, b)
        for t in range(4):
            if t == 3:
                between()
            act(arrived(t, a, b), v("p%d" % (4 + t), 0, b - a))

    def own_plane(t):
        act(plane(t), v("p%d" % t, 0, P))
        if t < 2:
            a = (0, OWN)[t]
            dma("y", v("FQ", P * t, P * t + P - a), plane(t, a, P))

    def quantise_and_score(r, c):
        q, a, b = "QX%d" % r, 128 * c, 128 * c + 128
        quant(q, a, b, v(XB[r], 4 * a, 4 * b))
        if r == 1 or r == 2 and c > 0:
            a0 = 0 if (r, c) == (2, 1) else a
            send(raw(v("LB%dc" % r, a0, b)), raw(v(q + "c", a0, b)), "a%dc%d" % (r, c))
        if r < 3 and c > 0:
            a0 = (0, 0, a)[c]
            send(v("LB%ds" % r, a0, b), v(q + "s", a0, b), "a%ds%d" % (r, c))
        if r > 1:
            mm(4 + c, "UR" if r < 4 else "QV", 0, q, a, 128)

    def take_scores(q, c):
        evac(q, v("SS", 128 * c, 128 * c + 128), v("p%d" % (4 + c), 0, 128))

    def gather_scores(r, cut):
        n = 16 * LANES[r]
        vcopy(v("GM", 0, cut), by(v("SS"), v("XL", 0, cut // 16)))
        act(v("GM", cut, n), by(v("SS"), v("XL", cut // 16, n // 16)))
        gap(3)
        for a, b in ((0, cut), (cut, n)):
            turn(v("SC", a, b), v("GM", a, b))

    def pairs(r, q, a, b):
        lanes = -(-b // LANES[r])
        (act if q == "s" else vcopy)(v("BX", a, b), by(v("SC", 0, 16 * lanes), v("MN%d" % r, a // 16, b // 16)))

    def compare(r, a, b):
        tt(v("C", a, b), by(v("SC"), v("MX%d" % r, a // 16, b // 16)), v("BX", a, b), A.is_le)

    def rank_sums(r, a, b):
        scan(v("CS", a, b), v("D0%d" % r, a, b), v("C", a, b), A.mult, A.add, 2.0 - LANES[r])

    def misses(r, a, b, at=0):
        tt(v("miss", at + a, at + b), by(v("CS"), v("KS%d" % r, a // 16, b // 16)), v("TH%d" % r, a, b), A.not_equal)

    def distances(s):
        act(v("miss", 24 * s, 24 * s + 24), v("CS", 23, 576, 24), AF.Abs, bias=-12.0 - s)

    def places(r, s0, s1, at=0, clear=A.mult):
        a, b = at + s0 * LANES[r], at + s1 * LANES[r]
        scan(v("HS", a, b), v("miss", a, b), v("AT", a, b), clear, A.add, P / 2048.0)

    def listed(name, r, at=0):
        W = LANES[r]
        ends = v("HS", at + W - 1, at + (W + 1) * W, W)
        if r == 1:
            ts(v(name + "1"), ends, 2048.0, A.mult, -float(P), A.add)
        else:
            vcopy(v(name + str(r)), ends)

    def upper(name, r):
        return v(name + str(r), UPC[r], UPC[r] + LANES[r] // 2)

    def lower(name, r):
        return v(name + str(r), LOC[r], LOC[r] + LANES[r] // 2 + 1)

    def next_tables(r):
        h, cl, lo, up = LANES[r] // 2, "CF%d" % r, LOC[r], UPC[r]
        for kind, c, to, of in (("bases", lo, slice(0, 128), slice(0, 128)), ("below", lo, slice(0, 112), slice(16, 128)),
                                ("above", lo, slice(16, 128), slice(0, 112)), ("tops", up, slice(1, 128), slice(0, 127)),
                                ("bases", lo + 1, slice(0, 128, 16), slice(0, 128, 16)),
                                ("below", lo + 1, slice(0, 128, 32), slice(16, 128, 32)),
                                ("above", lo + 1, slice(16, 128, 32), slice(0, 128, 32)),
                                ("tops", up, slice(0, 128, 16), slice(15, 128, 16))):
            a = table(r + 1, kind)
            dma("y", v("NX", a, a + h, rows=to), v(cl, c, c + h, rows=of))

    def upper_bases(r):
        act(v("VB%d" % r, 1, 8 * LANES[r] + 1), by(v("iotaR", 0, P), upper("CL" if r == 1 else "CM", r)))

    def new_tops(r, values):
        vcopy(by(v("UP"), upper("CL", r)), values)

    def links(r):
        vcopy(by(v("UP"), lower("CL" if r == 1 else "CM", r)), v("VB%d" % r))

    def blend_list():
        scan(v("ht"), v("climb"), v("UP"), A.add, A.max)
        gap()
        ts(v("UL"), v("ht", 15, P, 16), col["rise"], A.subtract)

    def make_e(r, win, lst, between=lambda: None):
        n, name = 8 * LANES[r], lst + str(r)

        def bases(copy, t, a=0, b=n + 16):
            copy(v("tmp", (n + 16) * t + a, (n + 16) * t + b), by(win(t), v(name, LOC[r] + a // 16, LOC[r] + b // 16)))

        def tops(t, a=0, b=n):
            c = (n + 16) * t + 1
            tt(v("E", 4 * a + t, 4 * b, 4), by(win(t), v(name, UPC[r] + a // 16, UPC[r] + b // 16)), v("tmp", c + a, c + b), A.add)

        bases(vcopy, 0)
        if r == 1:
            bases(act, 1, 0, 96)
            bases(act, 1, 96)
            tops(1, 0, 64)
        else:
            bases(act, 1)
        bases(act, 2)
        bases(act, 3)
        between()
        tops(0)
        tops(1, 64 if r == 1 else 0)
        tops(2)
        tops(3)

    def layer(q, a, n, order=(1, 0, 2, 3)):
        for b in order:
            mm(4 + b, "WW", 128 * b, q, a, n)

    def blend(r):
        n = 8 * LANES[r]

        def take_h(q, b):
            evac(q, plane(b, P, P + n), v("p%d" % (4 + b), 0, n), 0.015625)

        def near(t, a, b):
            return by(plane(t, 0, P + n), v("UL", a // 16, b // 16))

        def x(t, a, b):
            return v(XB[r + 1], 4 * a + t, 4 * b, 4)

        parts = [(1, 0, OWN), (2, 0, P), (3, 0, 192), (3, 192, 320), (3, 320, P)]
        if r < 3:
            for q, t in (("s", 1), ("v", 0), ("v", 2)):
                take_h(q, t)
        for t, a, b in parts:
            act(v("tb", P * t + a, P * t + b), near(t, a, b))
            if r < 3 and t == 1:
                take_h("s", 3)
        tt(x(0, 0, P), near(0, 0, P), v("FQ", 0, P), A.add)
        tt(x(1, OWN, P), near(1, OWN, P), v("FQ", P), A.add)
        for t, a, b in parts:
            tt(x(t, a, b), v("tb", P * t + a, P * t + b), v("p%d" % t, a, b), A.add)
        if r < 3:
            for c in range(3):
                quantise_and_score(r + 1, c)

    def mend(off):
        n = 16 * LANES[3]
        for t in range(4):
            evac("s", v("FP", n * t + 1, n * t + n, 2), v("p%d" % (4 + t), off, off + n // 2), 0.015625)
            scan(v("E", n * t, n * t + n), v("pair"), v("FP", n * t, n * t + n), A.mult, A.add)
        vcopy(by(v(XB[4]), v("PL")), v("E", 1, 4 * n, 2))

    dma("y", v("ub"), T.u[:, :])
    dma("s", v("tw32", 0, 24), T.tw[:, :])
    dma("s", v("tw32", 24, 48, rows=slice(0, 120)), T.tw[8:128, :])
    for c in range(3):
        dma("y", v("X1", 512 * c, 512 * c + 512), T.x[:, 512 * c:512 * c + 512])

    iota(v("ic"), [[0, 24]], 0, 1)
    iota(v("J0"), [[16, 38]], 0)
    iota(v("U0"), [[64, 4], [0, 2]], 0)
    memset(v("half"), 0.5)
    op("g", [v("half")], [v("zi")], lambda: g.affine_select(T.zi[:], T.half[:, 0:516], [[1, 516]], A.is_equal, 0.0, -3, -4))
    unpackers = [lambda b=b: quant("EC", 128 * b, 128 * b + 128, v("zi", 3 - b, 515 - b)) for b in range(4)]
    act(v("D01"), v("half"), scale=2.0)
    thresholds(1, False)
    act(v("W2"), v("half", 0, 48))
    act(v("TT", 96), v("half", 0, 24), scale=-2.0 * P)
    bit = {k2: v("ti", 60 + 2 * i, 61 + 2 * i) for i, k2 in enumerate((8, 23, 1, 16))}
    ts(v("i16"), v("ic"), 15, A.bitwise_and)
    for k2 in (8, 23, 1, 16):
        ts(bit[k2], v("ic", 0, 1), k2, A.bitwise_and)
    ts(col["i"], tower, 1.0, A.mult)
    ts(col["oct"], bit[8], 4.0, A.mult)
    for o in range(3):
        ts(v("ml", 2 * o, 2 * o + 2), v("i16", 0, 2), 3.0, A.mult, float(o), A.add)
    ts(v("J"), v("J0"), col["i"], A.add)
    ts(v("m16s"), v("J0", 0, 16), 1.0 / 16, A.mult, col["i"], A.is_equal)
    ts(col["a"], bit[23], col["oct"], A.add)
    vcopy(v("il"), v("i16", 0, 24))
    ts(v("ul"), v("U0"), col["oct"], A.add, 0.5, A.mult)
    ts(col["own"], bit[16], 0.5, A.mult)
    ts(col["d"], bit[1], -1.0, A.add)
    act(v("c16"), v("m16s"), AF.Identity, scale=-33792.0, bias=1024.0)
    for k2, x in (("m0", -1.0), (1, 12.0), (2, -6.0), (3, -3.0)):
        act(col[k2], v("m16s", 0, 1), scale=x)
    act(v("climb"), by(v("c16"), v("il")))
    act(col["e"], col["own"], AF.Relu, scale=1.0 / 8, bias=col["d"])
    act(col["f"], col["own"], AF.Identity, scale=33.0 / 8, bias=col["i"])
    todo += lists(1)
    gap(1)
    ts(col["b"], bit[1], 15.0, A.mult, col["a"], A.add)
    vcopy(v("fl", 0, 1), col["a"])
    ts(v("fl", 1, 2), col["a"], 64.0, A.add)

    vcopy(v("W2", 0, 48, 2), v("tw32", 0, 24))
    gap(2)
    ts(col["c"], bit[16], -15.0 / 16, A.mult, col["b"], A.add)
    gap(2)
    quant("QU", 0, 128, v("ub"))
    vcopy(v("W2", 1, 48, 2, rows=slice(0, 120)), v("tw32", 24, 48, rows=slice(0, 120)))
    gap(2)
    vcopy(words(v("URc")), by(words(v("QUc")), v("ul")))
    act(v("MT"), by(v("W2"), v("ml")))
    act(v("URs"), by(v("QUs"), v("ul")))
    act(v("TH1", 192, 288), v("TH1", 288, 384), AF.Identity, bias=20.0)
    act(col["rise"], col["i"], AF.Identity, scale=-1024.0, bias=15360.0)
    act(col["e"], col["e"], AF.Identity, scale=-48.0, bias=col["f"])
    tower0(1)
    quantise_and_score(1, 0)
    gap(1)
    vcopy(v("xl", 0, 1), col["c"])
    ts(v("xl", 1, 2), col["c"], 64.0, A.add, 95.0, A.min)
    quantise_and_score(1, 1)
    turn(v("TT", 0, 96), v("MT"))
    gap(1)
    quantise_and_score(1, 2)
    signs(1)
    for c in range(3):
        mm(4 + c, "UR", 0, "QX1", 128 * c, 128)
    take_scores("s", 0)
    take_scores("s", 1)
    vcopy(v("XL"), by(v("TT"), v("xl")))
    ts(v("PF"), by(v("TT"), v("fl")), 1 / 2048.0, A.mult)
    act(col["e"], col["d"], AF.Identity, scale=15.0, bias=col["e"])
    gap(2)
    unpackers[0]()
    take_scores("v", 2)
    todo[:0] = steps(1)
    gap(3)
    iota(v("iotaR"), [[1, 576]], 0)
    slots(1)

    todo += [lambda: memset(v("NX"), 0.0)]
    gather_scores(1, 160)
    act(v("AT", 0, 288), by(v("AD", 0, 24), v("KL1", 0, 18)))
    unpackers[1]()
    unpack("QX1", 0, planes=(0, 1))
    pairs(1, "s", 0, 96)
    pairs(1, "s", 96, 384)
    pairs(1, "v", 384, 576)
    act(v("AT", 288), by(v("AD", 0, 24), v("KL1", 18)))
    before("y", touches("y", [v("BX")], [], False))
    dma("y", raw(v("WWc")), T.wc[:, :])
    dma("y", v("WWs"), T.ws[:, :])
    own_plane(0)
    own_plane(1)
    todo += [lambda: ts(v("xn", 0, 1), col["e"], 15.0, A.add)] + lists(2)
    for a, b in ((0, 96), (384, 576), (96, 384)):
        compare(1, a, b)
    for a, b in ((0, 96), (384, 576), (96, 384)):
        rank_sums(1, a, b)
    unpackers[2]()
    for s in range(8):
        distances(s)
    misses(1, 288, 608)
    misses(1, 192, 288)
    places(1, 0, 8, clear=A.min)
    places(1, 12, 25)
    places(1, 8, 12)
    unpackers[3]()
    listed("CL", 1)
    send(v("LL1"), v("CL1"), "a1l")
    listed("CF", 1)

    tables(2)
    unpack_arrived(1, 0, 256, lambda: upper_bases(1))
    unpack_arrived(1, 256, P)
    unpack("QX1", 0, planes=(2, 3))
    gap(2)
    new_tops(1, v("iotaR", P, P + 192))
    gap(1)
    links(1)
    before("y", touches("y", [v("LL1")], [], False))
    next_tables(1)
    dma("y", v("vb"), T.v[:, :])
    make_e(1, arrived, "LL")
    own_plane(2)
    own_plane(3)
    tower0(2)
    gap(3)
    quant("QE1", 0, 192, v("E"))
    layer("QE1", 0, 192)
    blend_list()
    gap(2)
    blend(1)

    def scores(r):
        unpack("QX%d" % r, 0)
        todo[:0] = steps(r)
        for c in range(3):
            gap((3, 3, 0)[c])
            take_scores("ssv"[c], c)
        finish()

    scores(2)
    todo += lists(3)
    gather_scores(2, 96)
    spread(2)
    own_plane(0)
    own_plane(1)
    gap(1)
    pairs(2, "v", 0, 64)
    pairs(2, "v", 64, 144)
    compare(2, 0, 64)
    compare(2, 64, 144)
    gap(3)
    rank_sums(2, 0, 144)
    misses(2, 0, 160)
    misses(2, 0, 96, SECOND)
    places(2, 0, 13)
    misses(2, 96, 160, SECOND)
    listed("CL", 2)
    send(v("LL2"), v("CL2"), "a2l")
    tables(3)
    iota(v("opc", 0, 48), [[1, 3], [3, 16]], P + 3)
    iota(v("opc", 48, 51), [[1, 3]], P)
    iota(v("pair"), [[0, 48], [1, 2]], 0)
    listed("CF", 2)
    places(2, 0, 13, SECOND)
    gap(2)
    listed("CM", 2, SECOND)
    unpack_arrived(2, 0, 256, lambda: upper_bases(2))
    unpack_arrived(2, 256, P)
    new_tops(2, v("iotaR", P, P + 96))
    gap(3)
    links(2)
    before("y", touches("y", [v("LL2")], [], False))
    next_tables(2)
    make_e(2, arrived, "LL")
    own_plane(2)
    own_plane(3)
    tower0(3)
    quant("QE2", 0, 128, v("E", 0, 512))
    layer("QE2", 0, 128)
    blend_list()
    blend(2)

    scores(3)
    spread(3, 0, 1)
    gather_scores(3, 64)
    spread(3, 1, 2)
    for t in range(4):
        own_plane(t)
    quant("QV", 0, 128, v("vb"))
    pairs(3, "v", 0, 48)
    vcopy(v("opc", 15, 48, 16), v("opc", 48, 51))
    compare(3, 0, 48)
    rank_sums(3, 0, 36)
    misses(3, 0, 48)
    misses(3, 0, 48, SECOND)
    places(3, 0, 7)
    places(3, 0, 7, SECOND)
    listed("CL", 3)
    listed("CM", 3, SECOND)
    make_e(3, plane, "CL", lambda: (new_tops(3, v("opc", 0, 48)), upper_bases(3)))
    for t in range(4):
        act(v("FP", 96 * t, 96 * t + 96, 2), by(plane(t), upper("CL", 3)))
    links(3)
    quant("QE3", 0, 128, v("E", 0, 512))
    send(raw(v("LB1c", P, P + 48)), raw(v("QE3c", 0, 48)), "a3c")
    send(v("LB1s", P, P + 48), v("QE3s", 0, 48), "a3s")
    todo += [lambda t=t: ts(v("PL", 3 * t, 3 * t + 3), v("HS", 29, 42, 6), 4.0, A.mult, float(t), A.add) for t in range(4)]
    blend_list()
    gap(2)
    dma("y", T.op[:, :], v("UP", rows=slice(0, 128, 16)))
    blend(3)
    layer("LB1", P + 48 - 128, 128, range(4))
    mend(128 - 48)

    for c in range(3):
        quantise_and_score(4, c)
        dma("sys"[c], T.oc[:, 512 * c:512 * c + 512], raw(v("QX4c", 128 * c, 128 * c + 128)))
    for k2 in range(4):
        dma("yyss"[k2], T.osc[4 * k2:4 * k2 + 4, :], v("QX4s", rows=slice(32 * k2, 32 * k2 + 4)))
    for c in range(3):
        evac("v", v("ysb", 128 * c, 128 * c + 128), v("p%d" % (4 + c), 0, 128))
        dma("ysy"[c], T.y[:, 128 * c:128 * c + 128], v("ysb", 128 * c, 128 * c + 128))

    for sem, val in cnt.items():
        if waited.get(sem, 0) < val:
            g.wait_ge(T.sem[sem], val)
